import numpy as np, ml_dtypes
CORES = [35,38,43,46]
N = 4
import mx_ref
BF = ml_dtypes.bfloat16
def cols(t, e):
    v = np.concatenate([t.reshape(128, -1, 4), np.zeros((128, 1, 4), BF)], axis=1)
    return np.ascontiguousarray(v[:, e]).reshape(128, -1)
def cut(t, i, w=512):
    return t[:, w * i:w * i + w]
def tile(rs):
    return np.stack(rs, axis=2).reshape(128, -1).astype(BF)
def pick(q, e):
    c = np.concatenate([q[0].reshape(128, -1, 4), np.zeros((128, 1, 4), np.uint8)], axis=1); s = np.concatenate([q[1], np.ones((16, 1), np.uint8)], axis=1)
    return (np.ascontiguousarray(c[:, e].reshape(128, -1)), np.ascontiguousarray(s[:, e]))
def join(*qs):
    return (np.concatenate([q[0] for q in qs], axis=1), np.concatenate([q[1] for q in qs], axis=1))
def put(q, e, v):
    c, s = q[0].reshape(128, -1, 4).copy(), q[1].copy(); c[:, e] = v[0].reshape(128, -1, 4); s[:, e] = v[1]
    return (c.reshape(128, -1), s)
def pk(c, s):
    return (np.ascontiguousarray(c), mx_ref.live(s))
def emit(q):
    return q[0], q[1]
def decode(q):
    o = []
    for b in range(4):
        e = np.zeros((128, 128, 4), np.float32); e[np.arange(128), np.arange(128), b] = 1
        o.append(mx_ref.matmul(mx_ref.quantize(e.reshape(128, 512).astype(BF)), q))
    return np.stack(o, axis=2).reshape(128, -1)
def f(rng, *shape):
    return mx_ref.flush((rng.standard_normal(shape, dtype=np.float32) * np.exp2(rng.integers(-2, 3, shape[:-1] + (1,)))).astype(BF))
def wide(rng, *shape, cols=0):
    v = rng.standard_normal(shape, dtype=np.float32) * np.exp2(rng.integers(-12, 13, shape)).astype(np.float32)
    if cols: v *= np.repeat(np.exp2(rng.integers(-cols, cols + 1, shape[:-2] + (1, shape[-1] // 4))) * (rng.random(shape[:-2] + (1, shape[-1] // 4)) > 0.0625), 4, axis=-1).astype(np.float32)
    return mx_ref.flush(v.astype(BF))
T, CAPP, CAPR = 192, 112, 48
def big(v, k):
    v = v.astype(np.float32) * np.float32(k)
    v[np.abs(v) < np.float32(2.0 ** -6)] = 0
    return v.astype(BF)
def same(t):
    return np.repeat(t[None], N, axis=0)
def only(t, k):
    t = np.array(t)
    t[:, 4 * k:] = 0
    return t
def plain(rng):
    return {"x": f(rng, N, 128, 4 * T), "gr": big(f(rng, N, 128, 4 * T), 8), "rt": same(only(f(rng, 128, 512), N)), "w": f(rng, N, 128, 2048), "ub": big(f(rng, N, 128, 2048), 4), "pr": same(only(f(rng, 128, 512), 1)), "v": f(rng, N, 128, 512)}
def deal(rng, n, among):
    m, j, p = len(among), np.arange(n), rng.permutation(among)
    return np.stack([p[j % m], p[(j + 1 + j // m % (m - 1)) % m]], axis=1)
def routed(rng, to, far=False):
    g = np.arange(128) // (128 // N)
    rt = np.zeros((128, 128, 4), np.float32)
    rt[np.arange(128), g, 0] = 1 + rng.random(128)
    x = rng.standard_normal((N, 128, T, 4)) * (2 if far else 8)
    low = 0.125 * rng.choice([-1.0, 1.0], (N, 128, T))
    first, second = to[:, None, :, 0] == g[None, :, None], to[:, None, :, 1] == g[None, :, None]
    size = np.where(first, low, np.where(second, -4.0, -16.0)) if far else np.where(first, 16.0, np.where(second, 2.0, low))
    x[..., 0] = size * (1 + rng.random((N, 128, T)))
    if far: x, rt = x * 2.0 ** 25, rt * np.float32(2.0 ** 29)
    return {"x": mx_ref.flush(x.reshape(N, 128, 4 * T).astype(np.float32).astype(BF)), "rt": same(rt.reshape(128, 512).astype(BF))}
def setup_inputs(rng):
    return plain(rng)
def setup_inputs_crowd(rng):
    h = int(rng.integers(0, N))
    rest, n, to = np.delete(np.arange(N), h), [CAPP, T, CAPP + 1, CAPR, 0, CAPR + 1, CAPR - 1, 1], np.zeros((N, T, 2), int)
    for i in range(N):
        t = deal(rng, T, rest)
        t[np.arange(n[i]), rng.integers(0, 2, n[i])] = h
        to[(h + 1 + i) % N] = t[rng.permutation(T)]
    d = {**plain(rng), **routed(rng, to)}
    sign, pr = rng.choice([-1.0, 1.0], (128, 1, 4)), np.zeros((128, 128, 4), np.float32)
    pr[:, :1] = 2.0 ** 29 * sign * (1 + rng.random((128, 1, 4)))
    gr = 2.0 ** 28 * sign[None] * (1 + rng.random((N, 128, T, 4))) * rng.choice([-1.0, 1.0], (N, 1, T, 1))
    d["pr"] = same(pr.reshape(128, 512).astype(BF))
    d["gr"] = gr.reshape(N, 128, 4 * T).astype(np.float32).astype(BF)
    d["ub"] = (d["ub"].astype(np.float32) * np.float32(2.0 ** -22)).astype(BF)
    return d
def setup_inputs_dead(rng):
    rest = np.delete(np.arange(N), int(rng.integers(0, N)))
    to, dead = np.zeros((N, T, 2), int), np.zeros((N, T), bool)
    for q in range(N):
        s = rng.permutation(T)
        to[q] = deal(rng, T, rest)[s]
        dead[q] = s // (N - 1) % 4 != 0
    d = {**plain(rng), **routed(rng, to)}
    x = d["x"].astype(np.float32).reshape(N, 128, T, 4)
    x[..., 1:] = 16 * (1 + rng.random((N, 128, T, 3))) * np.where(dead, 1.0, -1.0)[:, None, :, None]
    d["x"] = x.reshape(N, 128, 4 * T).astype(BF)
    w = np.array(d["w"])
    w[rng.permutation(rest)[:N // 2]] = (-1 - rng.random((N // 2, 128, 2048))).astype(np.float32).astype(BF)
    d["w"] = w
    return d
def setup_inputs_one(rng):
    h = int(rng.integers(0, N))
    to = np.full((N, T, 2), h)
    for q in range(N): to[q, :, 1] = rng.permutation(deal(rng, T, np.delete(np.arange(N), h))[:, 0])
    return {**plain(rng), **routed(rng, to, far=True)}
def setup_inputs_spread(rng):
    d = plain(rng)
    x = (wide(rng, N, 128, 4 * T, cols=6).astype(np.float32) * np.float32(2.0 ** 8)).reshape(N, 128, T, 4)
    for q in range(N):
        i = rng.permutation(T)[:T // 8]
        x[q][:, i] = 2.0 ** -29 * (1 + rng.random((128, i.size, 4))) * rng.choice([-1.0, 1.0], (128, i.size, 4))
    d["x"] = x.reshape(N, 128, 4 * T).astype(BF)
    d["rt"] = (d["rt"].astype(np.float32) * np.float32(2.0 ** 20)).astype(BF)
    d["gr"] = big(wide(rng, N, 128, 4 * T, cols=3), 16)
    return d
def setup_inputs_ties(rng):
    u, o = sorted(rng.permutation(N)[:2].tolist())
    rest = np.delete(np.arange(N), [u, o])
    to, at = np.zeros((N, T, 2), int), []
    for q in range(N):
        t, s = deal(rng, T, rest), rng.permutation(T)
        t[:T // 2] = np.array([u, rest[0]])
        t[T // 2:T // 2 + 4, 1] = u
        to[q] = t[s]
        at.append(np.flatnonzero(s < T // 2))
    d = {**plain(rng), **routed(rng, to)}
    r = np.array(d["rt"]).reshape(N, 128, 128, 4)
    r[:, :, o] = r[:, :, u]
    x, g = d["x"].astype(np.float32).reshape(N, 128, T, 4), d["gr"].astype(np.float32).reshape(N, 128, T, 4)
    for q in range(N):
        i = at[q]
        x[q][:, i] = x[q][:, i[:1]].copy()
        g[q][:, i] = g[q][:, i[:1]].copy() * rng.choice([-1.0, 1.0], i.size)[None, :, None]
    return {**d, "x": x.reshape(N, 128, 4 * T).astype(BF), "gr": g.reshape(N, 128, 4 * T).astype(BF), "rt": r.reshape(N, 128, 512)}
def check_inputs(d):
    b = []
    for k in ("x", "gr", "rt", "w", "ub", "pr", "v"):
        a = np.abs(d[k].astype(np.float32))
        if not (np.isfinite(a).all() and ((a == 0) | (a >= 2.0 ** -30) & (a <= 2.0 ** 30)).all()): b.append("a value of " + k)
    for k, n in (("rt", N), ("pr", 1)):
        a = d[k].astype(np.float32)
        if (a != a[:1]).any(): b.append(k + " differs between ranks")
        if (a[:, :, 4 * n:] != 0).any(): b.append(k + " has numbers behind its first columns")
    return b
def reference(x, gr, rt, w, ub, pr, v):
    qz = lambda t: mx_ref.quantize(np.ascontiguousarray(t))
    to = []
    for q in range(N):
        s = mx_ref.matmul(qz(rt[q]), qz(x[q]))[:N] + np.float32(0)
        to.append(np.argsort(-s, axis=0, kind="stable")[:2])
    everyx, everyg = np.concatenate([x[q] for q in range(N)], axis=1), np.concatenate([gr[q] for q in range(N)], axis=1)
    came = np.zeros((N, 128, 2 * T, 4), np.float32)
    ct = np.zeros((N, 1, T), np.float32)
    for e in range(N):
        taken = [np.flatnonzero((to[q] == e).any(axis=0))[:CAPP] for q in range(N)]
        at = np.full((N, CAPP), -1)
        for q in range(N): at[q, :taken[q].size] = T * q + taken[q]
        at = at.reshape(-1)
        xs, gs = qz(cols(everyx, at)), qz(cols(everyg, at))
        forward = np.stack([mx_ref.matmul(qz(cut(w[e], i)), xs) for i in range(4)], axis=2).reshape(128, -1)
        m = qz(np.where(forward > 0, decode(gs), np.float32(0)).astype(BF))
        strength = np.abs(mx_ref.matmul(qz(pr[e]), m)[0])
        dx = decode(qz(tile([mx_ref.matmul(qz(cut(ub[e], i)), m) * np.float32(0.0625) for i in range(4)]))).reshape(128, -1, 4)
        for q in range(N):
            k = np.argsort(-strength[CAPP * q:CAPP * q + taken[q].size], kind="stable")[:CAPR]
            j = taken[q][k]
            second = (to[q][1, j] == e).astype(int)
            came[q][:, T * second + j] = dx[:, CAPP * q + k]
            ct[q, 0, j] += 1 + second
    oc, osc, y = np.zeros((N, 128, 4 * T), np.uint8), np.zeros((N, 16, T), np.uint8), np.zeros((N, 128, T), np.float32)
    for q in range(N):
        z = qz((came[q][:, :T] + came[q][:, T:]).reshape(128, 4 * T).astype(BF))
        oc[q], osc[q] = emit(z)
        y[q] = mx_ref.matmul(qz(v[q]), z)
    return {"oc": oc, "osc": osc, "ct": ct, "y": y}

@@ -1,0 +1,417 @@
+from concourse.bass import DstId, RemoteDMATransfer
+from concourse.mybir import dt, AluOpType as A, AxisListType, ActivationFunctionType as F
+
+NT, CP, CR = 192, 112, 48
+NS = 10
+TINY = 2.0 ** -100
+
+SCRATCH = {
+    "xt": ("sbuf", [128, 776], "bfloat16"), "gt": ("sbuf", [128, 776], "bfloat16"),
+    "rtt": ("sbuf", [128, 512], "bfloat16"), "prt": ("sbuf", [128, 512], "bfloat16"),
+    "wt": ("sbuf", [128, 2048], "bfloat16"), "ut": ("sbuf", [128, 2048], "bfloat16"),
+    "vt": ("sbuf", [128, 512], "bfloat16"), "et": ("sbuf", [128, 2048], "bfloat16"),
+    "pt": ("sbuf", [128, 1024], "bfloat16"), "zt": ("sbuf", [128, 768], "bfloat16"),
+    "pi": ("sbuf", [128, 8], "int32"), "pf": ("sbuf", [128, 16], "float32"), "ii": ("sbuf", [128, 48], "float32"),
+    "rl": ("sbuf", [128, 16], "uint16"), "zl": ("sbuf", [128, 8], "uint16"),
+    "tie": ("sbuf", [128, 8], "float32"), "sb": ("sbuf", [128, 16], "float32"),
+    "tri0": ("sbuf", [128, 112], "float32"), "tri": ("sbuf", [128, 112], "float32"),
+    "one": ("sbuf", [128, 128], "bfloat16"), "idn": ("sbuf", [128, 128], "bfloat16"),
+    "vals": ("sbuf", [128, 48], "bfloat16"), "k4": ("sbuf", [128, 512], "bfloat16"),
+    "zero": ("sbuf", [128, 192], "bfloat16"), "z3": ("sbuf", [128, 8], "float32"),
+    "s0": ("sbuf", [128, 192], "float32"), "dd": ("sbuf", [128, 576], "float32"), "sg": ("sbuf", [128, 576], "bfloat16"),
+    "u": ("sbuf", [128, 192], "bfloat16"), "win": ("sbuf", [128, 192], "bfloat16"), "m": ("sbuf", [128, 192], "bfloat16"),
+    "pref": ("sbuf", [128, 192], "bfloat16"),
+    "le": ("sbuf", [128, 192 * 16], "bfloat16"),
+    "cn": ("sbuf", [128, 32], "float32"), "cnt": ("sbuf", [128, 32], "float32"), "off": ("sbuf", [128, 32], "uint16"),
+    "tv": ("sbuf", [128, 384], "bfloat16"), "hh": ("sbuf", [128, 144], "float32"),
+    "offt": ("sbuf", [128, 48], "uint16"), "wgt": ("sbuf", [128, 48], "float32"),
+    "tab": ("sbuf", [128, 512], "bfloat16"), "gg": ("sbuf", [128, 1536], "bfloat16"), "hof": ("sbuf", [128, 64], "uint16"),
+    "ff": ("sbuf", [128, 144], "float32"), "cs": ("sbuf", [128, 32], "float32"), "cst": ("sbuf", [128, 32], "float32"),
+    "ysb": ("sbuf", [128, 192], "float32"), "ll": ("sbuf", [128, 32], "uint16"), "lo": ("sbuf", [128, 32], "uint16"),
+    "mt": ("sbuf", [128, 2048], "bfloat16"), "dxt": ("sbuf", [128, 2048], "bfloat16"), "ot": ("sbuf", [128, 2048], "bfloat16"),
+    "sm": ("sbuf", [128, 1792], "bfloat16"), "mk": ("sbuf", [128, 1792], "bfloat16"), "ra": ("sbuf", [128, 1344], "float32"),
+    "ca": ("sbuf", [128, 16], "float32"), "rk": ("sbuf", [128, 16], "float32"),
+    "pz": ("psum", [128, 2048], "float32"), "px": ("psum", [128, 2048], "float32"),
+}
+_CODES = [("xq", 194), ("gq", 194), ("rq", 128), ("rp", 160), ("pq", 128), ("pp", 128), ("wq", 512), ("uq", 512),
+          ("vq", 128), ("eq", 512), ("cq", 256), ("zq", 192), ("qm", 512), ("qd", 512), ("qo", 512)]
+for _k in range(4):
+    _CODES += [("lc%d" % _k, 224), ("ld%d" % _k, 64), ("zc%d" % _k, 192)]
+    if _k:
+        _CODES += [("sc%d" % _k, 224), ("sd%d" % _k, 48)]
+for _n, _w in _CODES:
+    SCRATCH[_n] = ("sbuf", [128, _w], "float8_e4m3fn_x4")
+    SCRATCH[_n + "s"] = ("sbuf", [128, _w], "uint8")
+
+SEMAPHORES = ["cV", "cS", "cP", "cG", "dx", "dgr", "drt", "dpr", "dw", "dub", "dv", "dz", "doy", "dos", "left"]
+for _k in (1, 2, 3):
+    SEMAPHORES += ["ax%d" % _k, "al%d" % _k, "ar%d" % _k]
+
+
+def rank_program(g, core, T, topo):
+    rank = T.rank_of(core)
+    if rank is None:
+        return
+    queue = {"V": g.vector, "S": g.scalar, "P": g.tensor, "G": g, "Y": g.sync}
+    total, waited, wrote, read = {}, {}, {}, {}
+
+    def need(q, tok):
+        if tok and waited.get((q, tok[0]), 0) < tok[1]:
+            queue[q].wait_ge(T.sem[tok[0]], tok[1])
+            waited[(q, tok[0])] = tok[1]
+
+    def deps(q, reads, writes):
+        own = "c" + q
+        toks = []
+        for k in reads:
+            toks.append(wrote.get(k))
+            if k[0] == "*":
+                toks += [t for t in read.get(k, []) if t[0] != own]
+        for k in writes:
+            w = wrote.get(k)
+            if not (q == "P" and w and w[0] == own):
+                toks.append(w)
+            toks += [t for t in read.get(k, []) if t[0] != own]
+        best = {}
+        for t in toks:
+            if t:
+                best[t[0]] = max(best.get(t[0], 0), t[1])
+        for s, v in best.items():
+            need(q, (s, v))
+
+    def mark(tok, reads, writes):
+        for k in reads:
+            read.setdefault(k, []).append(tok)
+        for k in writes:
+            wrote[k] = tok
+            read[k] = []
+
+    def run(q, call, reads, writes):
+        deps(q, reads, writes)
+        s = "c" + q
+        total[s] = total.get(s, 0) + 1
+        call(queue[q]).then_inc(T.sem[s], 1)
+        mark((s, total[s]), reads, writes)
+
+    def dma(q, sem, out, in_, reads, writes):
+        deps(q, reads, writes)
+        total[sem] = total.get(sem, 0) + 16
+        queue[q].dma_start(out, in_).then_inc(T.sem[sem], 16)
+        mark((sem, total[sem]), reads, writes)
+
+    def ts(out, in0, s1, s2, o0, o1, reads, writes):
+        if o1 is None:
+            run("V", lambda e: e.tensor_scalar(out, in0, s1, None, o0), reads, writes)
+        else:
+            run("V", lambda e: e.tensor_scalar(out, in0, s1, s2, o0, o1), reads, writes)
+
+    def tt(out, a, b, op, reads, writes):
+        run("V", lambda e: e.tensor_tensor(out, a, b, op), reads, writes)
+
+    def cp(out, a, reads, writes):
+        run("V", lambda e: e.tensor_copy(out, a), reads, writes)
+
+    def turn(out, a, reads, writes):
+        run("V", lambda e: e.transpose(out, a), reads, writes)
+
+    def fill(ap, v, writes):
+        run("V", lambda e: e.memset(ap, v), [], writes)
+
+    def act(out, a, f, reads, writes, **kw):
+        run("S", lambda e: e.activation(out, a, f, **kw), reads, writes)
+
+    def quant(q, a, b, tile, c, d, reads, writes):
+        o, s, i = T[q][:, a:b], T[q + "s"][:, a:b], T[tile][:, c:d]
+        run("V", lambda e: e.quantize_mx(o, s, i), reads, writes)
+
+    def mm(out, l, la, r, ra, n, start, stop, reads, writes):
+        w, ws, x, xs = T[l][:, la:la + 128], T[l + "s"][:, la:la + 128], T[r][:, ra:ra + n], T[r + "s"][:, ra:ra + n]
+        run("P", lambda e: e.matmul_mx(out, w, ws, x, xs, start, stop), reads, writes)
+
+    def pick(dst, c, n, src, a, b, offs, reads, key):
+        o, i = T[dst][:, c:c + n].bitcast(dt.uint32), T[src][:, a:b].bitcast(dt.uint32).indirect(offs)
+        run("V", lambda e: e.tensor_copy(o, i), reads, [key])
+        act(T[dst + "s"][:, c:c + n], T[src + "s"][:, a:b].indirect(offs), F.Copy, reads, [key + "s"])
+
+    peer = [T.cores[rank ^ k] for k in range(4)]
+    away = [k for k in (1, 2, 3) if topo.chip(peer[k]) != topo.chip(core)]
+    out_eng = topo.engines(core, peer[away[0]])
+    near_eng = [e for e in topo.engines(core, peer[1]) if e not in out_eng] or out_eng
+    eng = {k: (out_eng if k in away else near_eng) for k in (1, 2, 3)}
+    msk = {k: sum(1 << e for e in eng[k]) for k in eng}
+
+    def send(k, dst, src, sem):
+        rid, pid, _s = topo.addr(peer[k])
+        total["left"] = total.get("left", 0) + len(eng[k])
+        g.remote_dma(out_ap=dst, in_ap=src, remote_sem=T.sem["%s%d" % (sem, k)], local_sem=T.sem["left"], pid=pid,
+                     routing_id=rid, dma_engine_mask=msk[k])
+
+    def send_two(ks, dst, src, width, codes, sem):
+        tr = []
+        for k in ks:
+            rid, pid, _s = topo.addr(peer[k])
+            s, d = T[src % k][:, 0:width], T[dst % k][:, 0:width]
+            if codes:
+                s, d = s.bitcast(dt.uint8), d.bitcast(dt.uint8)
+            total["left"] = total.get("left", 0) + len(eng[k])
+            tr.append(RemoteDMATransfer(dst_ids=[DstId(rid=rid, pnc=pid)], dma_engine_mask=msk[k],
+                                        remote_sem=T.sem["%s%d" % (sem, k)], srcs=[s], dsts=[d]))
+        g.remote_dma_fused(tr, local_sem=T.sem["left"])
+
+    for k in (1, 2, 3):
+        n = len(eng[k])
+        wrote["lc%d" % k] = ("ax%d" % k, 2 * n)
+        wrote["ld%d" % k] = wrote["ld%ds" % k] = ("ar%d" % k, 2 * n)
+        wrote["ll%d" % k] = ("al%d" % k, n)
+        total["ax%d" % k] = total["ar%d" % k] = 2 * n
+        total["al%d" % k] = n
+
+    dma("S", "drt", T.rtt[:, 0:16], T.rt[:, 0:16], [], ["rtt"])
+    dma("Y", "dx", T.xt[:, 0:768], T.x[:, :], [], ["xt"])
+    dma("Y", "dgr", T.gt[:, 0:768], T.gr[:, :], [], ["gt"])
+    dma("Y", "dw", T.wt[:, :], T.w[:, :], [], ["wt"])
+    dma("Y", "dpr", T.prt[:, 0:8], T.pr[:, 0:8], [], ["prt"])
+    dma("Y", "dub", T.ut[:, :], T.ub[:, :], [], ["ut"])
+    dma("Y", "dv", T.vt[:, :], T.v[:, :], [], ["vt"])
+
+    def iota(out, pattern, base, ch, key, **kw):
+        run("G", lambda e: e.iota(out, pattern, base, ch, **kw), [], [key])
+
+    fl_ok = {"allow_small_or_imprecise_dtypes": True}
+    iota(T.pi[:, 0:1], [[0, 1]], 0, 1, "pi")
+    iota(T.ii[:, 16:26], [[0, 5], [2, 2]], 0, 0, "i10", **fl_ok)
+    iota(T.ii[:, 32:35], [[-1, 3]], 3, 0, "i3", **fl_ok)
+    iota(T.ii[:, 0:16], [[1, 16]], 0, 0, "i16", **fl_ok)
+    fill(T.rtt[:, 16:512], 0.0, ["rtz"])
+    fill(T.one[:, :], 1.0, ["one"])
+    fill(T.xt[:, 768:776], 0.0, ["xz"])
+    fill(T.gt[:, 768:776], 0.0, ["gz"])
+    ts(T.pi[:, 1:2], T.pi[:, 0:1], 15, None, A.bitwise_and, None, ["pi"], ["pi1"])
+    ts(T.pi[:, 2:3], T.pi[:, 0:1], 3, 1, A.arith_shift_right, A.bitwise_and, ["pi"], ["pi2"])
+    ts(T.pi[:, 3:4], T.pi[:, 0:1], 3, 3, A.arith_shift_right, A.bitwise_and, ["pi"], ["pi3"])
+    ts(T.pi[:, 4:5], T.pi[:, 0:1], 7, None, A.bitwise_and, None, ["pi"], ["pi4"])
+    ts(T.pi[:, 5:6], T.pi[:, 0:1], 4, 1, A.arith_shift_right, A.bitwise_and, ["pi"], ["pi5"])
+    cp(T.pf[:, 0:6], T.pi[:, 0:6], ["pi", "pi1", "pi2", "pi3", "pi4", "pi5"], ["pf"])
+    ts(T.rl[:, 0:10], T.ii[:, 16:26], T.pf[:, 2:3], None, A.add, None, ["i10", "pf"], ["rl"])
+    ts(T.tie[:, 4:7], T.ii[:, 32:35], T.pf[:, 3:4], 0.5, A.is_gt, A.subtract, ["i3", "pf"], ["tie0"])
+    ts(T.tie[:, 0:3], T.tie[:, 4:7], 2 * TINY, None, A.mult, None, ["tie0"], ["tie"])
+    ts(T.pf[:, 6:7], T.pf[:, 4:5], 16.0, 0.5, A.mult, A.add, ["pf"], ["pf6"])
+    ts(T.sb[:, :], T.ii[:, 0:16], T.pf[:, 6:7], None, A.add, None, ["i16", "pf6"], ["sb"])
+    ts(T.pf[:, 7:8], T.pf[:, 1:2], float(NS), None, A.is_lt, None, ["pf"], ["pf7"])
+    ts(T.pf[:, 8:9], T.pf[:, 7:8], -0.5, 1.0, A.mult, A.add, ["pf7"], ["pf8"])
+    ts(T.pf[:, 9:10], T.pf[:, 7:8], 96.0, None, A.mult, None, ["pf7"], ["pf9"])
+    fill(T.zero[:, :], 0.0, ["zero"])
+    fill(T.et[:, :], 0.0, ["et"])
+    fill(T.tri0[:, :], -TINY, ["tri0"])
+    run("G", lambda e: e.affine_select(T.idn[:, :], T.one[:, :], [[-1, 128]], A.is_equal, 0.0, 0, 1), ["one"], ["idn"])
+    run("G", lambda e: e.affine_select(T.tri[:, :], T.tri0[:, :], [[-1, 112]], A.is_gt, 0.0, 0, 1), ["tri0"], ["tri"])
+    iota(T.k4[:, :], [[0, 8], [1, 16], [16, 4]], 0, 0, "k4", **fl_ok)
+    iota(T.vals[:, :], [[1, 48]], 0, 0, "vals", **fl_ok)
+
+    quant("rq", 0, 128, "rtt", 0, 512, ["rtt", "rtz"], ["rq"])
+    pick("rp", 0, 160, "rq", 0, 128, T.rl[:, 0:10], ["rq", "rl"], "rp")
+    quant("xq", 0, 194, "xt", 0, 776, ["xt", "xz"], ["xq"])
+    for r in range(4):
+        mm(T.pz[:, 512 * r:512 * r + NT], "rp", 8 * r, "xq", 0, NT, True, True, ["rp", "rps", "xq"], ["*z%d" % r])
+    act(T.s0[:, :], T.pz[:, 0:NT], F.Copy, ["*z0"], ["s0"])
+    for r in (1, 2, 3):
+        a = NT * (r - 1)
+        tt(T.dd[:, a:a + NT], T.s0[:, :], T.pz[:, 512 * r:512 * r + NT], A.subtract, ["s0", "*z%d" % r], ["dd%d" % r])
+        act(T.sg[:, a:a + NT], T.dd[:, a:a + NT], F.Sign, ["dd%d" % r, "tie"], ["sg%d" % r], bias=T.tie[:, r - 1:r])
+    tt(T.u[:, :], T.sg[:, 0:NT], T.sg[:, NT:2 * NT], A.add, ["sg1", "sg2"], ["u"])
+    tt(T.win[:, :], T.u[:, :], T.sg[:, 2 * NT:3 * NT], A.add, ["u", "sg3"], ["win"])
+    ts(T.m[:, :], T.win[:, :], 0.0, None, A.is_gt, None, ["win"], ["m"])
+    run("V", lambda e: e.tensor_tensor_scan(T.pref[:, :], T.m[:, :], T.zero[:, :], 0.0, A.add, A.add), ["m", "zero"], ["pref"])
+    for t in range(NS):
+        act(T.le[:, NT * t:NT * t + NT], T.pref[:, :], F.Sign, ["pref", "sb"], ["cn%d" % t], bias=T.sb[:, t:t + 1], scale=-1.0,
+            accum_out=T.cn[:, t:t + 1])
+    for t in range(NS, 16):
+        a = NT * t
+        ts(T.le[:, a:a + NT], T.pref[:, :], T.sb[:, t:t + 1], None, A.is_le, None, ["pref", "sb"], ["le%d" % t])
+    for t in range(NS, 16):
+        a, o = T.le[:, NT * t:NT * t + NT], T.cn[:, t:t + 1]
+        run("V", lambda e: e.tensor_reduce(o, a, AxisListType.X, A.add), ["le%d" % t], ["cn%d" % t])
+    quant("gq", 0, 194, "gt", 0, 776, ["gt", "gz"], ["gq"])
+    cns = ["cn%d" % t for t in range(16)]
+    cp(T.cn[:, 16:32], T.cn[:, 0:16], cns, ["cnd"])
+    turn(T.cnt[:, :], T.cn[:, :], cns + ["cnd"], ["cnt"])
+    ts(T.off[:, :], T.cnt[:, :], T.pf[:, 8:9], T.pf[:, 9:10], A.mult, A.add, ["cnt", "pf8", "pf9"], ["off"])
+
+    def take(k):
+        e = rank ^ k
+        o = T.off[:, 8 * e:8 * e + 7]
+        d = ("sc%d" if k else "lc%d") % k
+        for c, src, part in ((CP, "xq", "x"), (0, "gq", "g")):
+            oc, ic = T[d][:, c:c + CP].bitcast(dt.uint32), T[src][:, 0:194].bitcast(dt.uint32).indirect(o)
+            run("V", lambda q: q.tensor_copy(oc, ic), [src, "off"], [d + part])
+            act(T[d + "s"][:, c:c + CP], T[src + "s"][:, 0:194].indirect(o), F.Copy, [src, "off"], [d + part + "s"])
+
+    def go(ks):
+        deps("G", [n % k for k in ks for n in ("sc%dx", "sc%dg")], [])
+        send_two(ks, "lc%d", "sc%d", 2 * CP, True, "ax")
+        deps("G", [n % k for k in ks for n in ("sc%dxs", "sc%dgs")], [])
+        send_two(ks, "lc%ds", "sc%ds", 2 * CP, False, "ax")
+
+    take(2)
+    take(1)
+    go((2, 1))
+    take(3)
+    go((3,))
+    take(0)
+    came = {k: ["lc%d" % k] for k in (1, 2, 3)}
+    came[0] = ["lc0x", "lc0g", "lc0xs", "lc0gs"]
+
+    for b in range(4):
+        act(T.et[:, 512 * b + b:512 * b + 512:4], T.idn[:, :], F.Copy, ["idn", "et"], ["et%d" % b])
+    quant("eq", 0, 512, "et", 0, 2048, ["et", "et0", "et1", "et2", "et3"], ["eq"])
+    quant("wq", 0, 512, "wt", 0, 2048, ["wt"], ["wq"])
+    for k in range(4):
+        fill(T.mt[:, 512 * k + 448:512 * k + 512], 0.0, ["mz%d" % k])
+        fill(T.dxt[:, 512 * k + 448:512 * k + 512], 0.0, ["dz%d" % k])
+    for k in range(4):
+        dma("Y", "dz", T["ld%d" % k][:, 48:50].bitcast(dt.uint8), T.xq[:, 192:194].bitcast(dt.uint8), ["xq"], [])
+        dma("Y", "dz", T["ld%ds" % k][:, 48:50], T.xqs[:, 192:194], ["xq"], [])
+    wrote["ldz"] = ("dz", total["dz"])
+
+    def stage1(k):
+        lc, c = "lc%d" % k, came[k]
+        for h in (0, 2):
+            for b in (h, h + 1):
+                x = 512 * (b % 2)
+                mm(T.px[:, x:x + 128], "wq", 128 * b, lc, 96, 128, True, True, ["wq"] + c, ["*x%d" % (b % 2)])
+                o = 448 * k + CP * b
+                act(T.sm[:, o:o + CP], T.px[:, x + 16:x + 128], F.Sign, ["*x%d" % (b % 2)], ["sm%d_%d" % (k, b)])
+            for b in (h, h + 1):
+                x = 1024 + 512 * (b % 2)
+                mm(T.px[:, x:x + 128], "eq", 128 * b, lc, 0, 128, True, True, ["eq"] + c, ["*x%d" % (2 + b % 2)])
+            o = 448 * k + CP * h
+            ts(T.mk[:, o:o + 2 * CP], T.sm[:, o:o + 2 * CP], 0.0, None, A.max, None,
+               ["sm%d_%d" % (k, h), "sm%d_%d" % (k, h + 1)], ["mk%d_%d" % (k, h)])
+            for b in (h, h + 1):
+                o, x = 448 * k + CP * b, 1024 + 512 * (b % 2)
+                tt(T.mt[:, 512 * k + b:512 * k + 448:4], T.mk[:, o:o + CP], T.px[:, x:x + CP], A.mult,
+                   ["mk%d_%d" % (k, h), "*x%d" % (2 + b % 2)], ["mt%d_%d" % (k, b)])
+        quant("qm", 128 * k, 128 * k + 128, "mt", 512 * k, 512 * k + 512,
+              ["mz%d" % k] + ["mt%d_%d" % (k, b) for b in range(4)], ["qm%d" % k])
+
+    def stage2(k):
+        m = "qm%d" % k
+        mm(T.px[:, 512:640], "qm", 128 * k, "pp", 0, 128, True, True, [m, "pp", "pps"], ["*x1"])
+        mm(T.px[:, 0:128], "pp", 0, "qm", 128 * k, 128, True, True, [m, "pp", "pps"], ["*x0"])
+        act(T.ca[:, 4 * k:4 * k + 1], T.px[:, 512:513], F.Abs, ["*x1"], ["ca%d" % k])
+        s, sd, sx = (slice(c + CP * k, c + CP * k + CP) for c in (0, 448, 896))
+        act(T.ra[:, s], T.px[:, 0:CP], F.Abs, ["*x0"], ["ra%d" % k])
+        ts(T.ra[:, sd], T.ra[:, s], T.ca[:, 4 * k:4 * k + 1], None, A.subtract, None, ["ra%d" % k, "ca%d" % k], ["rd%d" % k])
+        tt(T.ra[:, sx], T.ra[:, sd], T.tri[:, :], A.is_gt, ["rd%d" % k, "tri"], ["rx%d" % k])
+        run("V", lambda e: e.tensor_reduce(T.rk[:, 4 * k:4 * k + 1], T.ra[:, sx], AxisListType.X, A.add), ["rx%d" % k], ["rk%d" % k])
+        ts(T.ot[:, 512 * k:512 * k + 512], T.k4[:, :], T.rk[:, 4 * k:4 * k + 1], None, A.is_equal, None, ["k4", "rk%d" % k], ["ot%d" % k])
+        quant("qo", 128 * k, 128 * k + 128, "ot", 512 * k, 512 * k + 512, ["ot%d" % k], ["qo%d" % k])
+        for b, x in ((0, 2), (1, 3), (2, 1), (3, 0)):
+            mm(T.px[:, 512 * x:512 * x + 128], "uq", 128 * b, "qm", 128 * k, 128, True, True, ["uq", m], ["*x%d" % x])
+            act(T.dxt[:, 512 * k + b:512 * k + 448:4], T.px[:, 512 * x:512 * x + CP], F.Copy, ["*x%d" % x], ["dt%d_%d" % (k, b)], scale=0.0625)
+
+    def stage3(k):
+        for c in (0, 1):
+            mm(T.px[:, 1024:1152], "qo", 128 * k, "cq", 128 * c, 128, c == 0, c == 1, ["qo%d" % k, "cq"], ["*x2"])
+        quant("qd", 128 * k, 128 * k + 128, "dxt", 512 * k, 512 * k + 512,
+              ["dz%d" % k] + ["dt%d_%d" % (k, b) for b in range(4)], ["qd%d" % k])
+        cp(T.lo[:, 8 * k:8 * k + 3], T.px[:, 1024:1027], ["*x2"], ["lo%d" % k])
+        d = ("sd%d" if k else "ld%d") % k
+        pick(d, 0, CR, "qd", 128 * k, 128 * k + 128, T.lo[:, 8 * k:8 * k + 3], ["qd%d" % k, "lo%d" % k], d)
+        if k:
+            deps("G", ["lo%d" % k], [])
+            send(k, T.ll[:, 8 * k:8 * k + 3], T.lo[:, 8 * k:8 * k + 3], "al")
+            deps("G", [d], [])
+            send(k, T["ld%d" % k][:, 0:CR].bitcast(dt.uint8), T[d][:, 0:CR].bitcast(dt.uint8), "ar")
+            deps("G", [d + "s"], [])
+            send(k, T["ld%ds" % k][:, 0:CR], T[d + "s"][:, 0:CR], "ar")
+
+    def lookups():
+        h1, h2, h3, h4, h5, h6 = (T.hh[:, 24 * i:24 * i + 24] for i in range(6))
+        turn(T.tv[:, 0:NT], T.win[:, :], ["win"], ["tw"])
+        turn(T.tv[:, NT:2 * NT], T.pref[:, :], ["pref"], ["tp"])
+        tw, tp = T.tv[:, 0:NT:8], T.tv[:, NT:2 * NT:8]
+        ts(h1, tw, 0.0, None, A.is_gt, None, ["tw"], ["h1"])
+        ts(h2, tp, float(CP), None, A.is_le, None, ["tp"], ["h2"])
+        ts(h3, tp, float(CP + 1), None, A.subtract, None, ["tp"], ["h3"])
+        ts(h6, tw, -0.5, 2.5, A.mult, A.add, ["tw"], ["h6"])
+        tt(h4, h1, h2, A.mult, ["h1", "h2"], ["h4"])
+        tt(h5, h4, h3, A.mult, ["h4", "h3"], ["h5"])
+        ts(T.pf[:, 10:11], T.pf[:, 5:6], -1.0, 1.0, A.mult, A.add, ["pf"], ["pf10"])
+        for k in range(4):
+            e = rank ^ k
+            for h in (0, 1):
+                o, p = slice(12 * k + h, 12 * k + 12, 2), (10, 5)[h]
+                ts(T.offt[:, o], T.hh[:, 96 + e:120:4], float(CP), None, A.add, None, ["h5"], ["offt%d%d" % (k, h)])
+                ts(T.wgt[:, o], T.hh[:, 120 + e:144:4], T.pf[:, p:p + 1], None, A.mult, None, ["h6", "pf", "pf10"], ["wgt%d%d" % (k, h)])
+
+    def home(k, first, last):
+        tab = T.tab[:, 128 * k:128 * k + 128]
+        lst, key = (T.ll[:, 8 * k:8 * k + 3], "ll%d" % k) if k else (T.lo[:, 0:3], "lo0")
+        s, s1 = slice(192 * k, 192 * k + 192), slice(768 + 192 * k, 960 + 192 * k)
+        cp(tab.indirect(lst), T.vals[:, :], ["vals", key], ["tab%d" % k])
+        cp(T.gg[:, s], tab.indirect(T.offt[:, 12 * k:12 * k + 12]), ["tab%d" % k, "offt%d0" % k, "offt%d1" % k], ["gr0%d" % k])
+        turn(T.gg[:, s1], T.gg[:, s], ["gr0%d" % k], ["gr1%d" % k])
+        of = T.hof[:, 16 * k:16 * k + 12]
+        cp(of, T.gg[:, 768 + 192 * k:960 + 192 * k:16], ["gr1%d" % k], ["hof%d" % k])
+        pick("zc%d" % k, 0, NT, "ld%d" % k, 0, 50, of, ["hof%d" % k, "ld%d" % k, "ld%ds" % k, "ldz"], "zc%d" % k)
+        for b in range(4):
+            mm(T.pz[:, 512 * b:512 * b + NT], "eq", 128 * b, "zc%d" % k, 0, NT, first, last, ["eq", "zc%d" % k, "zc%ds" % k], ["*z%d" % b])
+        w, wf, wt = (slice(c + 12 * k, c + 12 * k + 12) for c in (0, 48, 96))
+        ts(T.ff[:, w], of, float(CR), None, A.is_lt, None, ["hof%d" % k], ["fl%d" % k])
+        tt(T.ff[:, wf], T.ff[:, w], T.wgt[:, w], A.mult, ["fl%d" % k, "wgt%d0" % k, "wgt%d1" % k], ["fw%d" % k])
+        if not first:
+            v = (36 if k == 1 else 84) + 12 * k
+            tt(T.ff[:, wt], T.ff[:, v:v + 12], T.ff[:, wf], A.add, ["fw%d" % k, "fw0" if k == 1 else "fs%d" % (k - 1)], ["fs%d" % k])
+
+    fill(T.tab[:, :], float(CR), ["tab0"])
+    for k in (1, 2, 3):
+        wrote["tab%d" % k] = wrote["tab0"]
+    stage1(0)
+    quant("uq", 0, 512, "ut", 0, 2048, ["ut"], ["uq"])
+    fill(T.prt[:, 8:512], 0.0, ["prz"])
+    fill(T.zl[:, :], 0, ["zl"])
+    quant("pq", 0, 128, "prt", 0, 512, ["prt", "prz"], ["pq"])
+    pick("pp", 0, 128, "pq", 0, 128, T.zl[:, :], ["pq", "zl"], "pp")
+    fill(T.pt[:, :], 0.0, ["pt"])
+    fill(T.z3[:, :], 0.0, ["z3"])
+    tt(T.pf[:, 11:12], T.pf[:, 0:1], T.pf[:, 1:2], A.subtract, ["pf"], ["pf11"])
+    ts(T.pt[:, 0:11:5], T.z3[:, 0:3], T.pf[:, 11:12], None, A.add, None, ["z3", "pf11", "pt"], ["pth"])
+    ts(T.pt[:, 512:523:5], T.z3[:, 0:3], T.pf[:, 1:2], None, A.add, None, ["z3", "pf", "pt"], ["ptl"])
+    quant("cq", 0, 256, "pt", 0, 1024, ["pt", "pth", "ptl"], ["cq"])
+    fill(T.cs[:, :], 0.0, ["csz"])
+    stage2(0)
+    lookups()
+    stage3(0)
+    home(0, True, False)
+    stage1(1)
+    stage2(1)
+    stage1(2)
+    stage3(1)
+    stage2(2)
+    stage1(3)
+    stage3(2)
+    stage2(3)
+    stage3(3)
+    quant("vq", 0, 128, "vt", 0, 512, ["vt"], ["vq"])
+    home(1, False, False)
+    home(2, False, False)
+    home(3, False, True)
+
+    tt(T.cs[:, 0:6], T.ff[:, 132:144:2], T.ff[:, 133:144:2], A.add, ["fs3", "csz"], ["cs"])
+    turn(T.cst[0:32, :], T.cs[0:32, :], ["cs", "csz"], ["cst"])
+    for b in (0, 1):
+        act(T.zt[:, b:768:4], T.pz[:, 512 * b:512 * b + NT], F.Copy, ["*z%d" % b], ["zt%d" % b])
+    for b in (2, 3):
+        cp(T.zt[:, b:768:4], T.pz[:, 512 * b:512 * b + NT], ["*z%d" % b], ["zt%d" % b])
+    quant("zq", 0, 192, "zt", 0, 768, ["zt0", "zt1", "zt2", "zt3"], ["zq"])
+    mm(T.px[:, 0:NT], "vq", 0, "zq", 0, NT, True, True, ["vq", "zq"], ["*x0"])
+    cp(T.ysb[:, :], T.px[:, 0:NT], ["*x0"], ["ysb"])
+    dma("S", "dos", T.ct[0:1, 0:NT], T.cst[0:6, 0:32], ["cst"], [])
+    dma("Y", "doy", T.oc[:, 0:768], T.zq[:, 0:NT].bitcast(dt.uint8), ["zq"], [])
+    for i in range(4):
+        q, s = ("S", "dos") if i < 3 else ("Y", "doy")
+        dma(q, s, T.osc[4 * i:4 * i + 4, 0:NT], T.zqs[32 * i:32 * i + 4, 0:NT], ["zq"], [])
+    dma("Y", "doy", T.y[:, :], T.ysb[:, :], ["ysb"], [])
+    for s, n in total.items():
+        need("G", (s, n))

@@ -4,10 +4,14 @@ from concourse.mybir import dt, AluOpType as A, AxisListType, ActivationFunction
 NT, CP, CR = 192, 112, 48
 NS = 10
 TINY = 2.0 ** -100
+EPS = 2.0 ** -120
+BELOW = 1.0 - 2.0 ** -24
+HOP, CY, PE, OUT, BACK = 0.11, 0.001, 0.0012, {1: 3.6, 2: 4.5, 3: 4.5}, 3.5
+AHEAD = {"k1": 1.0, "k2": 0.5, "out": 0.5, "first": 99.0}
 
 SCRATCH = {
     "xt": ("sbuf", [128, 776], "bfloat16"), "gt": ("sbuf", [128, 776], "bfloat16"),
-    "rtt": ("sbuf", [128, 512], "bfloat16"), "prt": ("sbuf", [128, 512], "bfloat16"),
+    "rtt": ("sbuf", [128, 512], "bfloat16"), "prt": ("sbuf", [128, 512], "bfloat16"), "nt": ("sbuf", [128, 512], "bfloat16"),
     "wt": ("sbuf", [128, 2048], "bfloat16"), "ut": ("sbuf", [128, 2048], "bfloat16"),
     "vt": ("sbuf", [128, 512], "bfloat16"), "et": ("sbuf", [128, 2048], "bfloat16"),
     "pt": ("sbuf", [128, 1024], "bfloat16"), "zt": ("sbuf", [128, 768], "bfloat16"),
@@ -16,12 +20,10 @@ SCRATCH = {
     "tie": ("sbuf", [128, 8], "float32"), "sb": ("sbuf", [128, 16], "float32"),
     "tri0": ("sbuf", [128, 112], "float32"), "tri": ("sbuf", [128, 112], "float32"),
     "one": ("sbuf", [128, 128], "bfloat16"), "idn": ("sbuf", [128, 128], "bfloat16"),
-    "vals": ("sbuf", [128, 48], "bfloat16"), "k4": ("sbuf", [128, 512], "bfloat16"),
-    "zero": ("sbuf", [128, 192], "bfloat16"), "z3": ("sbuf", [128, 8], "float32"),
+    "vals": ("sbuf", [128, 48], "bfloat16"), "k4": ("sbuf", [128, 512], "bfloat16"), "z3": ("sbuf", [128, 8], "float32"),
     "s0": ("sbuf", [128, 192], "float32"), "dd": ("sbuf", [128, 576], "float32"), "sg": ("sbuf", [128, 576], "bfloat16"),
     "u": ("sbuf", [128, 192], "bfloat16"), "win": ("sbuf", [128, 192], "bfloat16"), "m": ("sbuf", [128, 192], "bfloat16"),
-    "pref": ("sbuf", [128, 192], "bfloat16"),
-    "le": ("sbuf", [128, 192 * 16], "bfloat16"),
+    "pref": ("sbuf", [128, 192], "bfloat16"), "le": ("sbuf", [128, 192 * 16], "bfloat16"),
     "cn": ("sbuf", [128, 32], "float32"), "cnt": ("sbuf", [128, 32], "float32"), "off": ("sbuf", [128, 32], "uint16"),
     "tv": ("sbuf", [128, 384], "bfloat16"), "hh": ("sbuf", [128, 144], "float32"),
     "offt": ("sbuf", [128, 48], "uint16"), "wgt": ("sbuf", [128, 48], "float32"),
@@ -34,7 +36,7 @@ SCRATCH = {
     "pz": ("psum", [128, 2048], "float32"), "px": ("psum", [128, 2048], "float32"),
 }
 _CODES = [("xq", 194), ("gq", 194), ("rq", 128), ("rp", 160), ("pq", 128), ("pp", 128), ("wq", 512), ("uq", 512),
-          ("vq", 128), ("eq", 512), ("cq", 256), ("zq", 192), ("qm", 512), ("qd", 512), ("qo", 512)]
+          ("vq", 128), ("eq", 512), ("cq", 256), ("zq", 192), ("qm", 512), ("qd", 512), ("qo", 512), ("nq", 128)]
 for _k in range(4):
     _CODES += [("lc%d" % _k, 224), ("ld%d" % _k, 64), ("zc%d" % _k, 192)]
     if _k:
@@ -43,7 +45,7 @@ for _n, _w in _CODES:
     SCRATCH[_n] = ("sbuf", [128, _w], "float8_e4m3fn_x4")
     SCRATCH[_n + "s"] = ("sbuf", [128, _w], "uint8")
 
-SEMAPHORES = ["cV", "cS", "cP", "cG", "dx", "dgr", "drt", "dpr", "dw", "dub", "dv", "dz", "doy", "dos", "left"]
+SEMAPHORES = ["cV", "cS", "cP", "cG", "dx", "dgr", "drt", "dpr", "dw", "dub", "dv", "dz", "doy", "dos", "left", "az"]
 for _k in (1, 2, 3):
     SEMAPHORES += ["ax%d" % _k, "al%d" % _k, "ar%d" % _k]
 
@@ -53,129 +55,141 @@ def rank_program(g, core, T, topo):
     if rank is None:
         return
     queue = {"V": g.vector, "S": g.scalar, "P": g.tensor, "G": g, "Y": g.sync}
-    total, waited, wrote, read = {}, {}, {}, {}
+    tasks, wrote, read, total = [], {}, {}, {}
+    turn_of = [""]
 
-    def need(q, tok):
-        if tok and waited.get((q, tok[0]), 0) < tok[1]:
-            queue[q].wait_ge(T.sem[tok[0]], tok[1])
-            waited[(q, tok[0])] = tok[1]
-
-    def deps(q, reads, writes):
-        own = "c" + q
-        toks = []
+    def task(q, call, reads, writes, cost, sem=None, inc=1, late=0.0, after=()):
+        before = {i: True for i in after}
         for k in reads:
-            toks.append(wrote.get(k))
+            if k in wrote:
+                before[wrote[k]] = True
             if k[0] == "*":
-                toks += [t for t in read.get(k, []) if t[0] != own]
+                for i in read.get(k, []):
+                    if tasks[i]["q"] != q:
+                        before[i] = True
         for k in writes:
-            w = wrote.get(k)
-            if not (q == "P" and w and w[0] == own):
-                toks.append(w)
-            toks += [t for t in read.get(k, []) if t[0] != own]
-        best = {}
-        for t in toks:
-            if t:
-                best[t[0]] = max(best.get(t[0], 0), t[1])
-        for s, v in best.items():
-            need(q, (s, v))
-
-    def mark(tok, reads, writes):
+            if k in wrote:
+                i = wrote[k]
+                before[i] = before.get(i, False) or not (q == "P" and tasks[i]["q"] == "P")
+            for i in read.get(k, []):
+                before[i] = before.get(i, False) or tasks[i]["q"] != q
+        n = len(tasks)
+        tasks.append({"q": q, "call": call, "before": before, "cost": cost, "late": late, "sem": sem, "inc": inc,
+                      "ahead": AHEAD.get(turn_of[0], 0.0)})
         for k in reads:
-            read.setdefault(k, []).append(tok)
+            read.setdefault(k, []).append(n)
         for k in writes:
-            wrote[k] = tok
-            read[k] = []
+            wrote[k], read[k] = n, []
+        return n
 
-    def run(q, call, reads, writes):
-        deps(q, reads, writes)
-        s = "c" + q
-        total[s] = total.get(s, 0) + 1
-        call(queue[q]).then_inc(T.sem[s], 1)
-        mark((s, total[s]), reads, writes)
+    def run(q, call, reads, writes, cost):
+        return task(q, call, reads, writes, cost, "c" + q)
 
-    def dma(q, sem, out, in_, reads, writes):
-        deps(q, reads, writes)
-        total[sem] = total.get(sem, 0) + 16
-        queue[q].dma_start(out, in_).then_inc(T.sem[sem], 16)
-        mark((sem, total[sem]), reads, writes)
+    def dma(q, sem, out, in_, reads, writes, late):
+        return task(q, lambda e: e.dma_start(out, in_), reads, writes, 0.06, sem, 16, late)
 
-    def ts(out, in0, s1, s2, o0, o1, reads, writes):
+    def n_of(a):
+        n = 1
+        for w in a.shape[1:]:
+            n *= w
+        return n
+
+    def el(n):
+        return max(64, n) * CY
+
+    def ts(out, in0, s1, s2, o0, o1, reads, writes, fast=False):
+        c = el(n_of(in0) // (2 if fast else 1))
         if o1 is None:
-            run("V", lambda e: e.tensor_scalar(out, in0, s1, None, o0), reads, writes)
+            run("V", lambda e: e.tensor_scalar(out, in0, s1, None, o0), reads, writes, c)
         else:
-            run("V", lambda e: e.tensor_scalar(out, in0, s1, s2, o0, o1), reads, writes)
+            run("V", lambda e: e.tensor_scalar(out, in0, s1, s2, o0, o1), reads, writes, c)
 
-    def tt(out, a, b, op, reads, writes):
-        run("V", lambda e: e.tensor_tensor(out, a, b, op), reads, writes)
+    def tt(out, a, b, op, reads, writes, psum=False):
+        run("V", lambda e: e.tensor_tensor(out, a, b, op), reads, writes, el(n_of(out) * (1 if psum else 2)))
 
-    def cp(out, a, reads, writes):
-        run("V", lambda e: e.tensor_copy(out, a), reads, writes)
+    def cp(out, a, reads, writes, cost=None):
+        run("V", lambda e: e.tensor_copy(out, a), reads, writes, cost or el(n_of(out)))
 
     def turn(out, a, reads, writes):
-        run("V", lambda e: e.transpose(out, a), reads, writes)
+        run("V", lambda e: e.transpose(out, a), reads, writes, el(n_of(out) // 2))
 
     def fill(ap, v, writes):
-        run("V", lambda e: e.memset(ap, v), [], writes)
+        run("V", lambda e: e.memset(ap, v), [], writes, el(n_of(ap) // 2))
 
-    def act(out, a, f, reads, writes, **kw):
-        run("S", lambda e: e.activation(out, a, f, **kw), reads, writes)
+    def act(out, a, f, reads, writes, cost=None, **kw):
+        run("S", lambda e: e.activation(out, a, f, **kw), reads, writes, cost or el(n_of(out)))
+
+    def clear(ap, key):
+        act(ap, T.nt[:, 0:n_of(ap)], F.Copy, ["nt"], [key])
 
     def quant(q, a, b, tile, c, d, reads, writes):
         o, s, i = T[q][:, a:b], T[q + "s"][:, a:b], T[tile][:, c:d]
-        run("V", lambda e: e.quantize_mx(o, s, i), reads, writes)
+        run("V", lambda e: e.quantize_mx(o, s, i), reads, writes, 0.014 + 0.00026 * (d - c))
 
     def mm(out, l, la, r, ra, n, start, stop, reads, writes):
         w, ws, x, xs = T[l][:, la:la + 128], T[l + "s"][:, la:la + 128], T[r][:, ra:ra + n], T[r + "s"][:, ra:ra + n]
-        run("P", lambda e: e.matmul_mx(out, w, ws, x, xs, start, stop), reads, writes)
+        run("P", lambda e: e.matmul_mx(out, w, ws, x, xs, start, stop), reads, writes, (n + 16) * PE)
 
     def pick(dst, c, n, src, a, b, offs, reads, key):
         o, i = T[dst][:, c:c + n].bitcast(dt.uint32), T[src][:, a:b].bitcast(dt.uint32).indirect(offs)
-        run("V", lambda e: e.tensor_copy(o, i), reads, [key])
-        act(T[dst + "s"][:, c:c + n], T[src + "s"][:, a:b].indirect(offs), F.Copy, reads, [key + "s"])
+        cp(o, i, reads, [key], 0.05 + 1.5 * n * CY)
+        act(T[dst + "s"][:, c:c + n], T[src + "s"][:, a:b].indirect(offs), F.Copy, reads, [key + "s"], 0.065 + 1.5 * n * CY)
 
     peer = [T.cores[rank ^ k] for k in range(4)]
     away = [k for k in (1, 2, 3) if topo.chip(peer[k]) != topo.chip(core)]
     out_eng = topo.engines(core, peer[away[0]])
     near_eng = [e for e in topo.engines(core, peer[1]) if e not in out_eng] or out_eng
     eng = {k: (out_eng if k in away else near_eng) for k in (1, 2, 3)}
-    msk = {k: sum(1 << e for e in eng[k]) for k in eng}
+    half = {k: (out_eng[4 * away.index(k):4 * away.index(k) + 4] if k in away else near_eng) for k in (1, 2, 3)}
 
-    def send(k, dst, src, sem):
-        rid, pid, _s = topo.addr(peer[k])
-        total["left"] = total.get("left", 0) + len(eng[k])
-        g.remote_dma(out_ap=dst, in_ap=src, remote_sem=T.sem["%s%d" % (sem, k)], local_sem=T.sem["left"], pid=pid,
-                     routing_id=rid, dma_engine_mask=msk[k])
+    def bits(es):
+        return sum(1 << e for e in es)
 
-    def send_two(ks, dst, src, width, codes, sem):
-        tr = []
-        for k in ks:
-            rid, pid, _s = topo.addr(peer[k])
-            s, d = T[src % k][:, 0:width], T[dst % k][:, 0:width]
-            if codes:
-                s, d = s.bitcast(dt.uint8), d.bitcast(dt.uint8)
-            total["left"] = total.get("left", 0) + len(eng[k])
-            tr.append(RemoteDMATransfer(dst_ids=[DstId(rid=rid, pnc=pid)], dma_engine_mask=msk[k],
-                                        remote_sem=T.sem["%s%d" % (sem, k)], srcs=[s], dsts=[d]))
-        g.remote_dma_fused(tr, local_sem=T.sem["left"])
+    def send(parts, sem, reads, engines):
+        total["left"] = total.get("left", 0) + sum(len(engines[p[0]]) for p in parts)
 
-    for k in (1, 2, 3):
-        n = len(eng[k])
-        wrote["lc%d" % k] = ("ax%d" % k, 2 * n)
-        wrote["ld%d" % k] = wrote["ld%ds" % k] = ("ar%d" % k, 2 * n)
-        wrote["ll%d" % k] = ("al%d" % k, n)
-        total["ax%d" % k] = total["ar%d" % k] = 2 * n
-        total["al%d" % k] = n
+        def call(e):
+            if len(parts) == 1:
+                k, dst, src = parts[0]
+                rid, pid, _s = topo.addr(peer[k])
+                g.remote_dma(out_ap=dst, in_ap=src, remote_sem=T.sem[sem % k], local_sem=T.sem["left"], pid=pid,
+                             routing_id=rid, dma_engine_mask=bits(engines[k]))
+                return
+            tr = []
+            for k, dst, src in parts:
+                rid, pid, _s = topo.addr(peer[k])
+                tr.append(RemoteDMATransfer(dst_ids=[DstId(rid=rid, pnc=pid)], dma_engine_mask=bits(engines[k]),
+                                            remote_sem=T.sem[sem % k if "%" in sem else sem], srcs=[src], dsts=[dst]))
+            g.remote_dma_fused(tr, local_sem=T.sem["left"])
+        return task("G", call, reads, [], 0.9)
 
-    dma("S", "drt", T.rtt[:, 0:16], T.rt[:, 0:16], [], ["rtt"])
-    dma("Y", "dx", T.xt[:, 0:768], T.x[:, :], [], ["xt"])
-    dma("Y", "dgr", T.gt[:, 0:768], T.gr[:, :], [], ["gt"])
-    dma("Y", "dw", T.wt[:, :], T.w[:, :], [], ["wt"])
-    dma("Y", "dpr", T.prt[:, 0:8], T.pr[:, 0:8], [], ["prt"])
-    dma("Y", "dub", T.ut[:, :], T.ub[:, :], [], ["ut"])
-    dma("Y", "dv", T.vt[:, :], T.v[:, :], [], ["vt"])
+    def arrive(sem, n, keys, after, late):
+        total[sem] = total.get(sem, 0) + n
+        return task(None, None, [], keys, 0.0, sem, total[sem], late, after)
+
+    def codes(name, a, b):
+        return T[name][:, a:b].bitcast(dt.uint8)
+
+    dma("S", "drt", T.rtt[:, 0:16], T.rt[:, 0:16], [], ["rtt"], 2.0)
+    dma("Y", "dx", T.xt[:, 0:768], T.x[:, :], [], ["xt"], 3.3)
+    dma("Y", "dgr", T.gt[:, 0:768], T.gr[:, :], [], ["gt"], 4.3)
+    dma("Y", "dw", T.wt[:, :], T.w[:, :], [], ["wt"], 6.7)
+    dma("Y", "dpr", T.prt[:, 0:8], T.pr[:, 0:8], [], ["prt"], 6.9)
+    dma("Y", "dub", T.ut[:, :], T.ub[:, :], [], ["ut"], 9.4)
+    dma("Y", "dv", T.vt[:, :], T.v[:, :], [], ["vt"], 10.0)
+
+    turn_of[0] = "first"
+    fill(T.nt[:, :], 0.0, ["nt"])
+    quant("nq", 0, 128, "nt", 0, 512, ["nt"], ["nq"])
+    a = send([(k, codes("ld%d" % k, 48, 50), codes("nq", 0, 2)) for k in (2, 3, 1)], "az", ["nq"], half)
+    b = send([(k, T["ld%ds" % k][:, 48:50], T.nqs[:, 0:2]) for k in (2, 3, 1)], "az", ["nq"], half)
+    arrive("az", 2 * sum(len(half[k]) for k in half), ["ldz"], [a, b], 6.0)
+    turn_of[0] = ""
+    dma("Y", "dz", codes("ld0", 48, 50), codes("nq", 0, 2), ["nq"], [], 2.0)
+    dma("Y", "dz", T.ld0s[:, 48:50], T.nqs[:, 0:2], ["nq"], ["ldz0"], 2.0)
 
     def iota(out, pattern, base, ch, key, **kw):
-        run("G", lambda e: e.iota(out, pattern, base, ch, **kw), [], [key])
+        run("G", lambda e: e.iota(out, pattern, base, ch, **kw), [], [key], 0.15 + 2 * n_of(out) * CY)
 
     fl_ok = {"allow_small_or_imprecise_dtypes": True}
     iota(T.pi[:, 0:1], [[0, 1]], 0, 1, "pi")
@@ -194,17 +208,18 @@ def rank_program(g, core, T, topo):
     cp(T.pf[:, 0:6], T.pi[:, 0:6], ["pi", "pi1", "pi2", "pi3", "pi4", "pi5"], ["pf"])
     ts(T.rl[:, 0:10], T.ii[:, 16:26], T.pf[:, 2:3], None, A.add, None, ["i10", "pf"], ["rl"])
     ts(T.tie[:, 4:7], T.ii[:, 32:35], T.pf[:, 3:4], 0.5, A.is_gt, A.subtract, ["i3", "pf"], ["tie0"])
-    ts(T.tie[:, 0:3], T.tie[:, 4:7], 2 * TINY, None, A.mult, None, ["tie0"], ["tie"])
+    ts(T.tie[:, 0:2], T.tie[:, 4:6], 2 * TINY, None, A.mult, None, ["tie0"], ["tie"])
+    ts(T.tie[:, 2:3], T.tie[:, 6:7], -2 * TINY, None, A.mult, None, ["tie0"], ["tie3"])
     ts(T.pf[:, 6:7], T.pf[:, 4:5], 16.0, 0.5, A.mult, A.add, ["pf"], ["pf6"])
     ts(T.sb[:, :], T.ii[:, 0:16], T.pf[:, 6:7], None, A.add, None, ["i16", "pf6"], ["sb"])
     ts(T.pf[:, 7:8], T.pf[:, 1:2], float(NS), None, A.is_lt, None, ["pf"], ["pf7"])
     ts(T.pf[:, 8:9], T.pf[:, 7:8], -0.5, 1.0, A.mult, A.add, ["pf7"], ["pf8"])
     ts(T.pf[:, 9:10], T.pf[:, 7:8], 96.0, None, A.mult, None, ["pf7"], ["pf9"])
-    fill(T.zero[:, :], 0.0, ["zero"])
-    fill(T.et[:, :], 0.0, ["et"])
-    fill(T.tri0[:, :], -TINY, ["tri0"])
-    run("G", lambda e: e.affine_select(T.idn[:, :], T.one[:, :], [[-1, 128]], A.is_equal, 0.0, 0, 1), ["one"], ["idn"])
-    run("G", lambda e: e.affine_select(T.tri[:, :], T.tri0[:, :], [[-1, 112]], A.is_gt, 0.0, 0, 1), ["tri0"], ["tri"])
+    for b in range(4):
+        clear(T.et[:, 512 * b:512 * b + 512], "ez%d" % b)
+    fill(T.tri0[:, :], BELOW, ["tri0"])
+    run("G", lambda e: e.affine_select(T.idn[:, :], T.one[:, :], [[-1, 128]], A.is_equal, 0.0, 0, 1), ["one"], ["idn"], 0.4)
+    run("G", lambda e: e.affine_select(T.tri[:, :], T.tri0[:, :], [[-1, 112]], A.is_gt, 1.0, 0, 1), ["tri0"], ["tri"], 0.4)
     iota(T.k4[:, :], [[0, 8], [1, 16], [16, 4]], 0, 0, "k4", **fl_ok)
     iota(T.vals[:, :], [[1, 48]], 0, 0, "vals", **fl_ok)
 
@@ -216,21 +231,25 @@ def rank_program(g, core, T, topo):
     act(T.s0[:, :], T.pz[:, 0:NT], F.Copy, ["*z0"], ["s0"])
     for r in (1, 2, 3):
         a = NT * (r - 1)
-        tt(T.dd[:, a:a + NT], T.s0[:, :], T.pz[:, 512 * r:512 * r + NT], A.subtract, ["s0", "*z%d" % r], ["dd%d" % r])
-        act(T.sg[:, a:a + NT], T.dd[:, a:a + NT], F.Sign, ["dd%d" % r, "tie"], ["sg%d" % r], bias=T.tie[:, r - 1:r])
+        tt(T.dd[:, a:a + NT], T.s0[:, :], T.pz[:, 512 * r:512 * r + NT], A.subtract, ["s0", "*z%d" % r], ["dd%d" % r], True)
+        act(T.sg[:, a:a + NT], T.dd[:, a:a + NT], F.Sign, ["dd%d" % r, "tie", "tie3"], ["sg%d" % r], bias=T.tie[:, r - 1:r],
+            scale=(1.0, 1.0, -1.0)[r - 1])
     tt(T.u[:, :], T.sg[:, 0:NT], T.sg[:, NT:2 * NT], A.add, ["sg1", "sg2"], ["u"])
-    tt(T.win[:, :], T.u[:, :], T.sg[:, 2 * NT:3 * NT], A.add, ["u", "sg3"], ["win"])
-    ts(T.m[:, :], T.win[:, :], 0.0, None, A.is_gt, None, ["win"], ["m"])
-    run("V", lambda e: e.tensor_tensor_scan(T.pref[:, :], T.m[:, :], T.zero[:, :], 0.0, A.add, A.add), ["m", "zero"], ["pref"])
+    tt(T.m[:, :], T.u[:, :], T.sg[:, 2 * NT:3 * NT], A.is_gt, ["u", "sg3"], ["m"])
+    run("V", lambda e: e.tensor_tensor_scan(T.pref[:, :], T.m[:, :], T.nt[:, 0:NT], 0.0, A.add, A.add), ["m", "nt"], ["pref"], 0.1)
     for t in range(NS):
         act(T.le[:, NT * t:NT * t + NT], T.pref[:, :], F.Sign, ["pref", "sb"], ["cn%d" % t], bias=T.sb[:, t:t + 1], scale=-1.0,
             accum_out=T.cn[:, t:t + 1])
     for t in range(NS, 16):
         a = NT * t
-        ts(T.le[:, a:a + NT], T.pref[:, :], T.sb[:, t:t + 1], None, A.is_le, None, ["pref", "sb"], ["le%d" % t])
-    for t in range(NS, 16):
+        ts(T.le[:, a:a + NT], T.pref[:, :], T.sb[:, t:t + 1], None, A.is_le, None, ["pref", "sb"], ["le%d" % t], True)
+
+    def count(t):
         a, o = T.le[:, NT * t:NT * t + NT], T.cn[:, t:t + 1]
-        run("V", lambda e: e.tensor_reduce(o, a, AxisListType.X, A.add), ["le%d" % t], ["cn%d" % t])
+        run("V", lambda e: e.tensor_reduce(o, a, AxisListType.X, A.add), ["le%d" % t], ["cn%d" % t], 0.19)
+
+    for t in range(NS, 16):
+        count(t)
     quant("gq", 0, 194, "gt", 0, 776, ["gt", "gz"], ["gq"])
     cns = ["cn%d" % t for t in range(16)]
     cp(T.cn[:, 16:32], T.cn[:, 0:16], cns, ["cnd"])
@@ -238,123 +257,152 @@ def rank_program(g, core, T, topo):
     ts(T.off[:, :], T.cnt[:, :], T.pf[:, 8:9], T.pf[:, 9:10], A.mult, A.add, ["cnt", "pf8", "pf9"], ["off"])
 
     def take(k):
-        e = rank ^ k
-        o = T.off[:, 8 * e:8 * e + 7]
+        o = T.off[:, 8 * (rank ^ k):8 * (rank ^ k) + 7]
         d = ("sc%d" if k else "lc%d") % k
-        for c, src, part in ((CP, "xq", "x"), (0, "gq", "g")):
+
+        def part(c, src, key):
             oc, ic = T[d][:, c:c + CP].bitcast(dt.uint32), T[src][:, 0:194].bitcast(dt.uint32).indirect(o)
-            run("V", lambda q: q.tensor_copy(oc, ic), [src, "off"], [d + part])
-            act(T[d + "s"][:, c:c + CP], T[src + "s"][:, 0:194].indirect(o), F.Copy, [src, "off"], [d + part + "s"])
+            cp(oc, ic, [src, "off"], [d + key], 0.05 + 1.5 * CP * CY)
+            act(T[d + "s"][:, c:c + CP], T[src + "s"][:, 0:194].indirect(o), F.Copy, [src, "off"], [d + key + "s"], 0.065 + 1.5 * CP * CY)
+        part(CP, "xq", "x")
+        part(0, "gq", "g")
 
     def go(ks):
-        deps("G", [n % k for k in ks for n in ("sc%dx", "sc%dg")], [])
-        send_two(ks, "lc%d", "sc%d", 2 * CP, True, "ax")
-        deps("G", [n % k for k in ks for n in ("sc%dxs", "sc%dgs")], [])
-        send_two(ks, "lc%ds", "sc%ds", 2 * CP, False, "ax")
+        a = send([(k, codes("lc%d" % k, 0, 2 * CP), codes("sc%d" % k, 0, 2 * CP)) for k in ks], "ax%d",
+                 [n % k for k in ks for n in ("sc%dx", "sc%dg")], eng)
+        b = send([(k, T["lc%ds" % k][:, 0:2 * CP], T["sc%ds" % k][:, 0:2 * CP]) for k in ks], "ax%d",
+                 [n % k for k in ks for n in ("sc%dxs", "sc%dgs")], eng)
+        for k in ks:
+            arrive("ax%d" % k, 2 * len(eng[k]), ["lc%d" % k], [a, b], OUT[k])
 
+    turn_of[0] = "out"
     take(2)
     take(1)
     go((2, 1))
     take(3)
     go((3,))
+    turn_of[0] = ""
     take(0)
     came = {k: ["lc%d" % k] for k in (1, 2, 3)}
     came[0] = ["lc0x", "lc0g", "lc0xs", "lc0gs"]
 
     for b in range(4):
-        act(T.et[:, 512 * b + b:512 * b + 512:4], T.idn[:, :], F.Copy, ["idn", "et"], ["et%d" % b])
-    quant("eq", 0, 512, "et", 0, 2048, ["et", "et0", "et1", "et2", "et3"], ["eq"])
+        act(T.et[:, 512 * b + b:512 * b + 512:4], T.idn[:, :], F.Copy, ["idn", "ez%d" % b], ["et%d" % b])
+    quant("eq", 0, 512, "et", 0, 2048, ["et0", "et1", "et2", "et3"], ["eq"])
     quant("wq", 0, 512, "wt", 0, 2048, ["wt"], ["wq"])
+    quant("uq", 0, 512, "ut", 0, 2048, ["ut"], ["uq"])
+    quant("vq", 0, 128, "vt", 0, 512, ["vt"], ["vq"])
+    clear(T.prt[:, 8:512], "prz")
+    fill(T.zl[:, :], 0, ["zl"])
+    quant("pq", 0, 128, "prt", 0, 512, ["prt", "prz"], ["pq"])
+    pick("pp", 0, 128, "pq", 0, 128, T.zl[:, :], ["pq", "zl"], "pp")
+    clear(T.pt[:, 0:512], "pt0")
+    clear(T.pt[:, 512:1024], "pt1")
+    fill(T.z3[:, :], 0.0, ["z3"])
+    tt(T.pf[:, 11:12], T.pf[:, 0:1], T.pf[:, 1:2], A.subtract, ["pf"], ["pf11"])
+    ts(T.pt[:, 0:11:5], T.z3[:, 0:3], T.pf[:, 11:12], None, A.add, None, ["z3", "pf11", "pt0"], ["pth"])
+    ts(T.pt[:, 512:523:5], T.z3[:, 0:3], T.pf[:, 1:2], None, A.add, None, ["z3", "pf", "pt1"], ["ptl"])
+    quant("cq", 0, 256, "pt", 0, 1024, ["pt0", "pt1", "pth", "ptl"], ["cq"])
     for k in range(4):
-        fill(T.mt[:, 512 * k + 448:512 * k + 512], 0.0, ["mz%d" % k])
-        fill(T.dxt[:, 512 * k + 448:512 * k + 512], 0.0, ["dz%d" % k])
-    for k in range(4):
-        dma("Y", "dz", T["ld%d" % k][:, 48:50].bitcast(dt.uint8), T.xq[:, 192:194].bitcast(dt.uint8), ["xq"], [])
-        dma("Y", "dz", T["ld%ds" % k][:, 48:50], T.xqs[:, 192:194], ["xq"], [])
-    wrote["ldz"] = ("dz", total["dz"])
+        clear(T.mt[:, 512 * k + 448:512 * k + 512], "mz%d" % k)
+        clear(T.dxt[:, 512 * k + 448:512 * k + 512], "dz%d" % k)
+
+    def bank(k, x):
+        return (T.px if k % 2 else T.pz), 512 * x, "*%s%d" % ("zx"[k % 2], x)
 
     def stage1(k):
         lc, c = "lc%d" % k, came[k]
-        for h in (0, 2):
-            for b in (h, h + 1):
-                x = 512 * (b % 2)
-                mm(T.px[:, x:x + 128], "wq", 128 * b, lc, 96, 128, True, True, ["wq"] + c, ["*x%d" % (b % 2)])
-                o = 448 * k + CP * b
-                act(T.sm[:, o:o + CP], T.px[:, x + 16:x + 128], F.Sign, ["*x%d" % (b % 2)], ["sm%d_%d" % (k, b)])
-            for b in (h, h + 1):
-                x = 1024 + 512 * (b % 2)
-                mm(T.px[:, x:x + 128], "eq", 128 * b, lc, 0, 128, True, True, ["eq"] + c, ["*x%d" % (2 + b % 2)])
-            o = 448 * k + CP * h
-            ts(T.mk[:, o:o + 2 * CP], T.sm[:, o:o + 2 * CP], 0.0, None, A.max, None,
-               ["sm%d_%d" % (k, h), "sm%d_%d" % (k, h + 1)], ["mk%d_%d" % (k, h)])
-            for b in (h, h + 1):
-                o, x = 448 * k + CP * b, 1024 + 512 * (b % 2)
-                tt(T.mt[:, 512 * k + b:512 * k + 448:4], T.mk[:, o:o + CP], T.px[:, x:x + CP], A.mult,
-                   ["mk%d_%d" % (k, h), "*x%d" % (2 + b % 2)], ["mt%d_%d" % (k, b)])
+        for b in range(4):
+            ps, x, key = bank(k, b % 2)
+            mm(ps[:, x:x + 128], "wq", 128 * b, lc, 96, 128, True, True, ["wq"] + c, [key])
+            o = 448 * k + CP * b
+            if b == 3:
+                ts(T.mk[:, o:o + CP], ps[:, x + 16:x + 128], 0.0, None, A.is_gt, None, [key], ["mk%d_%d" % (k, b)])
+            else:
+                act(T.sm[:, o:o + CP], ps[:, x + 16:x + 128], F.Sign, [key], ["sm%d_%d" % (k, b)])
+                act(T.mk[:, o:o + CP], T.sm[:, o:o + CP], F.Relu, ["sm%d_%d" % (k, b)], ["mk%d_%d" % (k, b)])
+            ps, x, key = bank(k, 2 + b % 2)
+            mm(ps[:, x:x + 128], "eq", 128 * b, lc, 0, 128, True, True, ["eq"] + c, [key])
+            tt(T.mt[:, 512 * k + b:512 * k + 448:4], T.mk[:, o:o + CP], ps[:, x:x + CP], A.mult,
+               ["mk%d_%d" % (k, b), key], ["mt%d_%d" % (k, b)], True)
         quant("qm", 128 * k, 128 * k + 128, "mt", 512 * k, 512 * k + 512,
               ["mz%d" % k] + ["mt%d_%d" % (k, b) for b in range(4)], ["qm%d" % k])
 
     def stage2(k):
         m = "qm%d" % k
-        mm(T.px[:, 512:640], "qm", 128 * k, "pp", 0, 128, True, True, [m, "pp", "pps"], ["*x1"])
-        mm(T.px[:, 0:128], "pp", 0, "qm", 128 * k, 128, True, True, [m, "pp", "pps"], ["*x0"])
-        act(T.ca[:, 4 * k:4 * k + 1], T.px[:, 512:513], F.Abs, ["*x1"], ["ca%d" % k])
+        pc, xc, kc = bank(k, 1)
+        pr, xr, kr = bank(k, 0)
+        mm(pc[:, xc:xc + 128], "qm", 128 * k, "pp", 0, 128, True, True, [m, "pp", "pps"], [kc])
+        mm(pr[:, xr:xr + 128], "pp", 0, "qm", 128 * k, 128, True, True, [m, "pp", "pps"], [kr])
+        act(T.ca[:, 4 * k:4 * k + 1], pc[:, xc:xc + 1], F.Abs, [kc, "eps"], ["ca%d" % k], bias=T.pf[:, 12:13])
         s, sd, sx = (slice(c + CP * k, c + CP * k + CP) for c in (0, 448, 896))
-        act(T.ra[:, s], T.px[:, 0:CP], F.Abs, ["*x0"], ["ra%d" % k])
-        ts(T.ra[:, sd], T.ra[:, s], T.ca[:, 4 * k:4 * k + 1], None, A.subtract, None, ["ra%d" % k, "ca%d" % k], ["rd%d" % k])
-        tt(T.ra[:, sx], T.ra[:, sd], T.tri[:, :], A.is_gt, ["rd%d" % k, "tri"], ["rx%d" % k])
-        run("V", lambda e: e.tensor_reduce(T.rk[:, 4 * k:4 * k + 1], T.ra[:, sx], AxisListType.X, A.add), ["rx%d" % k], ["rk%d" % k])
-        ts(T.ot[:, 512 * k:512 * k + 512], T.k4[:, :], T.rk[:, 4 * k:4 * k + 1], None, A.is_equal, None, ["k4", "rk%d" % k], ["ot%d" % k])
+        act(T.ra[:, s], pr[:, xr:xr + CP], F.Abs, [kr, "eps"], ["ra%d" % k], bias=T.pf[:, 12:13])
+        act(T.ra[:, sd], T.tri[:, :], F.Copy, ["tri", "ca%d" % k], ["rd%d" % k], scale=T.ca[:, 4 * k:4 * k + 1])
+        tt(T.ra[:, sx], T.ra[:, s], T.ra[:, sd], A.is_gt, ["rd%d" % k, "ra%d" % k], ["rx%d" % k])
+        run("V", lambda e: e.tensor_reduce(T.rk[:, 4 * k:4 * k + 1], T.ra[:, sx], AxisListType.X, A.add), ["rx%d" % k], ["rk%d" % k], 0.11)
+        ts(T.ot[:, 512 * k:512 * k + 512], T.k4[:, :], T.rk[:, 4 * k:4 * k + 1], None, A.is_equal, None, ["k4", "rk%d" % k], ["ot%d" % k], True)
         quant("qo", 128 * k, 128 * k + 128, "ot", 512 * k, 512 * k + 512, ["ot%d" % k], ["qo%d" % k])
-        for b, x in ((0, 2), (1, 3), (2, 1), (3, 0)):
-            mm(T.px[:, 512 * x:512 * x + 128], "uq", 128 * b, "qm", 128 * k, 128, True, True, ["uq", m], ["*x%d" % x])
-            act(T.dxt[:, 512 * k + b:512 * k + 448:4], T.px[:, 512 * x:512 * x + CP], F.Copy, ["*x%d" % x], ["dt%d_%d" % (k, b)], scale=0.0625)
+        for b, y in ((0, 2), (1, 3), (2, 1), (3, 0)):
+            ps, x, key = bank(k, y)
+            mm(ps[:, x:x + 128], "uq", 128 * b, "qm", 128 * k, 128, True, True, ["uq", m], [key])
+            act(T.dxt[:, 512 * k + b:512 * k + 448:4], ps[:, x:x + CP], F.Copy, [key], ["dt%d_%d" % (k, b)], scale=0.0625)
 
     def stage3(k):
+        ps, x, key = bank(k, 2)
         for c in (0, 1):
-            mm(T.px[:, 1024:1152], "qo", 128 * k, "cq", 128 * c, 128, c == 0, c == 1, ["qo%d" % k, "cq"], ["*x2"])
+            mm(ps[:, x:x + 128], "qo", 128 * k, "cq", 128 * c, 128, c == 0, c == 1, ["qo%d" % k, "cq"], [key])
         quant("qd", 128 * k, 128 * k + 128, "dxt", 512 * k, 512 * k + 512,
               ["dz%d" % k] + ["dt%d_%d" % (k, b) for b in range(4)], ["qd%d" % k])
-        cp(T.lo[:, 8 * k:8 * k + 3], T.px[:, 1024:1027], ["*x2"], ["lo%d" % k])
+        cp(T.lo[:, 8 * k:8 * k + 3], ps[:, x:x + 3], [key], ["lo%d" % k])
         d = ("sd%d" if k else "ld%d") % k
         pick(d, 0, CR, "qd", 128 * k, 128 * k + 128, T.lo[:, 8 * k:8 * k + 3], ["qd%d" % k, "lo%d" % k], d)
         if k:
-            deps("G", ["lo%d" % k], [])
-            send(k, T.ll[:, 8 * k:8 * k + 3], T.lo[:, 8 * k:8 * k + 3], "al")
-            deps("G", [d], [])
-            send(k, T["ld%d" % k][:, 0:CR].bitcast(dt.uint8), T[d][:, 0:CR].bitcast(dt.uint8), "ar")
-            deps("G", [d + "s"], [])
-            send(k, T["ld%ds" % k][:, 0:CR], T[d + "s"][:, 0:CR], "ar")
+            a = send([(k, T.ll[:, 8 * k:8 * k + 3], T.lo[:, 8 * k:8 * k + 3])], "al%d", ["lo%d" % k], eng)
+            b = send([(k, codes("ld%d" % k, 0, CR), codes(d, 0, CR))], "ar%d", [d], eng)
+            c = send([(k, T["ld%ds" % k][:, 0:CR], T[d + "s"][:, 0:CR])], "ar%d", [d + "s"], eng)
+            arrive("al%d" % k, len(eng[k]), ["ll%d" % k], [a], BACK)
+            arrive("ar%d" % k, 2 * len(eng[k]), ["ld%d" % k, "ld%ds" % k], [b, c], BACK)
 
-    def lookups():
-        h1, h2, h3, h4, h5, h6 = (T.hh[:, 24 * i:24 * i + 24] for i in range(6))
-        turn(T.tv[:, 0:NT], T.win[:, :], ["win"], ["tw"])
-        turn(T.tv[:, NT:2 * NT], T.pref[:, :], ["pref"], ["tp"])
-        tw, tp = T.tv[:, 0:NT:8], T.tv[:, NT:2 * NT:8]
-        ts(h1, tw, 0.0, None, A.is_gt, None, ["tw"], ["h1"])
-        ts(h2, tp, float(CP), None, A.is_le, None, ["tp"], ["h2"])
-        ts(h3, tp, float(CP + 1), None, A.subtract, None, ["tp"], ["h3"])
-        ts(h6, tw, -0.5, 2.5, A.mult, A.add, ["tw"], ["h6"])
-        tt(h4, h1, h2, A.mult, ["h1", "h2"], ["h4"])
-        tt(h5, h4, h3, A.mult, ["h4", "h3"], ["h5"])
-        ts(T.pf[:, 10:11], T.pf[:, 5:6], -1.0, 1.0, A.mult, A.add, ["pf"], ["pf10"])
-        for k in range(4):
-            e = rank ^ k
-            for h in (0, 1):
-                o, p = slice(12 * k + h, 12 * k + 12, 2), (10, 5)[h]
-                ts(T.offt[:, o], T.hh[:, 96 + e:120:4], float(CP), None, A.add, None, ["h5"], ["offt%d%d" % (k, h)])
-                ts(T.wgt[:, o], T.hh[:, 120 + e:144:4], T.pf[:, p:p + 1], None, A.mult, None, ["h6", "pf", "pf10"], ["wgt%d%d" % (k, h)])
+    fill(T.pf[:, 12:13], EPS, ["eps"])
+    for k in range(4):
+        turn_of[0] = "k%d" % k
+        stage1(k)
+        stage2(k)
+        stage3(k)
+    turn_of[0] = ""
+
+    h1, h2, h3, h4, h5, h6 = (T.hh[:, 24 * i:24 * i + 24] for i in range(6))
+    tt(T.win[:, :], T.u[:, :], T.sg[:, 2 * NT:3 * NT], A.subtract, ["u", "sg3"], ["win"])
+    turn(T.tv[:, 0:NT], T.win[:, :], ["win"], ["tw"])
+    turn(T.tv[:, NT:2 * NT], T.pref[:, :], ["pref"], ["tp"])
+    tw, tp = T.tv[:, 0:NT:8], T.tv[:, NT:2 * NT:8]
+    ts(h1, tw, 0.0, None, A.is_gt, None, ["tw"], ["h1"])
+    ts(h2, tp, float(CP), None, A.is_le, None, ["tp"], ["h2"])
+    ts(h3, tp, float(CP + 1), None, A.subtract, None, ["tp"], ["h3"])
+    ts(h6, tw, -0.5, 2.5, A.mult, A.add, ["tw"], ["h6"])
+    tt(h4, h1, h2, A.mult, ["h1", "h2"], ["h4"])
+    tt(h5, h4, h3, A.mult, ["h4", "h3"], ["h5"])
+    ts(T.pf[:, 10:11], T.pf[:, 5:6], -1.0, 1.0, A.mult, A.add, ["pf"], ["pf10"])
+    for k in range(4):
+        e = rank ^ k
+        for h in (0, 1):
+            o, p = slice(12 * k + h, 12 * k + 12, 2), (10, 5)[h]
+            ts(T.offt[:, o], T.hh[:, 96 + e:120:4], float(CP), None, A.add, None, ["h5"], ["offt%d%d" % (k, h)])
+            act(T.wgt[:, o], T.hh[:, 120 + e:144:4], F.Copy, ["h6", "pf", "pf10"], ["wgt%d%d" % (k, h)], scale=T.pf[:, p:p + 1])
+    for k in range(4):
+        fill(T.tab[:, 128 * k:128 * k + 128], float(CR), ["tab%d" % k])
+    fill(T.cs[:, :], 0.0, ["csz"])
 
     def home(k, first, last):
         tab = T.tab[:, 128 * k:128 * k + 128]
         lst, key = (T.ll[:, 8 * k:8 * k + 3], "ll%d" % k) if k else (T.lo[:, 0:3], "lo0")
         s, s1 = slice(192 * k, 192 * k + 192), slice(768 + 192 * k, 960 + 192 * k)
-        cp(tab.indirect(lst), T.vals[:, :], ["vals", key], ["tab%d" % k])
-        cp(T.gg[:, s], tab.indirect(T.offt[:, 12 * k:12 * k + 12]), ["tab%d" % k, "offt%d0" % k, "offt%d1" % k], ["gr0%d" % k])
+        cp(tab.indirect(lst), T.vals[:, :], ["vals", key], ["tab%d" % k], 0.23)
+        cp(T.gg[:, s], tab.indirect(T.offt[:, 12 * k:12 * k + 12]), ["tab%d" % k, "offt%d0" % k, "offt%d1" % k], ["gr0%d" % k], 0.34)
         turn(T.gg[:, s1], T.gg[:, s], ["gr0%d" % k], ["gr1%d" % k])
         of = T.hof[:, 16 * k:16 * k + 12]
         cp(of, T.gg[:, 768 + 192 * k:960 + 192 * k:16], ["gr1%d" % k], ["hof%d" % k])
-        pick("zc%d" % k, 0, NT, "ld%d" % k, 0, 50, of, ["hof%d" % k, "ld%d" % k, "ld%ds" % k, "ldz"], "zc%d" % k)
+        pick("zc%d" % k, 0, NT, "ld%d" % k, 0, 50, of, ["hof%d" % k, "ld%d" % k, "ld%ds" % k, "ldz" if k else "ldz0"], "zc%d" % k)
         for b in range(4):
             mm(T.pz[:, 512 * b:512 * b + NT], "eq", 128 * b, "zc%d" % k, 0, NT, first, last, ["eq", "zc%d" % k, "zc%ds" % k], ["*z%d" % b])
         w, wf, wt = (slice(c + 12 * k, c + 12 * k + 12) for c in (0, 48, 96))
@@ -364,42 +412,9 @@ def rank_program(g, core, T, topo):
             v = (36 if k == 1 else 84) + 12 * k
             tt(T.ff[:, wt], T.ff[:, v:v + 12], T.ff[:, wf], A.add, ["fw%d" % k, "fw0" if k == 1 else "fs%d" % (k - 1)], ["fs%d" % k])
 
-    fill(T.tab[:, :], float(CR), ["tab0"])
-    for k in (1, 2, 3):
-        wrote["tab%d" % k] = wrote["tab0"]
-    stage1(0)
-    quant("uq", 0, 512, "ut", 0, 2048, ["ut"], ["uq"])
-    fill(T.prt[:, 8:512], 0.0, ["prz"])
-    fill(T.zl[:, :], 0, ["zl"])
-    quant("pq", 0, 128, "prt", 0, 512, ["prt", "prz"], ["pq"])
-    pick("pp", 0, 128, "pq", 0, 128, T.zl[:, :], ["pq", "zl"], "pp")
-    fill(T.pt[:, :], 0.0, ["pt"])
-    fill(T.z3[:, :], 0.0, ["z3"])
-    tt(T.pf[:, 11:12], T.pf[:, 0:1], T.pf[:, 1:2], A.subtract, ["pf"], ["pf11"])
-    ts(T.pt[:, 0:11:5], T.z3[:, 0:3], T.pf[:, 11:12], None, A.add, None, ["z3", "pf11", "pt"], ["pth"])
-    ts(T.pt[:, 512:523:5], T.z3[:, 0:3], T.pf[:, 1:2], None, A.add, None, ["z3", "pf", "pt"], ["ptl"])
-    quant("cq", 0, 256, "pt", 0, 1024, ["pt", "pth", "ptl"], ["cq"])
-    fill(T.cs[:, :], 0.0, ["csz"])
-    stage2(0)
-    lookups()
-    stage3(0)
-    home(0, True, False)
-    stage1(1)
-    stage2(1)
-    stage1(2)
-    stage3(1)
-    stage2(2)
-    stage1(3)
-    stage3(2)
-    stage2(3)
-    stage3(3)
-    quant("vq", 0, 128, "vt", 0, 512, ["vt"], ["vq"])
-    home(1, False, False)
-    home(2, False, False)
-    home(3, False, True)
+    for k in range(4):
+        home(k, k == 0, k == 3)
 
-    tt(T.cs[:, 0:6], T.ff[:, 132:144:2], T.ff[:, 133:144:2], A.add, ["fs3", "csz"], ["cs"])
-    turn(T.cst[0:32, :], T.cs[0:32, :], ["cs", "csz"], ["cst"])
     for b in (0, 1):
         act(T.zt[:, b:768:4], T.pz[:, 512 * b:512 * b + NT], F.Copy, ["*z%d" % b], ["zt%d" % b])
     for b in (2, 3):
@@ -407,11 +422,80 @@ def rank_program(g, core, T, topo):
     quant("zq", 0, 192, "zt", 0, 768, ["zt0", "zt1", "zt2", "zt3"], ["zq"])
     mm(T.px[:, 0:NT], "vq", 0, "zq", 0, NT, True, True, ["vq", "zq"], ["*x0"])
     cp(T.ysb[:, :], T.px[:, 0:NT], ["*x0"], ["ysb"])
-    dma("S", "dos", T.ct[0:1, 0:NT], T.cst[0:6, 0:32], ["cst"], [])
-    dma("Y", "doy", T.oc[:, 0:768], T.zq[:, 0:NT].bitcast(dt.uint8), ["zq"], [])
+    tt(T.cs[:, 0:6], T.ff[:, 132:144:2], T.ff[:, 133:144:2], A.add, ["fs3", "csz"], ["cs"])
+    turn(T.cst[0:32, :], T.cs[0:32, :], ["cs", "csz"], ["cst"])
+    dma("S", "dos", T.ct[0:1, 0:NT], T.cst[0:6, 0:32], ["cst"], [], 2.0)
+    dma("Y", "doy", T.oc[:, 0:768], T.zq[:, 0:NT].bitcast(dt.uint8), ["zq"], [], 2.0)
     for i in range(4):
         q, s = ("S", "dos") if i < 3 else ("Y", "doy")
-        dma(q, s, T.osc[4 * i:4 * i + 4, 0:NT], T.zqs[32 * i:32 * i + 4, 0:NT], ["zq"], [])
-    dma("Y", "doy", T.y[:, :], T.ysb[:, :], ["ysb"], [])
-    for s, n in total.items():
-        need("G", (s, n))
+        dma(q, s, T.osc[4 * i:4 * i + 4, 0:NT], T.zqs[32 * i:32 * i + 4, 0:NT], ["zq"], [], 2.0)
+    dma("Y", "doy", T.y[:, :], T.ysb[:, :], ["ysb"], [], 2.0)
+
+    n = len(tasks)
+    follow = [[] for _i in range(n)]
+    for i, t in enumerate(tasks):
+        for j in t["before"]:
+            follow[j].append(i)
+    rest = [0.0] * n
+    for i in range(n - 1, -1, -1):
+        far = max([rest[j] + (HOP if tasks[j]["before"][i] else 0.0) for j in follow[i]] or [0.0])
+        rest[i] = far + tasks[i]["cost"] + tasks[i]["late"] + tasks[i]["ahead"]
+    left = [len(t["before"]) for t in tasks]
+    ready = [0.0] * n
+    free = {q: 0.0 for q in ("V", "S", "P", "G", "Y", None)}
+    able = [i for i in range(n) if not left[i]]
+    order = []
+    while able:
+        best = None
+        for q in free:
+            mine = [i for i in able if tasks[i]["q"] == q]
+            if not mine:
+                continue
+            at = max(free[q], min(ready[i] for i in mine)) if q else min(ready[i] for i in mine)
+            pool = [i for i in mine if ready[i] <= at + 1e-9]
+            i = min(pool) if q == "Y" else max(pool, key=lambda j: rest[j])
+            for j in mine:
+                if q not in ("Y", None) and ready[j] < at + 0.5 * tasks[i]["cost"] and rest[j] > rest[i] + 1.0:
+                    i = j
+            at = max(at, ready[i])
+            if best is None or at < best[0]:
+                best = (at, i)
+        at, i = best
+        t = tasks[i]
+        able.remove(i)
+        order.append(i)
+        if t["q"]:
+            free[t["q"]] = at + t["cost"]
+        done = at + t["cost"] + t["late"]
+        for j in follow[i]:
+            ready[j] = max(ready[j], done + HOP if tasks[j]["before"][i] else at + t["cost"])
+            left[j] -= 1
+            if not left[j]:
+                able.append(j)
+
+    waited, token = {}, {}
+
+    def need(q, tok):
+        if waited.get((q, tok[0]), 0) < tok[1]:
+            queue[q].wait_ge(T.sem[tok[0]], tok[1])
+            waited[(q, tok[0])] = tok[1]
+
+    for i in order:
+        t = tasks[i]
+        if t["q"] is None:
+            token[i] = (t["sem"], t["inc"])
+            continue
+        best = {}
+        for j, full in t["before"].items():
+            if full:
+                s, v = token[j]
+                best[s] = max(best.get(s, 0), v)
+        for s, v in best.items():
+            need(t["q"], (s, v))
+        made = t["call"](queue[t["q"]])
+        if t["sem"]:
+            made.then_inc(T.sem[t["sem"]], t["inc"])
+            total[t["sem"]] = total.get(t["sem"], 0) + t["inc"]
+            token[i] = (t["sem"], total[t["sem"]])
+    for s, v in total.items():
+        need("G", (s, v))

@@ -2,32 +2,36 @@ from concourse.bass import DstId, RemoteDMATransfer
 from concourse.mybir import dt, AluOpType as A, AxisListType, ActivationFunctionType as F
 
 NT, CP, CR = 192, 112, 48
-NS = 10
+NS = 7
 TINY = 2.0 ** -100
 EPS = 2.0 ** -120
 BELOW = 1.0 - 2.0 ** -24
 HOP, CY, PE, OUT, BACK = 0.11, 0.001, 0.0012, {1: 3.6, 2: 4.5, 3: 4.5}, 3.5
-AHEAD = {"k1": 1.0, "k2": 0.5, "out": 0.5, "first": 99.0}
+AHEAD = {"first": 99.0, "route": 5.3, "prep": -9.2, "out": -1.6, "look": -1.4, "ct": -0.3, "": -4.1,
+         "k0": -1.0, "k0b": 0.3, "k0c": 1.8, "k1": 1.5, "k1b": 0.8, "k1c": 0.3, "k2": 1.6, "k2b": 0.4, "k2c": -0.5,
+         "k3": 0.2, "k3b": 0.0, "k3c": -0.2, "h0": -19.3, "h1": -9.4, "h2": 0.1, "h3": -12.4}
+HOLD, GAP = 0.3, 1.0
 
 SCRATCH = {
     "xt": ("sbuf", [128, 776], "bfloat16"), "gt": ("sbuf", [128, 776], "bfloat16"),
-    "rtt": ("sbuf", [128, 512], "bfloat16"), "prt": ("sbuf", [128, 512], "bfloat16"), "nt": ("sbuf", [128, 512], "bfloat16"),
+    "rtt": ("sbuf", [128, 512], "bfloat16"), "prt": ("sbuf", [128, 512], "bfloat16"), "nt": ("sbuf", [128, 768], "bfloat16"),
     "wt": ("sbuf", [128, 2048], "bfloat16"), "ut": ("sbuf", [128, 2048], "bfloat16"),
     "vt": ("sbuf", [128, 512], "bfloat16"), "et": ("sbuf", [128, 2048], "bfloat16"),
     "pt": ("sbuf", [128, 1024], "bfloat16"), "zt": ("sbuf", [128, 768], "bfloat16"),
-    "pi": ("sbuf", [128, 8], "int32"), "pf": ("sbuf", [128, 16], "float32"), "ii": ("sbuf", [128, 48], "float32"),
+    "pi": ("sbuf", [128, 16], "int32"), "pf": ("sbuf", [128, 24], "float32"), "ii": ("sbuf", [128, 48], "float32"),
     "rl": ("sbuf", [128, 16], "uint16"), "zl": ("sbuf", [128, 8], "uint16"),
     "tie": ("sbuf", [128, 8], "float32"), "sb": ("sbuf", [128, 16], "float32"),
     "tri0": ("sbuf", [128, 112], "float32"), "tri": ("sbuf", [128, 112], "float32"),
     "one": ("sbuf", [128, 128], "bfloat16"), "idn": ("sbuf", [128, 128], "bfloat16"),
     "vals": ("sbuf", [128, 48], "bfloat16"), "k4": ("sbuf", [128, 512], "bfloat16"), "z3": ("sbuf", [128, 8], "float32"),
     "s0": ("sbuf", [128, 192], "float32"), "dd": ("sbuf", [128, 576], "float32"), "sg": ("sbuf", [128, 576], "bfloat16"),
-    "u": ("sbuf", [128, 192], "bfloat16"), "win": ("sbuf", [128, 192], "bfloat16"), "m": ("sbuf", [128, 192], "bfloat16"),
-    "pref": ("sbuf", [128, 192], "bfloat16"), "le": ("sbuf", [128, 192 * 16], "bfloat16"),
+    "seg": ("sbuf", [128, 576], "bfloat16"), "ss": ("sbuf", [128, 576], "bfloat16"),
+    "win": ("sbuf", [128, 192], "bfloat16"), "m": ("sbuf", [128, 192], "bfloat16"), "pref": ("sbuf", [128, 192], "bfloat16"),
+    "le": ("sbuf", [128, 192 * (32 - NS)], "bfloat16"),
     "cn": ("sbuf", [128, 32], "float32"), "cnt": ("sbuf", [128, 32], "float32"), "off": ("sbuf", [128, 32], "uint16"),
     "tv": ("sbuf", [128, 384], "bfloat16"), "hh": ("sbuf", [128, 144], "float32"),
     "offt": ("sbuf", [128, 48], "uint16"), "wgt": ("sbuf", [128, 48], "float32"),
-    "tab": ("sbuf", [128, 512], "bfloat16"), "gg": ("sbuf", [128, 1536], "bfloat16"), "hof": ("sbuf", [128, 64], "uint16"),
+    "tab": ("sbuf", [128, 512], "bfloat16"), "gg": ("sbuf", [128, 1536], "bfloat16"), "hof": ("sbuf", [128, 48], "uint16"),
     "ff": ("sbuf", [128, 144], "float32"), "cs": ("sbuf", [128, 32], "float32"), "cst": ("sbuf", [128, 32], "float32"),
     "ysb": ("sbuf", [128, 192], "float32"), "ll": ("sbuf", [128, 32], "uint16"), "lo": ("sbuf", [128, 32], "uint16"),
     "mt": ("sbuf", [128, 2048], "bfloat16"), "dxt": ("sbuf", [128, 2048], "bfloat16"), "ot": ("sbuf", [128, 2048], "bfloat16"),
@@ -38,9 +42,9 @@ SCRATCH = {
 _CODES = [("xq", 194), ("gq", 194), ("rq", 128), ("rp", 160), ("pq", 128), ("pp", 128), ("wq", 512), ("uq", 512),
           ("vq", 128), ("eq", 512), ("cq", 256), ("zq", 192), ("qm", 512), ("qd", 512), ("qo", 512), ("nq", 128)]
 for _k in range(4):
-    _CODES += [("lc%d" % _k, 224), ("ld%d" % _k, 64), ("zc%d" % _k, 192)]
+    _CODES += [("lc%d" % _k, 224), ("ld%d" % _k, 200), ("zc%d" % _k, 192)]
     if _k:
-        _CODES += [("sc%d" % _k, 224), ("sd%d" % _k, 48)]
+        _CODES += [("sc%d" % _k, 224), ("sd%d" % _k, 192)]
 for _n, _w in _CODES:
     SCRATCH[_n] = ("sbuf", [128, _w], "float8_e4m3fn_x4")
     SCRATCH[_n + "s"] = ("sbuf", [128, _w], "uint8")
@@ -107,6 +111,9 @@ def rank_program(g, core, T, topo):
     def tt(out, a, b, op, reads, writes, psum=False):
         run("V", lambda e: e.tensor_tensor(out, a, b, op), reads, writes, el(n_of(out) * (1 if psum else 2)))
 
+    def scan(out, a, b, op, reads, writes):
+        run("V", lambda e: e.tensor_tensor_scan(out, a, b, 0.0, op, A.add), reads, writes, el(n_of(out) // 2))
+
     def cp(out, a, reads, writes, cost=None):
         run("V", lambda e: e.tensor_copy(out, a), reads, writes, cost or el(n_of(out)))
 
@@ -145,20 +152,20 @@ def rank_program(g, core, T, topo):
     def bits(es):
         return sum(1 << e for e in es)
 
-    def send(parts, sem, reads, engines):
-        total["left"] = total.get("left", 0) + sum(len(engines[p[0]]) for p in parts)
+    def send(parts, sem, reads):
+        total["left"] = total.get("left", 0) + sum(len(p[3]) for p in parts)
 
         def call(e):
             if len(parts) == 1:
-                k, dst, src = parts[0]
+                k, dst, src, es = parts[0]
                 rid, pid, _s = topo.addr(peer[k])
                 g.remote_dma(out_ap=dst, in_ap=src, remote_sem=T.sem[sem % k], local_sem=T.sem["left"], pid=pid,
-                             routing_id=rid, dma_engine_mask=bits(engines[k]))
+                             routing_id=rid, dma_engine_mask=bits(es))
                 return
             tr = []
-            for k, dst, src in parts:
+            for k, dst, src, es in parts:
                 rid, pid, _s = topo.addr(peer[k])
-                tr.append(RemoteDMATransfer(dst_ids=[DstId(rid=rid, pnc=pid)], dma_engine_mask=bits(engines[k]),
+                tr.append(RemoteDMATransfer(dst_ids=[DstId(rid=rid, pnc=pid)], dma_engine_mask=bits(es),
                                             remote_sem=T.sem[sem % k if "%" in sem else sem], srcs=[src], dsts=[dst]))
             g.remote_dma_fused(tr, local_sem=T.sem["left"])
         return task("G", call, reads, [], 0.9)
@@ -181,21 +188,27 @@ def rank_program(g, core, T, topo):
     turn_of[0] = "first"
     fill(T.nt[:, :], 0.0, ["nt"])
     quant("nq", 0, 128, "nt", 0, 512, ["nt"], ["nq"])
-    a = send([(k, codes("ld%d" % k, 48, 50), codes("nq", 0, 2)) for k in (2, 3, 1)], "az", ["nq"], half)
-    b = send([(k, T["ld%ds" % k][:, 48:50], T.nqs[:, 0:2]) for k in (2, 3, 1)], "az", ["nq"], half)
+    a = send([(k, codes("ld%d" % k, 0, 2), codes("nq", 0, 2), half[k]) for k in (2, 3, 1)], "az", ["nq"])
+    b = send([(k, T["ld%ds" % k][:, 0:2], T.nqs[:, 0:2], half[k]) for k in (2, 3, 1)], "az", ["nq"])
     arrive("az", 2 * sum(len(half[k]) for k in half), ["ldz"], [a, b], 6.0)
     turn_of[0] = ""
-    dma("Y", "dz", codes("ld0", 48, 50), codes("nq", 0, 2), ["nq"], [], 2.0)
-    dma("Y", "dz", T.ld0s[:, 48:50], T.nqs[:, 0:2], ["nq"], ["ldz0"], 2.0)
+    dma("Y", "dz", codes("ld0", 0, 2), codes("nq", 0, 2), ["nq"], [], 2.0)
+    dma("Y", "dz", T.ld0s[:, 0:2], T.nqs[:, 0:2], ["nq"], ["ldz0"], 2.0)
+
+    turn_of[0] = "prep"
 
     def iota(out, pattern, base, ch, key, **kw):
         run("G", lambda e: e.iota(out, pattern, base, ch, **kw), [], [key], 0.15 + 2 * n_of(out) * CY)
+
+    def pf(i):
+        return T.pf[:, i:i + 1]
 
     fl_ok = {"allow_small_or_imprecise_dtypes": True}
     iota(T.pi[:, 0:1], [[0, 1]], 0, 1, "pi")
     iota(T.ii[:, 16:26], [[0, 5], [2, 2]], 0, 0, "i10", **fl_ok)
     iota(T.ii[:, 32:35], [[-1, 3]], 3, 0, "i3", **fl_ok)
-    iota(T.ii[:, 0:16], [[1, 16]], 0, 0, "i16", **fl_ok)
+    iota(T.ii[:, 0:16], [[7, 16]], 0, 0, "i16", **fl_ok)
+    iota(T.tri0[:, :], [[1, 7], [7, 16]], 0, 0, "tri0", **fl_ok)
     fill(T.rtt[:, 16:512], 0.0, ["rtz"])
     fill(T.one[:, :], 1.0, ["one"])
     fill(T.xt[:, 768:776], 0.0, ["xz"])
@@ -205,24 +218,36 @@ def rank_program(g, core, T, topo):
     ts(T.pi[:, 3:4], T.pi[:, 0:1], 3, 3, A.arith_shift_right, A.bitwise_and, ["pi"], ["pi3"])
     ts(T.pi[:, 4:5], T.pi[:, 0:1], 7, None, A.bitwise_and, None, ["pi"], ["pi4"])
     ts(T.pi[:, 5:6], T.pi[:, 0:1], 4, 1, A.arith_shift_right, A.bitwise_and, ["pi"], ["pi5"])
-    cp(T.pf[:, 0:6], T.pi[:, 0:6], ["pi", "pi1", "pi2", "pi3", "pi4", "pi5"], ["pf"])
-    ts(T.rl[:, 0:10], T.ii[:, 16:26], T.pf[:, 2:3], None, A.add, None, ["i10", "pf"], ["rl"])
-    ts(T.tie[:, 4:7], T.ii[:, 32:35], T.pf[:, 3:4], 0.5, A.is_gt, A.subtract, ["i3", "pf"], ["tie0"])
-    ts(T.tie[:, 0:2], T.tie[:, 4:6], 2 * TINY, None, A.mult, None, ["tie0"], ["tie"])
-    ts(T.tie[:, 2:3], T.tie[:, 6:7], -2 * TINY, None, A.mult, None, ["tie0"], ["tie3"])
-    ts(T.pf[:, 6:7], T.pf[:, 4:5], 16.0, 0.5, A.mult, A.add, ["pf"], ["pf6"])
-    ts(T.sb[:, :], T.ii[:, 0:16], T.pf[:, 6:7], None, A.add, None, ["i16", "pf6"], ["sb"])
-    ts(T.pf[:, 7:8], T.pf[:, 1:2], float(NS), None, A.is_lt, None, ["pf"], ["pf7"])
-    ts(T.pf[:, 8:9], T.pf[:, 7:8], -0.5, 1.0, A.mult, A.add, ["pf7"], ["pf8"])
-    ts(T.pf[:, 9:10], T.pf[:, 7:8], 96.0, None, A.mult, None, ["pf7"], ["pf9"])
+    ts(T.pi[:, 6:7], T.pi[:, 0:1], 4, None, A.arith_shift_right, None, ["pi"], ["pi6"])
+    cp(T.pf[:, 0:7], T.pi[:, 0:7], ["pi", "pi1", "pi2", "pi3", "pi4", "pi5", "pi6"], ["pf"])
+    ts(T.rl[:, 0:10], T.ii[:, 16:26], pf(2), None, A.add, None, ["i10", "pf"], ["rl"])
+    ts(T.tie[:, 4:7], T.ii[:, 32:35], pf(3), 0.5, A.is_gt, A.subtract, ["i3", "pf"], ["tie0"])
+    ts(T.tie[:, 0:3], T.tie[:, 4:7], 2 * TINY, None, A.mult, None, ["tie0"], ["tie"])
+    fill(T.seg[:, :], 1.0, ["seg1"])
+    fill(T.seg[:, 0:3 * NT:3], 0.0, ["seg1", "seg"])
+    ts(pf(16), pf(4), 0.5, None, A.add, None, ["pf"], ["pf16"])
+    ts(T.sb[:, :], T.ii[:, 0:16], pf(16), None, A.add, None, ["i16", "pf16"], ["sb"])
+    ts(pf(7), pf(1), float(NS), None, A.is_lt, None, ["pf"], ["pf7"])
+    ts(pf(8), pf(7), -0.5, 1.0, A.mult, A.add, ["pf7"], ["pf8"])
+    ts(pf(19), pf(8), 7.0, None, A.mult, None, ["pf8"], ["pf19"])
+    ts(pf(20), pf(7), 0.5 * NT, None, A.mult, None, ["pf7"], ["pf20"])
+    ts(pf(9), pf(1), pf(19), pf(20), A.mult, A.add, ["pf", "pf19", "pf20"], ["pf9"])
+    ts(pf(13), pf(1), 7.0, pf(6), A.mult, A.add, ["pf"], ["pf13"])
+    cp(T.pi[:, 7:8], pf(13), ["pf13"], ["pi7"])
+    ts(T.pi[:, 8:9], T.pi[:, 7:8], 15, None, A.bitwise_and, None, ["pi7"], ["pi8"])
+    cp(pf(14), T.pi[:, 8:9], ["pi8"], ["pf14"])
+    tt(pf(15), pf(13), pf(14), A.subtract, ["pf13", "pf14"], ["pf15"])
+    ts(pf(17), pf(0), float(CP), 128.0, A.is_ge, A.mult, ["pf"], ["pf17"])
+    ts(pf(18), pf(17), pf(13), None, A.add, None, ["pf17", "pf13"], ["pf18"])
+    ts(T.tri[:, :], T.tri0[:, :], pf(18), BELOW - 1.0, A.is_lt, A.mult, ["tri0", "pf18"], ["tri1"])
+    ts(T.tri[:, :], T.tri[:, :], 1.0, None, A.add, None, ["tri1"], ["tri"])
     for b in range(4):
         clear(T.et[:, 512 * b:512 * b + 512], "ez%d" % b)
-    fill(T.tri0[:, :], BELOW, ["tri0"])
     run("G", lambda e: e.affine_select(T.idn[:, :], T.one[:, :], [[-1, 128]], A.is_equal, 0.0, 0, 1), ["one"], ["idn"], 0.4)
-    run("G", lambda e: e.affine_select(T.tri[:, :], T.tri0[:, :], [[-1, 112]], A.is_gt, 1.0, 0, 1), ["tri0"], ["tri"], 0.4)
     iota(T.k4[:, :], [[0, 8], [1, 16], [16, 4]], 0, 0, "k4", **fl_ok)
-    iota(T.vals[:, :], [[1, 48]], 0, 0, "vals", **fl_ok)
+    iota(T.vals[:, :], [[1, CR]], 2, 0, "vals", **fl_ok)
 
+    turn_of[0] = "route"
     quant("rq", 0, 128, "rtt", 0, 512, ["rtt", "rtz"], ["rq"])
     pick("rp", 0, 160, "rq", 0, 128, T.rl[:, 0:10], ["rq", "rl"], "rp")
     quant("xq", 0, 194, "xt", 0, 776, ["xt", "xz"], ["xq"])
@@ -232,60 +257,57 @@ def rank_program(g, core, T, topo):
     for r in (1, 2, 3):
         a = NT * (r - 1)
         tt(T.dd[:, a:a + NT], T.s0[:, :], T.pz[:, 512 * r:512 * r + NT], A.subtract, ["s0", "*z%d" % r], ["dd%d" % r], True)
-        act(T.sg[:, a:a + NT], T.dd[:, a:a + NT], F.Sign, ["dd%d" % r, "tie", "tie3"], ["sg%d" % r], bias=T.tie[:, r - 1:r],
-            scale=(1.0, 1.0, -1.0)[r - 1])
-    tt(T.u[:, :], T.sg[:, 0:NT], T.sg[:, NT:2 * NT], A.add, ["sg1", "sg2"], ["u"])
-    tt(T.m[:, :], T.u[:, :], T.sg[:, 2 * NT:3 * NT], A.is_gt, ["u", "sg3"], ["m"])
-    run("V", lambda e: e.tensor_tensor_scan(T.pref[:, :], T.m[:, :], T.nt[:, 0:NT], 0.0, A.add, A.add), ["m", "nt"], ["pref"], 0.1)
+        act(T.sg[:, r - 1:3 * NT:3], T.dd[:, a:a + NT], F.Sign, ["dd%d" % r, "tie"], ["sg%d" % r], bias=T.tie[:, r - 1:r])
+    scan(T.ss[:, :], T.seg[:, :], T.sg[:, :], A.mult, ["seg", "sg1", "sg2", "sg3"], ["ss"])
+    ts(T.m[:, :], T.ss[:, 2:3 * NT:3], 0.0, None, A.is_gt, None, ["ss"], ["m"], True)
+    scan(T.pref[:, :], T.m[:, :], T.nt[:, 0:NT], A.add, ["m", "nt"], ["pref"])
+
+    def piece(i, t):
+        return T.le[:, NT * i + 7 * t:NT * i + NT]
+
     for t in range(NS):
-        act(T.le[:, NT * t:NT * t + NT], T.pref[:, :], F.Sign, ["pref", "sb"], ["cn%d" % t], bias=T.sb[:, t:t + 1], scale=-1.0,
+        act(piece(t, t), T.pref[:, 7 * t:NT], F.Sign, ["pref", "sb"], ["cn%d" % t], bias=T.sb[:, t:t + 1], scale=-1.0,
             accum_out=T.cn[:, t:t + 1])
     for t in range(NS, 16):
-        a = NT * t
-        ts(T.le[:, a:a + NT], T.pref[:, :], T.sb[:, t:t + 1], None, A.is_le, None, ["pref", "sb"], ["le%d" % t], True)
-
-    def count(t):
-        a, o = T.le[:, NT * t:NT * t + NT], T.cn[:, t:t + 1]
-        run("V", lambda e: e.tensor_reduce(o, a, AxisListType.X, A.add), ["le%d" % t], ["cn%d" % t], 0.19)
-
+        ts(piece(t, t), T.pref[:, 7 * t:NT], T.sb[:, t:t + 1], None, A.is_le, None, ["pref", "sb"], ["le%d" % t], True)
     for t in range(NS, 16):
-        count(t)
+        scan(piece(t + 16 - NS, t), piece(t, t), T.nt[:, 0:NT - 7 * t], A.add, ["le%d" % t, "nt"], ["ls%d" % t])
+    mine, last = ["cn%d" % t for t in range(NS)], T.le[:, NT * 17 - 1:NT * (32 - NS):NT]
+    act(T.cn[:, 16:16 + NS], T.cn[:, 0:NS], F.Copy, mine, ["cnd"])
+    for c in (0, 16):
+        cp(T.cn[:, c + NS:c + 16], last, ["ls%d" % t for t in range(NS, 16)], ["cnl%d" % c])
+    turn(T.cnt[:, :], T.cn[:, :], mine + ["cnd", "cnl0", "cnl16"], ["cnt"])
+    ts(T.off[:, :], T.cnt[:, :], pf(8), pf(9), A.mult, A.add, ["cnt", "pf8", "pf9"], ["off"])
+    turn_of[0] = "prep"
     quant("gq", 0, 194, "gt", 0, 776, ["gt", "gz"], ["gq"])
-    cns = ["cn%d" % t for t in range(16)]
-    cp(T.cn[:, 16:32], T.cn[:, 0:16], cns, ["cnd"])
-    turn(T.cnt[:, :], T.cn[:, :], cns + ["cnd"], ["cnt"])
-    ts(T.off[:, :], T.cnt[:, :], T.pf[:, 8:9], T.pf[:, 9:10], A.mult, A.add, ["cnt", "pf8", "pf9"], ["off"])
 
     def take(k):
         o = T.off[:, 8 * (rank ^ k):8 * (rank ^ k) + 7]
         d = ("sc%d" if k else "lc%d") % k
 
         def part(c, src, key):
-            oc, ic = T[d][:, c:c + CP].bitcast(dt.uint32), T[src][:, 0:194].bitcast(dt.uint32).indirect(o)
-            cp(oc, ic, [src, "off"], [d + key], 0.05 + 1.5 * CP * CY)
-            act(T[d + "s"][:, c:c + CP], T[src + "s"][:, 0:194].indirect(o), F.Copy, [src, "off"], [d + key + "s"], 0.065 + 1.5 * CP * CY)
+            cost, r = 1.5 * CP * CY, [src, "off"]
+            cp(T[d][:, c:c + CP].bitcast(dt.uint32), T[src][:, 0:194].bitcast(dt.uint32).indirect(o), r, [d + key], 0.05 + cost)
+            act(T[d + "s"][:, c:c + CP], T[src + "s"][:, 0:194].indirect(o), F.Copy, r, [d + key + "s"], 0.065 + cost)
         part(CP, "xq", "x")
         part(0, "gq", "g")
 
-    def go(ks):
-        a = send([(k, codes("lc%d" % k, 0, 2 * CP), codes("sc%d" % k, 0, 2 * CP)) for k in ks], "ax%d",
-                 [n % k for k in ks for n in ("sc%dx", "sc%dg")], eng)
-        b = send([(k, T["lc%ds" % k][:, 0:2 * CP], T["sc%ds" % k][:, 0:2 * CP]) for k in ks], "ax%d",
-                 [n % k for k in ks for n in ("sc%dxs", "sc%dgs")], eng)
-        for k in ks:
-            arrive("ax%d" % k, 2 * len(eng[k]), ["lc%d" % k], [a, b], OUT[k])
-
     turn_of[0] = "out"
-    take(2)
-    take(1)
-    go((2, 1))
-    take(3)
-    go((3,))
-    turn_of[0] = ""
+    out = {}
+    for k in (1, 2, 3):
+        take(k)
+        out[k] = send([(k, codes("lc%d" % k, 0, 2 * CP), codes("sc%d" % k, 0, 2 * CP), eng[k])], "ax%d",
+                      ["sc%dx" % k, "sc%dg" % k])
+    b = send([(k, T["lc%ds" % k][:, 0:2 * CP], T["sc%ds" % k][:, 0:2 * CP], half[k]) for k in (2, 3, 1)], "ax%d",
+             [n % k for k in (2, 3, 1) for n in ("sc%dxs", "sc%dgs")])
+    for k in (1, 2, 3):
+        arrive("ax%d" % k, len(eng[k]) + len(half[k]), ["lc%d" % k], [out[k], b], OUT[k])
+    turn_of[0] = "k0"
     take(0)
     came = {k: ["lc%d" % k] for k in (1, 2, 3)}
     came[0] = ["lc0x", "lc0g", "lc0xs", "lc0gs"]
 
+    turn_of[0] = "prep"
     for b in range(4):
         act(T.et[:, 512 * b + b:512 * b + 512:4], T.idn[:, :], F.Copy, ["idn", "ez%d" % b], ["et%d" % b])
     quant("eq", 0, 512, "et", 0, 2048, ["et0", "et1", "et2", "et3"], ["eq"])
@@ -299,13 +321,18 @@ def rank_program(g, core, T, topo):
     clear(T.pt[:, 0:512], "pt0")
     clear(T.pt[:, 512:1024], "pt1")
     fill(T.z3[:, :], 0.0, ["z3"])
-    tt(T.pf[:, 11:12], T.pf[:, 0:1], T.pf[:, 1:2], A.subtract, ["pf"], ["pf11"])
-    ts(T.pt[:, 0:11:5], T.z3[:, 0:3], T.pf[:, 11:12], None, A.add, None, ["z3", "pf11", "pt0"], ["pth"])
-    ts(T.pt[:, 512:523:5], T.z3[:, 0:3], T.pf[:, 1:2], None, A.add, None, ["z3", "pf", "pt1"], ["ptl"])
-    quant("cq", 0, 256, "pt", 0, 1024, ["pt0", "pt1", "pth", "ptl"], ["cq"])
+    tt(pf(11), pf(0), pf(1), A.subtract, ["pf"], ["pf11"])
+    ts(T.pt[:, 0:11:5], T.z3[:, 0:3], pf(11), None, A.add, None, ["z3", "pf11", "pt0"], ["pth"])
+    ts(T.pt[:, 512:523:5], T.z3[:, 0:3], pf(1), None, A.add, None, ["z3", "pf", "pt1"], ["ptl"])
+    ts(T.pt[:, 16:27:5], T.z3[:, 0:3], pf(15), None, A.add, None, ["z3", "pf15", "pt0"], ["psh"])
+    ts(T.pt[:, 528:539:5], T.z3[:, 0:3], pf(14), None, A.add, None, ["z3", "pf14", "pt1"], ["psl"])
+    quant("cq", 0, 256, "pt", 0, 1024, ["pt0", "pt1", "pth", "ptl", "psh", "psl"], ["cq"])
     for k in range(4):
         clear(T.mt[:, 512 * k + 448:512 * k + 512], "mz%d" % k)
         clear(T.dxt[:, 512 * k + 448:512 * k + 512], "dz%d" % k)
+        if k:
+            quant("sd%d" % k, 0, 192, "nt", 0, 768, ["nt"], ["sd%d" % k, "sd%ds" % k])
+    fill(pf(12), EPS, ["eps"])
 
     def bank(k, x):
         return (T.px if k % 2 else T.pz), 512 * x, "*%s%d" % ("zx"[k % 2], x)
@@ -329,18 +356,18 @@ def rank_program(g, core, T, topo):
               ["mz%d" % k] + ["mt%d_%d" % (k, b) for b in range(4)], ["qm%d" % k])
 
     def stage2(k):
-        m = "qm%d" % k
+        m, rk, one_hot = "qm%d" % k, T.rk[:, 4 * k:4 * k + 1], T.ot[:, 512 * k:512 * k + 512]
         pc, xc, kc = bank(k, 1)
         pr, xr, kr = bank(k, 0)
         mm(pc[:, xc:xc + 128], "qm", 128 * k, "pp", 0, 128, True, True, [m, "pp", "pps"], [kc])
         mm(pr[:, xr:xr + 128], "pp", 0, "qm", 128 * k, 128, True, True, [m, "pp", "pps"], [kr])
-        act(T.ca[:, 4 * k:4 * k + 1], pc[:, xc:xc + 1], F.Abs, [kc, "eps"], ["ca%d" % k], bias=T.pf[:, 12:13])
+        act(T.ca[:, 4 * k:4 * k + 1], pc[:, xc:xc + 1], F.Abs, [kc, "eps"], ["ca%d" % k], bias=pf(12))
         s, sd, sx = (slice(c + CP * k, c + CP * k + CP) for c in (0, 448, 896))
-        act(T.ra[:, s], pr[:, xr:xr + CP], F.Abs, [kr, "eps"], ["ra%d" % k], bias=T.pf[:, 12:13])
+        act(T.ra[:, s], pr[:, xr:xr + CP], F.Abs, [kr, "eps"], ["ra%d" % k], bias=pf(12))
         act(T.ra[:, sd], T.tri[:, :], F.Copy, ["tri", "ca%d" % k], ["rd%d" % k], scale=T.ca[:, 4 * k:4 * k + 1])
         tt(T.ra[:, sx], T.ra[:, s], T.ra[:, sd], A.is_gt, ["rd%d" % k, "ra%d" % k], ["rx%d" % k])
-        run("V", lambda e: e.tensor_reduce(T.rk[:, 4 * k:4 * k + 1], T.ra[:, sx], AxisListType.X, A.add), ["rx%d" % k], ["rk%d" % k], 0.11)
-        ts(T.ot[:, 512 * k:512 * k + 512], T.k4[:, :], T.rk[:, 4 * k:4 * k + 1], None, A.is_equal, None, ["k4", "rk%d" % k], ["ot%d" % k], True)
+        run("V", lambda e: e.tensor_reduce(rk, T.ra[:, sx], AxisListType.X, A.add), ["rx%d" % k], ["rk%d" % k], 0.11)
+        ts(one_hot, T.k4[:, :], rk, None, A.is_equal, None, ["k4", "rk%d" % k], ["ot%d" % k], True)
         quant("qo", 128 * k, 128 * k + 128, "ot", 512 * k, 512 * k + 512, ["ot%d" % k], ["qo%d" % k])
         for b, y in ((0, 2), (1, 3), (2, 1), (3, 0)):
             ps, x, key = bank(k, y)
@@ -353,26 +380,29 @@ def rank_program(g, core, T, topo):
             mm(ps[:, x:x + 128], "qo", 128 * k, "cq", 128 * c, 128, c == 0, c == 1, ["qo%d" % k, "cq"], [key])
         quant("qd", 128 * k, 128 * k + 128, "dxt", 512 * k, 512 * k + 512,
               ["dz%d" % k] + ["dt%d_%d" % (k, b) for b in range(4)], ["qd%d" % k])
-        cp(T.lo[:, 8 * k:8 * k + 3], ps[:, x:x + 3], [key], ["lo%d" % k])
-        d = ("sd%d" if k else "ld%d") % k
+        cp(T.lo[:, 8 * k:8 * k + 7], ps[:, x:x + 7], [key], ["lo%d" % k])
+        if not k:
+            pick("ld0", 2, CR, "qd", 0, 128, T.lo[:, 0:3], ["qd0", "lo0", "ldz0"], "ld0")
+            return
+        d = "sd%d" % k
         pick(d, 0, CR, "qd", 128 * k, 128 * k + 128, T.lo[:, 8 * k:8 * k + 3], ["qd%d" % k, "lo%d" % k], d)
-        if k:
-            a = send([(k, T.ll[:, 8 * k:8 * k + 3], T.lo[:, 8 * k:8 * k + 3])], "al%d", ["lo%d" % k], eng)
-            b = send([(k, codes("ld%d" % k, 0, CR), codes(d, 0, CR))], "ar%d", [d], eng)
-            c = send([(k, T["ld%ds" % k][:, 0:CR], T[d + "s"][:, 0:CR])], "ar%d", [d + "s"], eng)
-            arrive("al%d" % k, len(eng[k]), ["ll%d" % k], [a], BACK)
-            arrive("ar%d" % k, 2 * len(eng[k]), ["ld%d" % k, "ld%ds" % k], [b, c], BACK)
+        a = send([(k, T.ll[:, 8 * k:8 * k + 3], T.lo[:, 8 * k + 4:8 * k + 7], eng[k])], "al%d", ["lo%d" % k])
+        b = send([(k, codes("ld%d" % k, 2, 2 + CR), codes(d, 0, CR), eng[k][0:4]),
+                  (k, T["ld%ds" % k][:, 2:2 + 4 * CR], T[d + "s"][:, 0:4 * CR], eng[k][4:8])], "ar%d", [d, d + "s"])
+        arrive("al%d" % k, len(eng[k]), ["ll%d" % k], [a], BACK)
+        arrive("ar%d" % k, len(eng[k]), ["ld%d" % k, "ld%ds" % k], [b], BACK)
 
-    fill(T.pf[:, 12:13], EPS, ["eps"])
     for k in range(4):
         turn_of[0] = "k%d" % k
         stage1(k)
+        turn_of[0] = "k%db" % k
         stage2(k)
+        turn_of[0] = "k%dc" % k
         stage3(k)
-    turn_of[0] = ""
 
+    turn_of[0] = "look"
     h1, h2, h3, h4, h5, h6 = (T.hh[:, 24 * i:24 * i + 24] for i in range(6))
-    tt(T.win[:, :], T.u[:, :], T.sg[:, 2 * NT:3 * NT], A.subtract, ["u", "sg3"], ["win"])
+    cp(T.win[:, :], T.ss[:, 2:3 * NT:3], ["ss"], ["win"], el(NT // 2))
     turn(T.tv[:, 0:NT], T.win[:, :], ["win"], ["tw"])
     turn(T.tv[:, NT:2 * NT], T.pref[:, :], ["pref"], ["tp"])
     tw, tp = T.tv[:, 0:NT:8], T.tv[:, NT:2 * NT:8]
@@ -382,39 +412,42 @@ def rank_program(g, core, T, topo):
     ts(h6, tw, -0.5, 2.5, A.mult, A.add, ["tw"], ["h6"])
     tt(h4, h1, h2, A.mult, ["h1", "h2"], ["h4"])
     tt(h5, h4, h3, A.mult, ["h4", "h3"], ["h5"])
-    ts(T.pf[:, 10:11], T.pf[:, 5:6], -1.0, 1.0, A.mult, A.add, ["pf"], ["pf10"])
+    ts(pf(10), pf(5), -1.0, 1.0, A.mult, A.add, ["pf"], ["pf10"])
     for k in range(4):
         e = rank ^ k
         for h in (0, 1):
             o, p = slice(12 * k + h, 12 * k + 12, 2), (10, 5)[h]
             ts(T.offt[:, o], T.hh[:, 96 + e:120:4], float(CP), None, A.add, None, ["h5"], ["offt%d%d" % (k, h)])
-            act(T.wgt[:, o], T.hh[:, 120 + e:144:4], F.Copy, ["h6", "pf", "pf10"], ["wgt%d%d" % (k, h)], scale=T.pf[:, p:p + 1])
+            act(T.wgt[:, o], T.hh[:, 120 + e:144:4], F.Copy, ["h6", "pf", "pf10"], ["wgt%d%d" % (k, h)], scale=pf(p))
     for k in range(4):
-        fill(T.tab[:, 128 * k:128 * k + 128], float(CR), ["tab%d" % k])
+        fill(T.tab[:, 128 * k:128 * k + 128], 0.0, ["tab%d" % k])
     fill(T.cs[:, :], 0.0, ["csz"])
 
     def home(k, first, last):
-        tab = T.tab[:, 128 * k:128 * k + 128]
-        lst, key = (T.ll[:, 8 * k:8 * k + 3], "ll%d" % k) if k else (T.lo[:, 0:3], "lo0")
+        tab, zc, offt = T.tab[:, 128 * k:128 * k + 128], "zc%d" % k, T.offt[:, 12 * k:12 * k + 12]
+        lst, key = (T.ll[:, 8 * k:8 * k + 3], "ll%d" % k) if k else (T.lo[:, 4:7], "lo0")
         s, s1 = slice(192 * k, 192 * k + 192), slice(768 + 192 * k, 960 + 192 * k)
         cp(tab.indirect(lst), T.vals[:, :], ["vals", key], ["tab%d" % k], 0.23)
-        cp(T.gg[:, s], tab.indirect(T.offt[:, 12 * k:12 * k + 12]), ["tab%d" % k, "offt%d0" % k, "offt%d1" % k], ["gr0%d" % k], 0.34)
+        act(T.gg[:, s], tab.indirect(offt), F.Copy, ["tab%d" % k, "offt%d0" % k, "offt%d1" % k], ["gr0%d" % k], 0.35)
         turn(T.gg[:, s1], T.gg[:, s], ["gr0%d" % k], ["gr1%d" % k])
-        of = T.hof[:, 16 * k:16 * k + 12]
+        of = T.hof[:, 12 * k:12 * k + 12]
         cp(of, T.gg[:, 768 + 192 * k:960 + 192 * k:16], ["gr1%d" % k], ["hof%d" % k])
-        pick("zc%d" % k, 0, NT, "ld%d" % k, 0, 50, of, ["hof%d" % k, "ld%d" % k, "ld%ds" % k, "ldz" if k else "ldz0"], "zc%d" % k)
+        pick(zc, 0, NT, "ld%d" % k, 0, 50, of, ["hof%d" % k, "ld%d" % k, "ld%ds" % k, "ldz" if k else "ldz0"], zc)
         for b in range(4):
-            mm(T.pz[:, 512 * b:512 * b + NT], "eq", 128 * b, "zc%d" % k, 0, NT, first, last, ["eq", "zc%d" % k, "zc%ds" % k], ["*z%d" % b])
-        w, wf, wt = (slice(c + 12 * k, c + 12 * k + 12) for c in (0, 48, 96))
-        ts(T.ff[:, w], of, float(CR), None, A.is_lt, None, ["hof%d" % k], ["fl%d" % k])
-        tt(T.ff[:, wf], T.ff[:, w], T.wgt[:, w], A.mult, ["fl%d" % k, "wgt%d0" % k, "wgt%d1" % k], ["fw%d" % k])
-        if not first:
-            v = (36 if k == 1 else 84) + 12 * k
-            tt(T.ff[:, wt], T.ff[:, v:v + 12], T.ff[:, wf], A.add, ["fw%d" % k, "fw0" if k == 1 else "fs%d" % (k - 1)], ["fs%d" % k])
+            mm(T.pz[:, 512 * b:512 * b + NT], "eq", 128 * b, zc, 0, NT, first, last, ["eq", zc, zc + "s"], ["*z%d" % b])
 
     for k in range(4):
+        turn_of[0] = "h%d" % k
         home(k, k == 0, k == 3)
+    turn_of[0] = "ct"
+    ts(T.ff[:, 0:48], T.hof[:, 0:48], 1.0, None, A.is_gt, None, ["hof%d" % k for k in range(4)], ["fl"])
+    tt(T.ff[:, 48:96], T.ff[:, 0:48], T.wgt[:, :], A.mult, ["fl"] + ["wgt%d%d" % (k, h) for k in range(4) for h in (0, 1)], ["fw"])
+    tt(T.ff[:, 96:120], T.ff[:, 48:72], T.ff[:, 72:96], A.add, ["fw"], ["fs"])
+    tt(T.ff[:, 120:132], T.ff[:, 96:108], T.ff[:, 108:120], A.add, ["fs"], ["ft"])
+    tt(T.cs[:, 0:6], T.ff[:, 120:132:2], T.ff[:, 121:132:2], A.add, ["ft", "csz"], ["cs"])
+    turn(T.cst[0:32, :], T.cs[0:32, :], ["cs", "csz"], ["cst"])
 
+    turn_of[0] = ""
     for b in (0, 1):
         act(T.zt[:, b:768:4], T.pz[:, 512 * b:512 * b + NT], F.Copy, ["*z%d" % b], ["zt%d" % b])
     for b in (2, 3):
@@ -422,8 +455,6 @@ def rank_program(g, core, T, topo):
     quant("zq", 0, 192, "zt", 0, 768, ["zt0", "zt1", "zt2", "zt3"], ["zq"])
     mm(T.px[:, 0:NT], "vq", 0, "zq", 0, NT, True, True, ["vq", "zq"], ["*x0"])
     cp(T.ysb[:, :], T.px[:, 0:NT], ["*x0"], ["ysb"])
-    tt(T.cs[:, 0:6], T.ff[:, 132:144:2], T.ff[:, 133:144:2], A.add, ["fs3", "csz"], ["cs"])
-    turn(T.cst[0:32, :], T.cs[0:32, :], ["cs", "csz"], ["cst"])
     dma("S", "dos", T.ct[0:1, 0:NT], T.cst[0:6, 0:32], ["cst"], [], 2.0)
     dma("Y", "doy", T.oc[:, 0:768], T.zq[:, 0:NT].bitcast(dt.uint8), ["zq"], [], 2.0)
     for i in range(4):
@@ -439,7 +470,7 @@ def rank_program(g, core, T, topo):
     rest = [0.0] * n
     for i in range(n - 1, -1, -1):
         far = max([rest[j] + (HOP if tasks[j]["before"][i] else 0.0) for j in follow[i]] or [0.0])
-        rest[i] = far + tasks[i]["cost"] + tasks[i]["late"] + tasks[i]["ahead"]
+        rest[i] = max(far, 0.0) + tasks[i]["cost"] + tasks[i]["late"] + tasks[i]["ahead"]
     left = [len(t["before"]) for t in tasks]
     ready = [0.0] * n
     free = {q: 0.0 for q in ("V", "S", "P", "G", "Y", None)}
@@ -448,14 +479,14 @@ def rank_program(g, core, T, topo):
     while able:
         best = None
         for q in free:
-            mine = [i for i in able if tasks[i]["q"] == q]
+            mine = sorted(i for i in able if tasks[i]["q"] == q)
             if not mine:
                 continue
             at = max(free[q], min(ready[i] for i in mine)) if q else min(ready[i] for i in mine)
             pool = [i for i in mine if ready[i] <= at + 1e-9]
             i = min(pool) if q == "Y" else max(pool, key=lambda j: rest[j])
             for j in mine:
-                if q not in ("Y", None) and ready[j] < at + 0.5 * tasks[i]["cost"] and rest[j] > rest[i] + 1.0:
+                if q not in ("Y", None) and ready[j] < at + HOLD * tasks[i]["cost"] and rest[j] > rest[i] + GAP:
                     i = j
             at = max(at, ready[i])
             if best is None or at < best[0]:

@@ -6,30 +6,33 @@ NS = 7
 TINY = 2.0 ** -100
 EPS = 2.0 ** -120
 BELOW = 1.0 - 2.0 ** -24
-HOP, CY, PE, OUT, BACK = 0.11, 0.001, 0.0012, {1: 3.6, 2: 4.5, 3: 4.5}, 3.5
-AHEAD = {"first": 99.0, "route": 5.3, "prep": -9.2, "out": -1.6, "look": -1.4, "ct": -0.3, "": -4.1,
-         "k0": -1.0, "k0b": 0.3, "k0c": 1.8, "k1": 1.5, "k1b": 0.8, "k1c": 0.3, "k2": 1.6, "k2b": 0.4, "k2c": -0.5,
-         "k3": 0.2, "k3b": 0.0, "k3c": -0.2, "h0": -19.3, "h1": -9.4, "h2": 0.1, "h3": -12.4}
-HOLD, GAP = 0.3, 1.0
+WHOLE = 1.5 * 2.0 ** 23
+HOP, CY, PE, OUT, BACK = 0.11, 0.001, 0.0012, {1: 2.2, 2: 2.7, 3: 4.5}, 3.6
+AHEAD = {"first": 0.2, "early": 21.0, "route": 0.8, "prep": -8.9, "out": 0.1, "look": -4.3, "ct": -2.1, "": -11.3,
+         "k0": -4.2, "k0b": 4.3, "k0c": 0.1, "k1": 2.7, "k1b": -3.1, "k1c": 0.0, "k2": -3.0, "k2b": 0.3, "k2c": 0.5,
+         "k3": -0.4, "k3b": 1.4, "k3c": 3.1, "h0": -13.7, "h1": -2.0, "h2": -1.8, "h3": -2.5}
+HOLD, GAP = 0.5, 1.0
+TAB = {0: 0, 2: 1, 3: 2, 1: 3}
+POS = {0: 0, 3: 1, 1: 2, 2: 3}
 
 SCRATCH = {
     "xt": ("sbuf", [128, 776], "bfloat16"), "gt": ("sbuf", [128, 776], "bfloat16"),
-    "rtt": ("sbuf", [128, 512], "bfloat16"), "prt": ("sbuf", [128, 512], "bfloat16"), "nt": ("sbuf", [128, 768], "bfloat16"),
-    "wt": ("sbuf", [128, 2048], "bfloat16"), "ut": ("sbuf", [128, 2048], "bfloat16"),
-    "vt": ("sbuf", [128, 512], "bfloat16"), "et": ("sbuf", [128, 2048], "bfloat16"),
+    "rtt": ("sbuf", [128, 512], "bfloat16"), "prt": ("sbuf", [128, 16], "bfloat16"), "nt": ("sbuf", [128, 512], "bfloat16"),
+    "wt": ("sbuf", [128, 2048], "bfloat16"), "ut": ("sbuf", [128, 2048], "bfloat16"), "ppt": ("sbuf", [128, 512], "bfloat16"),
+    "vt": ("sbuf", [128, 512], "bfloat16"), "et": ("sbuf", [128, 2048], "bfloat16"), "wnt": ("sbuf", [128, 512], "bfloat16"),
     "pt": ("sbuf", [128, 1024], "bfloat16"), "zt": ("sbuf", [128, 768], "bfloat16"),
-    "pi": ("sbuf", [128, 16], "int32"), "pf": ("sbuf", [128, 24], "float32"), "ii": ("sbuf", [128, 48], "float32"),
-    "rl": ("sbuf", [128, 16], "uint16"), "zl": ("sbuf", [128, 8], "uint16"),
-    "tie": ("sbuf", [128, 8], "float32"), "sb": ("sbuf", [128, 16], "float32"),
+    "fi": ("sbuf", [128, 224], "float32"), "own": ("sbuf", [128, 224], "float32"),
+    "pf": ("sbuf", [128, 24], "float32"), "ii": ("sbuf", [128, 48], "float32"),
+    "rl": ("sbuf", [128, 16], "uint16"), "tie": ("sbuf", [128, 8], "float32"), "sb": ("sbuf", [128, 16], "float32"),
     "tri0": ("sbuf", [128, 112], "float32"), "tri": ("sbuf", [128, 112], "float32"),
-    "one": ("sbuf", [128, 128], "bfloat16"), "idn": ("sbuf", [128, 128], "bfloat16"),
-    "vals": ("sbuf", [128, 48], "bfloat16"), "k4": ("sbuf", [128, 512], "bfloat16"), "z3": ("sbuf", [128, 8], "float32"),
+    "idn": ("sbuf", [128, 128], "bfloat16"), "idr": ("sbuf", [128, 128], "bfloat16"), "gid": ("sbuf", [128, 192], "bfloat16"),
+    "vals": ("sbuf", [128, 50], "bfloat16"), "k4": ("sbuf", [128, 512], "bfloat16"),
     "s0": ("sbuf", [128, 192], "float32"), "dd": ("sbuf", [128, 576], "float32"), "sg": ("sbuf", [128, 576], "bfloat16"),
     "seg": ("sbuf", [128, 576], "bfloat16"), "ss": ("sbuf", [128, 576], "bfloat16"),
     "win": ("sbuf", [128, 192], "bfloat16"), "m": ("sbuf", [128, 192], "bfloat16"), "pref": ("sbuf", [128, 192], "bfloat16"),
     "le": ("sbuf", [128, 192 * (32 - NS)], "bfloat16"),
     "cn": ("sbuf", [128, 32], "float32"), "cnt": ("sbuf", [128, 32], "float32"), "off": ("sbuf", [128, 32], "uint16"),
-    "tv": ("sbuf", [128, 384], "bfloat16"), "hh": ("sbuf", [128, 144], "float32"),
+    "tv": ("sbuf", [128, 384], "bfloat16"), "hh": ("sbuf", [128, 240], "float32"),
     "offt": ("sbuf", [128, 48], "uint16"), "wgt": ("sbuf", [128, 48], "float32"),
     "tab": ("sbuf", [128, 512], "bfloat16"), "gg": ("sbuf", [128, 1536], "bfloat16"), "hof": ("sbuf", [128, 48], "uint16"),
     "ff": ("sbuf", [128, 144], "float32"), "cs": ("sbuf", [128, 32], "float32"), "cst": ("sbuf", [128, 32], "float32"),
@@ -39,17 +42,17 @@ SCRATCH = {
     "ca": ("sbuf", [128, 16], "float32"), "rk": ("sbuf", [128, 16], "float32"),
     "pz": ("psum", [128, 2048], "float32"), "px": ("psum", [128, 2048], "float32"),
 }
-_CODES = [("xq", 194), ("gq", 194), ("rq", 128), ("rp", 160), ("pq", 128), ("pp", 128), ("wq", 512), ("uq", 512),
-          ("vq", 128), ("eq", 512), ("cq", 256), ("zq", 192), ("qm", 512), ("qd", 512), ("qo", 512), ("nq", 128)]
+_CODES = [("xq", 194), ("gq", 194), ("rq", 128), ("rp", 160), ("pp", 128), ("wq", 512), ("uq", 512), ("wn", 128),
+          ("vq", 128), ("eq", 512), ("cq", 256), ("zq", 192), ("qm", 512), ("qd", 512), ("qo", 512), ("nq", 224)]
 for _k in range(4):
-    _CODES += [("lc%d" % _k, 224), ("ld%d" % _k, 200), ("zc%d" % _k, 192)]
+    _CODES += [("lc%d" % _k, 224), ("zc%d" % _k, 192)]
     if _k:
-        _CODES += [("sc%d" % _k, 224), ("sd%d" % _k, 192)]
+        _CODES += [("sc%d" % _k, 224), ("ld%d" % _k, 128)]
 for _n, _w in _CODES:
     SCRATCH[_n] = ("sbuf", [128, _w], "float8_e4m3fn_x4")
     SCRATCH[_n + "s"] = ("sbuf", [128, _w], "uint8")
 
-SEMAPHORES = ["cV", "cS", "cP", "cG", "dx", "dgr", "drt", "dpr", "dw", "dub", "dv", "dz", "doy", "dos", "left", "az"]
+SEMAPHORES = ["cV", "cS", "cP", "cG", "dx", "dgr", "drt", "dpr", "dw", "dub", "dv", "doy", "dos", "left", "az"]
 for _k in (1, 2, 3):
     SEMAPHORES += ["ax%d" % _k, "al%d" % _k, "ar%d" % _k]
 
@@ -111,14 +114,14 @@ def rank_program(g, core, T, topo):
     def tt(out, a, b, op, reads, writes, psum=False):
         run("V", lambda e: e.tensor_tensor(out, a, b, op), reads, writes, el(n_of(out) * (1 if psum else 2)))
 
-    def scan(out, a, b, op, reads, writes):
-        run("V", lambda e: e.tensor_tensor_scan(out, a, b, 0.0, op, A.add), reads, writes, el(n_of(out) // 2))
+    def scan(out, a, b, op, reads, writes, start=0.0):
+        run("V", lambda e: e.tensor_tensor_scan(out, a, b, start, op, A.add), reads, writes, el(n_of(out) // 2))
 
     def cp(out, a, reads, writes, cost=None):
         run("V", lambda e: e.tensor_copy(out, a), reads, writes, cost or el(n_of(out)))
 
-    def turn(out, a, reads, writes):
-        run("V", lambda e: e.transpose(out, a), reads, writes, el(n_of(out) // 2))
+    def turn(out, a, reads, writes, wide=False):
+        run("V", lambda e: e.transpose(out, a), reads, writes, el(n_of(out) // (1 if wide else 2)))
 
     def fill(ap, v, writes):
         run("V", lambda e: e.memset(ap, v), [], writes, el(n_of(ap) // 2))
@@ -178,74 +181,66 @@ def rank_program(g, core, T, topo):
         return T[name][:, a:b].bitcast(dt.uint8)
 
     dma("S", "drt", T.rtt[:, 0:16], T.rt[:, 0:16], [], ["rtt"], 2.0)
-    dma("Y", "dx", T.xt[:, 0:768], T.x[:, :], [], ["xt"], 3.3)
+    dma("Y", "dx", T.xt[:, 0:768], T.x[:, :], [], ["xt"], 3.0)
     dma("Y", "dgr", T.gt[:, 0:768], T.gr[:, :], [], ["gt"], 4.3)
     dma("Y", "dw", T.wt[:, :], T.w[:, :], [], ["wt"], 6.7)
     dma("Y", "dpr", T.prt[:, 0:8], T.pr[:, 0:8], [], ["prt"], 6.9)
     dma("Y", "dub", T.ut[:, :], T.ub[:, :], [], ["ut"], 9.4)
     dma("Y", "dv", T.vt[:, :], T.v[:, :], [], ["vt"], 10.0)
 
-    turn_of[0] = "first"
+    turn_of[0] = "early"
     fill(T.nt[:, :], 0.0, ["nt"])
-    quant("nq", 0, 128, "nt", 0, 512, ["nt"], ["nq"])
-    a = send([(k, codes("ld%d" % k, 0, 2), codes("nq", 0, 2), half[k]) for k in (2, 3, 1)], "az", ["nq"])
-    b = send([(k, T["ld%ds" % k][:, 0:2], T.nqs[:, 0:2], half[k]) for k in (2, 3, 1)], "az", ["nq"])
-    arrive("az", 2 * sum(len(half[k]) for k in half), ["ldz"], [a, b], 6.0)
-    turn_of[0] = ""
-    dma("Y", "dz", codes("ld0", 0, 2), codes("nq", 0, 2), ["nq"], [], 2.0)
-    dma("Y", "dz", T.ld0s[:, 0:2], T.nqs[:, 0:2], ["nq"], ["ldz0"], 2.0)
-
-    turn_of[0] = "prep"
+    turn_of[0] = "first"
+    quant("nq", 48, 176, "nt", 0, 512, ["nt"], ["nq"])
+    a = send([(k, codes("ld%d" % k, z, z + 2), codes("nq", c, c + 2), eng[k]) for k, z, c in ((2, 64, 174), (1, 48, 48))],
+             "az", ["nq"])
+    arrive("az", len(eng[1]) + len(eng[2]), ["ldz"], [a], 6.0)
 
     def iota(out, pattern, base, ch, key, **kw):
-        run("G", lambda e: e.iota(out, pattern, base, ch, **kw), [], [key], 0.15 + 2 * n_of(out) * CY)
+        run("G", lambda e: e.iota(out, pattern, base, ch, **kw), [], key if isinstance(key, list) else [key],
+            0.15 + 2 * n_of(out) * CY)
 
     def pf(i):
         return T.pf[:, i:i + 1]
 
     fl_ok = {"allow_small_or_imprecise_dtypes": True}
-    iota(T.pi[:, 0:1], [[0, 1]], 0, 1, "pi")
+    E3, TIE2, P7, P15, ODD, HIGH, ENT = (T.own[:, 32 * i:32 * i + 1] for i in range(7))
+    turn_of[0] = "early"
+    for i, (pattern, ch) in enumerate([([[0, 2], [1, 2], [0, 8]], 0), ([[2, 4], [0, 8]], 0), ([[0, 4], [1, 8]], 0)]):
+        iota(T.fi[:, 32 * i:32 * i + 32], pattern, 0, ch, "fi%d" % i, **fl_ok)
     iota(T.ii[:, 16:26], [[0, 5], [2, 2]], 0, 0, "i10", **fl_ok)
-    iota(T.ii[:, 32:35], [[-1, 3]], 3, 0, "i3", **fl_ok)
+    turn(T.own[:, 0:96], T.fi[:, 0:96], ["fi0", "fi1", "fi2"], ["owa"], True)
+    turn_of[0] = "prep"
+    for i, (pattern, ch) in enumerate([([[0, 2], [1, 16]], 0), ([[1, 2], [0, 16]], 0), ([[16, 2], [0, 16]], 1),
+                                       ([[16, 2], [112, 16]], 1)], 3):
+        iota(T.fi[:, 32 * i:32 * i + 32], pattern, 0, ch, "fi%d" % i, **fl_ok)
+    turn(T.own[:, 96:224], T.fi[:, 96:224], ["fi%d" % i for i in range(3, 7)], ["owb"], True)
+    iota(T.ii[:, 32:35], [[-2, 3]], 5, 0, "i3", **fl_ok)
     iota(T.ii[:, 0:16], [[7, 16]], 0, 0, "i16", **fl_ok)
-    iota(T.tri0[:, :], [[1, 7], [7, 16]], 0, 0, "tri0", **fl_ok)
-    fill(T.rtt[:, 16:512], 0.0, ["rtz"])
-    fill(T.one[:, :], 1.0, ["one"])
-    fill(T.xt[:, 768:776], 0.0, ["xz"])
-    fill(T.gt[:, 768:776], 0.0, ["gz"])
-    ts(T.pi[:, 1:2], T.pi[:, 0:1], 15, None, A.bitwise_and, None, ["pi"], ["pi1"])
-    ts(T.pi[:, 2:3], T.pi[:, 0:1], 3, 1, A.arith_shift_right, A.bitwise_and, ["pi"], ["pi2"])
-    ts(T.pi[:, 3:4], T.pi[:, 0:1], 3, 3, A.arith_shift_right, A.bitwise_and, ["pi"], ["pi3"])
-    ts(T.pi[:, 4:5], T.pi[:, 0:1], 7, None, A.bitwise_and, None, ["pi"], ["pi4"])
-    ts(T.pi[:, 5:6], T.pi[:, 0:1], 4, 1, A.arith_shift_right, A.bitwise_and, ["pi"], ["pi5"])
-    ts(T.pi[:, 6:7], T.pi[:, 0:1], 4, None, A.arith_shift_right, None, ["pi"], ["pi6"])
-    cp(T.pf[:, 0:7], T.pi[:, 0:7], ["pi", "pi1", "pi2", "pi3", "pi4", "pi5", "pi6"], ["pf"])
-    ts(T.rl[:, 0:10], T.ii[:, 16:26], pf(2), None, A.add, None, ["i10", "pf"], ["rl"])
-    ts(T.tie[:, 4:7], T.ii[:, 32:35], pf(3), 0.5, A.is_gt, A.subtract, ["i3", "pf"], ["tie0"])
-    ts(T.tie[:, 0:3], T.tie[:, 4:7], 2 * TINY, None, A.mult, None, ["tie0"], ["tie"])
-    fill(T.seg[:, :], 1.0, ["seg1"])
-    fill(T.seg[:, 0:3 * NT:3], 0.0, ["seg1", "seg"])
-    ts(pf(16), pf(4), 0.5, None, A.add, None, ["pf"], ["pf16"])
-    ts(T.sb[:, :], T.ii[:, 0:16], pf(16), None, A.add, None, ["i16", "pf16"], ["sb"])
-    ts(pf(7), pf(1), float(NS), None, A.is_lt, None, ["pf"], ["pf7"])
-    ts(pf(8), pf(7), -0.5, 1.0, A.mult, A.add, ["pf7"], ["pf8"])
-    ts(pf(19), pf(8), 7.0, None, A.mult, None, ["pf8"], ["pf19"])
-    ts(pf(20), pf(7), 0.5 * NT, None, A.mult, None, ["pf7"], ["pf20"])
-    ts(pf(9), pf(1), pf(19), pf(20), A.mult, A.add, ["pf", "pf19", "pf20"], ["pf9"])
-    ts(pf(13), pf(1), 7.0, pf(6), A.mult, A.add, ["pf"], ["pf13"])
-    cp(T.pi[:, 7:8], pf(13), ["pf13"], ["pi7"])
-    ts(T.pi[:, 8:9], T.pi[:, 7:8], 15, None, A.bitwise_and, None, ["pi7"], ["pi8"])
-    cp(pf(14), T.pi[:, 8:9], ["pi8"], ["pf14"])
-    tt(pf(15), pf(13), pf(14), A.subtract, ["pf13", "pf14"], ["pf15"])
-    ts(pf(17), pf(0), float(CP), 128.0, A.is_ge, A.mult, ["pf"], ["pf17"])
-    ts(pf(18), pf(17), pf(13), None, A.add, None, ["pf17", "pf13"], ["pf18"])
+    iota(T.seg[:, :], [[0, NT], [1, 3]], 0, 0, "seg", **fl_ok)
+    iota(T.ot[:, 0:512], [[0, 512]], 1, 0, ["one", "oneb"], **fl_ok)
+    iota(T.tri0[:, :], [[16, 7], [112, 16]], 0, 0, "tri0", **fl_ok)
+    turn_of[0] = "early"
+    clear(T.rtt[:, 16:512], "rtz")
+    clear(T.xt[:, 768:776], "xz")
+    turn_of[0] = "prep"
+    clear(T.gt[:, 768:776], "gz")
+    turn_of[0] = "early"
+    ts(T.rl[:, 0:10], T.ii[:, 16:26], E3, None, A.add, None, ["i10", "owa"], ["rl"])
+    turn_of[0] = "prep"
+    ts(T.tie[:, 0:3], T.ii[:, 32:35], TIE2, TINY, A.subtract, A.mult, ["i3", "owa"], ["tie"])
+    ts(T.sb[:, :], T.ii[:, 0:16], P7, 0.5, A.add, A.add, ["i16", "owa"], ["sb"])
+    ts(pf(9), P15, 3.5, 0.5 * NT, A.mult, A.add, ["owb"], ["pf9"])
+    ts(pf(17), HIGH, float(CP), 2048.0, A.is_ge, A.mult, ["owb"], ["pf17"])
+    ts(pf(18), pf(17), ENT, None, A.add, None, ["pf17", "owb"], ["pf18"])
     ts(T.tri[:, :], T.tri0[:, :], pf(18), BELOW - 1.0, A.is_lt, A.mult, ["tri0", "pf18"], ["tri1"])
     ts(T.tri[:, :], T.tri[:, :], 1.0, None, A.add, None, ["tri1"], ["tri"])
     for b in range(4):
         clear(T.et[:, 512 * b:512 * b + 512], "ez%d" % b)
-    run("G", lambda e: e.affine_select(T.idn[:, :], T.one[:, :], [[-1, 128]], A.is_equal, 0.0, 0, 1), ["one"], ["idn"], 0.4)
+    run("G", lambda e: e.affine_select(T.idn[:, :], T.ot[:, 0:128], [[-1, 128]], A.is_equal, 0.0, 0, 1), ["one"], ["idn"], 0.4)
+    iota(T.idr[:, :], [[1, 128]], -CP, 0, "idr", **fl_ok)
     iota(T.k4[:, :], [[0, 8], [1, 16], [16, 4]], 0, 0, "k4", **fl_ok)
-    iota(T.vals[:, :], [[1, CR]], 2, 0, "vals", **fl_ok)
+    iota(T.vals[:, :], [[1, CR + 2]], 0, 0, "vals", **fl_ok)
 
     turn_of[0] = "route"
     quant("rq", 0, 128, "rtt", 0, 512, ["rtt", "rtz"], ["rq"])
@@ -269,15 +264,16 @@ def rank_program(g, core, T, topo):
         act(piece(t, t), T.pref[:, 7 * t:NT], F.Sign, ["pref", "sb"], ["cn%d" % t], bias=T.sb[:, t:t + 1], scale=-1.0,
             accum_out=T.cn[:, t:t + 1])
     for t in range(NS, 16):
-        ts(piece(t, t), T.pref[:, 7 * t:NT], T.sb[:, t:t + 1], None, A.is_le, None, ["pref", "sb"], ["le%d" % t], True)
+        ts(piece(t, t), T.pref[:, 7 * t:NT], T.sb[:, t:t + 1], 2.0, A.is_le, A.mult, ["pref", "sb"], ["le%d" % t], True)
     for t in range(NS, 16):
-        scan(piece(t + 16 - NS, t), piece(t, t), T.nt[:, 0:NT - 7 * t], A.add, ["le%d" % t, "nt"], ["ls%d" % t])
+        scan(piece(t + 16 - NS, t), piece(t, t), T.nt[:, 0:NT - 7 * t], A.add, ["le%d" % t, "nt"], ["ls%d" % t],
+             float(7 * t - NT))
     mine, last = ["cn%d" % t for t in range(NS)], T.le[:, NT * 17 - 1:NT * (32 - NS):NT]
     act(T.cn[:, 16:16 + NS], T.cn[:, 0:NS], F.Copy, mine, ["cnd"])
     for c in (0, 16):
         cp(T.cn[:, c + NS:c + 16], last, ["ls%d" % t for t in range(NS, 16)], ["cnl%d" % c])
     turn(T.cnt[:, :], T.cn[:, :], mine + ["cnd", "cnl0", "cnl16"], ["cnt"])
-    ts(T.off[:, :], T.cnt[:, :], pf(8), pf(9), A.mult, A.add, ["cnt", "pf8", "pf9"], ["off"])
+    ts(T.off[:, :], T.cnt[:, :], 0.5, pf(9), A.mult, A.add, ["cnt", "pf9"], ["off"])
     turn_of[0] = "prep"
     quant("gq", 0, 194, "gt", 0, 776, ["gt", "gz"], ["gq"])
 
@@ -314,24 +310,20 @@ def rank_program(g, core, T, topo):
     quant("wq", 0, 512, "wt", 0, 2048, ["wt"], ["wq"])
     quant("uq", 0, 512, "ut", 0, 2048, ["ut"], ["uq"])
     quant("vq", 0, 128, "vt", 0, 512, ["vt"], ["vq"])
-    clear(T.prt[:, 8:512], "prz")
-    fill(T.zl[:, :], 0, ["zl"])
-    quant("pq", 0, 128, "prt", 0, 512, ["prt", "prz"], ["pq"])
-    pick("pp", 0, 128, "pq", 0, 128, T.zl[:, :], ["pq", "zl"], "pp")
+    for t in range(4):
+        act(T.ppt[:, t:512:4], T.nt[:, 0:128], F.Identity, ["nt", "prt"], ["ppt%d" % t], bias=T.prt[:, t:t + 1])
+    quant("pp", 0, 128, "ppt", 0, 512, ["ppt%d" % t for t in range(4)], ["pp"])
+    for t, v in ((0, -256.0), (1, 160.0), (2, -1.0), (3, 0.0)):
+        act(T.wnt[:, t:512:4], T.ot[:, 0:128], F.Copy, ["one"], ["wnt%d" % t], scale=v)
+    quant("wn", 0, 128, "wnt", 0, 512, ["wnt%d" % t for t in range(4)], ["wn"])
     clear(T.pt[:, 0:512], "pt0")
     clear(T.pt[:, 512:1024], "pt1")
-    fill(T.z3[:, :], 0.0, ["z3"])
-    tt(pf(11), pf(0), pf(1), A.subtract, ["pf"], ["pf11"])
-    ts(T.pt[:, 0:11:5], T.z3[:, 0:3], pf(11), None, A.add, None, ["z3", "pf11", "pt0"], ["pth"])
-    ts(T.pt[:, 512:523:5], T.z3[:, 0:3], pf(1), None, A.add, None, ["z3", "pf", "pt1"], ["ptl"])
-    ts(T.pt[:, 16:27:5], T.z3[:, 0:3], pf(15), None, A.add, None, ["z3", "pf15", "pt0"], ["psh"])
-    ts(T.pt[:, 528:539:5], T.z3[:, 0:3], pf(14), None, A.add, None, ["z3", "pf14", "pt1"], ["psl"])
-    quant("cq", 0, 256, "pt", 0, 1024, ["pt0", "pt1", "pth", "ptl", "psh", "psl"], ["cq"])
+    ts(T.pt[:, 0:11:5], T.nt[:, 0:3], HIGH, None, A.add, None, ["nt", "owb", "pt0"], ["pth"])
+    ts(T.pt[:, 512:523:5], T.nt[:, 0:3], P15, None, A.add, None, ["nt", "owb", "pt1"], ["ptl"])
+    quant("cq", 0, 256, "pt", 0, 1024, ["pt0", "pt1", "pth", "ptl"], ["cq"])
     for k in range(4):
         clear(T.mt[:, 512 * k + 448:512 * k + 512], "mz%d" % k)
         clear(T.dxt[:, 512 * k + 448:512 * k + 512], "dz%d" % k)
-        if k:
-            quant("sd%d" % k, 0, 192, "nt", 0, 768, ["nt"], ["sd%d" % k, "sd%ds" % k])
     fill(pf(12), EPS, ["eps"])
 
     def bank(k, x):
@@ -359,15 +351,18 @@ def rank_program(g, core, T, topo):
         m, rk, one_hot = "qm%d" % k, T.rk[:, 4 * k:4 * k + 1], T.ot[:, 512 * k:512 * k + 512]
         pc, xc, kc = bank(k, 1)
         pr, xr, kr = bank(k, 0)
-        mm(pc[:, xc:xc + 128], "qm", 128 * k, "pp", 0, 128, True, True, [m, "pp", "pps"], [kc])
-        mm(pr[:, xr:xr + 128], "pp", 0, "qm", 128 * k, 128, True, True, [m, "pp", "pps"], [kr])
+        mm(pc[:, xc:xc + 128], "qm", 128 * k, "pp", 0, 128, True, True, [m, "pp"], [kc])
+        mm(pr[:, xr:xr + 128], "pp", 0, "qm", 128 * k, 128, True, True, [m, "pp"], [kr])
         act(T.ca[:, 4 * k:4 * k + 1], pc[:, xc:xc + 1], F.Abs, [kc, "eps"], ["ca%d" % k], bias=pf(12))
         s, sd, sx = (slice(c + CP * k, c + CP * k + CP) for c in (0, 448, 896))
         act(T.ra[:, s], pr[:, xr:xr + CP], F.Abs, [kr, "eps"], ["ra%d" % k], bias=pf(12))
         act(T.ra[:, sd], T.tri[:, :], F.Copy, ["tri", "ca%d" % k], ["rd%d" % k], scale=T.ca[:, 4 * k:4 * k + 1])
-        tt(T.ra[:, sx], T.ra[:, s], T.ra[:, sd], A.is_gt, ["rd%d" % k, "ra%d" % k], ["rx%d" % k])
-        run("V", lambda e: e.tensor_reduce(rk, T.ra[:, sx], AxisListType.X, A.add), ["rx%d" % k], ["rk%d" % k], 0.11)
-        ts(one_hot, T.k4[:, :], rk, None, A.is_equal, None, ["k4", "rk%d" % k], ["ot%d" % k], True)
+        if k:
+            tt(T.ra[:, sx], T.ra[:, s], T.ra[:, sd], A.is_gt, ["rd%d" % k, "ra%d" % k], ["rx%d" % k])
+            run("V", lambda e: e.tensor_reduce(rk, T.ra[:, sx], AxisListType.X, A.add), ["rx%d" % k], ["rk%d" % k], 0.11)
+            ts(one_hot, T.k4[:, :], rk, None, A.is_equal, None, ["k4", "rk%d" % k], ["ot%d" % k], True)
+        else:
+            tt(T.ot[:, 0:448:4], T.ra[:, s], T.ra[:, sd], A.is_gt, ["rd0", "ra0"], ["ot0", "one"])
         quant("qo", 128 * k, 128 * k + 128, "ot", 512 * k, 512 * k + 512, ["ot%d" % k], ["qo%d" % k])
         for b, y in ((0, 2), (1, 3), (2, 1), (3, 0)):
             ps, x, key = bank(k, y)
@@ -376,22 +371,38 @@ def rank_program(g, core, T, topo):
 
     def stage3(k):
         ps, x, key = bank(k, 2)
-        for c in (0, 1):
-            mm(ps[:, x:x + 128], "qo", 128 * k, "cq", 128 * c, 128, c == 0, c == 1, ["qo%d" % k, "cq"], [key])
         quant("qd", 128 * k, 128 * k + 128, "dxt", 512 * k, 512 * k + 512,
               ["dz%d" % k] + ["dt%d_%d" % (k, b) for b in range(4)], ["qd%d" % k])
-        cp(T.lo[:, 8 * k:8 * k + 7], ps[:, x:x + 7], [key], ["lo%d" % k])
         if not k:
-            pick("ld0", 2, CR, "qd", 0, 128, T.lo[:, 0:3], ["qd0", "lo0", "ldz0"], "ld0")
+            mm(ps[:, x:x + 128], "wn", 0, "qo", 0, 128, True, True, ["qo0", "wn"], [key])
+            tt(T.tab[:, 0:CP], T.idr[:, 0:CP], ps[:, x:x + CP], A.max, ["idr", key], ["tab0"], True)
             return
-        d = "sd%d" % k
-        pick(d, 0, CR, "qd", 128 * k, 128 * k + 128, T.lo[:, 8 * k:8 * k + 3], ["qd%d" % k, "lo%d" % k], d)
-        a = send([(k, T.ll[:, 8 * k:8 * k + 3], T.lo[:, 8 * k + 4:8 * k + 7], eng[k])], "al%d", ["lo%d" % k])
-        b = send([(k, codes("ld%d" % k, 2, 2 + CR), codes(d, 0, CR), eng[k][0:4]),
-                  (k, T["ld%ds" % k][:, 2:2 + 4 * CR], T[d + "s"][:, 0:4 * CR], eng[k][4:8])], "ar%d", [d, d + "s"])
-        arrive("al%d" % k, len(eng[k]), ["ll%d" % k], [a], BACK)
-        arrive("ar%d" % k, len(eng[k]), ["ld%d" % k, "ld%ds" % k], [b], BACK)
+        if k == 3:
+            a = send([(3, codes("ld3", 0, CP + 2), codes("qd", 384, 386 + CP), eng[3])], "ar%d", ["qd3"])
+            b = send([(3, T.ld3s[:, 0:CP + 2], T.qds[:, 384:386 + CP], eng[3])], "ar%d", ["qd3"])
+            arrive("ar3", 2 * len(eng[3]), ["ld3", "ld3s"], [a, b], BACK)
+        for c in (0, 1):
+            mm(ps[:, x:x + 128], "qo", 128 * k, "cq", 128 * c, 128, c == 0, c == 1, ["qo%d" % k, "cq"], [key])
+        cp(T.lo[:, 8 * k:8 * k + 3], ps[:, x:x + 3], [key], ["lo%d" % k])
+        if k < 3:
+            d, (c, z, h) = "sd%d" % k, {1: (0, 0, 0), 2: (176, 128, 66)}[k]
+            pick("nq", c, CR, "qd", 128 * k, 128 * k + 128, T.lo[:, 8 * k:8 * k + 3], ["qd%d" % k, "lo%d" % k], d)
+        if k != 2:
+            to = (1,) if k == 1 else (2, 3)
+            a = send([(j, T.ll[:, 8 * j:8 * j + 3], T.lo[:, 8 * j:8 * j + 3], half[j]) for j in to], "al%d",
+                     ["lo%d" % j for j in to])
+            for j in to:
+                arrive("al%d" % j, len(half[j]), ["ll%d" % j], [a], BACK - 0.5)
+        if k < 3:
+            b = send([(k, codes("ld%d" % k, h, h + 24), codes("nq", c, c + 24), eng[k][0:2]),
+                      (k, codes("ld%d" % k, h + 24, h + 48), codes("nq", c + 24, c + 48), eng[k][2:4]),
+                      (k, T["ld%ds" % k][:, h + z - c:h + z - c + 96], T.nqs[:, z:z + 96], eng[k][4:8])], "ar%d",
+                     [d, d + "s", "nq"])
+            arrive("ar%d" % k, len(eng[k]), ["ld%d" % k, "ld%ds" % k], [b], BACK)
 
+    turn_of[0] = "look"
+    fill(T.tab[:, 0:384], 0.0, ["tab0", "tab2", "tab3"])
+    fill(T.tab[:, 384:512], float(CR), ["tab1"])
     for k in range(4):
         turn_of[0] = "k%d" % k
         stage1(k)
@@ -401,38 +412,55 @@ def rank_program(g, core, T, topo):
         stage3(k)
 
     turn_of[0] = "look"
-    h1, h2, h3, h4, h5, h6 = (T.hh[:, 24 * i:24 * i + 24] for i in range(6))
+    h1, h2, h3, h4, h5, h6, h7, h8, h9, h10 = (T.hh[:, 24 * i:24 * i + 24] for i in range(10))
     cp(T.win[:, :], T.ss[:, 2:3 * NT:3], ["ss"], ["win"], el(NT // 2))
     turn(T.tv[:, 0:NT], T.win[:, :], ["win"], ["tw"])
     turn(T.tv[:, NT:2 * NT], T.pref[:, :], ["pref"], ["tp"])
     tw, tp = T.tv[:, 0:NT:8], T.tv[:, NT:2 * NT:8]
     ts(h1, tw, 0.0, None, A.is_gt, None, ["tw"], ["h1"])
     ts(h2, tp, float(CP), None, A.is_le, None, ["tp"], ["h2"])
-    ts(h3, tp, float(CP + 1), None, A.subtract, None, ["tp"], ["h3"])
-    ts(h6, tw, -0.5, 2.5, A.mult, A.add, ["tw"], ["h6"])
+    ts(h6, tw, 4.0, 1.0, A.is_lt, A.add, ["tw"], ["h6"])
     tt(h4, h1, h2, A.mult, ["h1", "h2"], ["h4"])
+    ts(h7, tp, 1.0 / 7, -4.0 / 7, A.mult, A.add, ["tp"], ["h7"])
+    ts(h8, h7, WHOLE, WHOLE, A.add, A.subtract, ["h7"], ["h8"])
+    ts(h9, h8, -111.0, -16.0 - CP, A.mult, A.add, ["h8"], ["h9"])
+    act(h10, tp, F.Copy, ["tp"], ["h10"], scale=16.0)
+    tt(h3, h9, h10, A.add, ["h9", "h10"], ["h3"])
     tt(h5, h4, h3, A.mult, ["h4", "h3"], ["h5"])
-    ts(pf(10), pf(5), -1.0, 1.0, A.mult, A.add, ["pf"], ["pf10"])
-    for k in range(4):
+    ts(pf(10), ODD, -1.0, 1.0, A.mult, A.add, ["owb"], ["pf10"])
+    for k in (0, 1, 2, 3):
         e = rank ^ k
         for h in (0, 1):
-            o, p = slice(12 * k + h, 12 * k + 12, 2), (10, 5)[h]
+            o, p = slice(12 * POS[k] + h, 12 * POS[k] + 12, 2), (pf(10), ODD)[h]
             ts(T.offt[:, o], T.hh[:, 96 + e:120:4], float(CP), None, A.add, None, ["h5"], ["offt%d%d" % (k, h)])
-            act(T.wgt[:, o], T.hh[:, 120 + e:144:4], F.Copy, ["h6", "pf", "pf10"], ["wgt%d%d" % (k, h)], scale=pf(p))
-    for k in range(4):
-        fill(T.tab[:, 128 * k:128 * k + 128], 0.0, ["tab%d" % k])
+            act(T.wgt[:, o], T.hh[:, 120 + e:144:4], F.Copy, ["h6", "owb", "pf10"], ["wgt%d%d" % (k, h)], scale=p)
     fill(T.cs[:, :], 0.0, ["csz"])
 
     def home(k, first, last):
-        tab, zc, offt = T.tab[:, 128 * k:128 * k + 128], "zc%d" % k, T.offt[:, 12 * k:12 * k + 12]
-        lst, key = (T.ll[:, 8 * k:8 * k + 3], "ll%d" % k) if k else (T.lo[:, 4:7], "lo0")
+        tab, zc, q = T.tab[:, 128 * TAB[k]:128 * TAB[k] + 128], "zc%d" % k, 12 * POS[k]
+        offt, of, ko = T.offt[:, q:q + 12], T.hof[:, q:q + 12], ["offt%d0" % k, "offt%d1" % k]
         s, s1 = slice(192 * k, 192 * k + 192), slice(768 + 192 * k, 960 + 192 * k)
-        cp(tab.indirect(lst), T.vals[:, :], ["vals", key], ["tab%d" % k], 0.23)
-        act(T.gg[:, s], tab.indirect(offt), F.Copy, ["tab%d" % k, "offt%d0" % k, "offt%d1" % k], ["gr0%d" % k], 0.35)
+        lst, g1 = T.ll[:, 8 * k:8 * k + 3], T.gg[:, 768 + 192 * k:960 + 192 * k:16]
+        if k in (1, 2):
+            cp(tab.indirect(lst), T.vals[:, 2 * k - 2:2 * k - 2 + CR], ["vals", "ll%d" % k], ["tab%d" % k], 0.23)
+        elif k:
+            cp(tab.indirect(lst), T.ot[:, 448:448 + CR], ["oneb", "ll3"], ["tab3"], 0.23)
+            act(T.gid[:, :], T.idr[:, :].indirect(offt), F.Copy, ["idr"] + ko, ["gid"], 0.35)
+        if k == 3:
+            run("V", lambda e: e.tensor_tensor(T.gg[:, s], tab.indirect(offt), T.gid[:, :], A.mult),
+                ["tab3", "gid"] + ko, ["gr03"], 0.35)
+        else:
+            act(T.gg[:, s], tab.indirect(offt), F.Copy, ["tab%d" % k] + ko, ["gr0%d" % k], 0.35)
         turn(T.gg[:, s1], T.gg[:, s], ["gr0%d" % k], ["gr1%d" % k])
-        of = T.hof[:, 12 * k:12 * k + 12]
-        cp(of, T.gg[:, 768 + 192 * k:960 + 192 * k:16], ["gr1%d" % k], ["hof%d" % k])
-        pick(zc, 0, NT, "ld%d" % k, 0, 50, of, ["hof%d" % k, "ld%d" % k, "ld%ds" % k, "ldz" if k else "ldz0"], zc)
+        if k in (1, 2):
+            cp(of, g1, ["gr1%d" % k], ["hof%d" % k])
+            pick(zc, 0, NT, "ld%d" % k, 64 * k - 64, 64 * k - 14, of, ["hof%d" % k, "ld%d" % k, "ld%ds" % k, "ldz"], zc)
+        else:
+            ts(of, g1, 0.0, float(CP), A.min, A.add, ["gr1%d" % k], ["hof%d" % k])
+            if k:
+                pick(zc, 0, NT, "ld3", 0, CP + 2, of, ["hof3", "ld3", "ld3s"], zc)
+            else:
+                pick(zc, 0, NT, "qd", 0, 128, of, ["hof0", "qd0"], zc)
         for b in range(4):
             mm(T.pz[:, 512 * b:512 * b + NT], "eq", 128 * b, zc, 0, NT, first, last, ["eq", zc, zc + "s"], ["*z%d" % b])
 
@@ -440,22 +468,27 @@ def rank_program(g, core, T, topo):
         turn_of[0] = "h%d" % k
         home(k, k == 0, k == 3)
     turn_of[0] = "ct"
-    ts(T.ff[:, 0:48], T.hof[:, 0:48], 1.0, None, A.is_gt, None, ["hof%d" % k for k in range(4)], ["fl"])
-    tt(T.ff[:, 48:96], T.ff[:, 0:48], T.wgt[:, :], A.mult, ["fl"] + ["wgt%d%d" % (k, h) for k in range(4) for h in (0, 1)], ["fw"])
+    ts(T.ff[:, 0:24], T.hof[:, 0:24], CP - 0.5, None, A.is_lt, None, ["hof0", "hof3"], ["fl0"])
+    ts(T.ff[:, 24:36], T.hof[:, 24:36], CR - 0.5, None, A.is_lt, None, ["hof1"], ["fl1"])
+    ts(T.ff[:, 36:48], T.hof[:, 36:48], 1.0, None, A.is_gt, None, ["hof2"], ["fl2"])
+    tt(T.ff[:, 48:96], T.ff[:, 0:48], T.wgt[:, :], A.mult,
+       ["fl0", "fl1", "fl2"] + ["wgt%d%d" % (k, h) for k in range(4) for h in (0, 1)], ["fw"])
     tt(T.ff[:, 96:120], T.ff[:, 48:72], T.ff[:, 72:96], A.add, ["fw"], ["fs"])
     tt(T.ff[:, 120:132], T.ff[:, 96:108], T.ff[:, 108:120], A.add, ["fs"], ["ft"])
     tt(T.cs[:, 0:6], T.ff[:, 120:132:2], T.ff[:, 121:132:2], A.add, ["ft", "csz"], ["cs"])
-    turn(T.cst[0:32, :], T.cs[0:32, :], ["cs", "csz"], ["cst"])
+    turn(T.cst[0:32, :], T.cs[0:32, :], ["cs", "csz"], ["cst"], True)
 
     turn_of[0] = ""
-    for b in (0, 1):
-        act(T.zt[:, b:768:4], T.pz[:, 512 * b:512 * b + NT], F.Copy, ["*z%d" % b], ["zt%d" % b])
-    for b in (2, 3):
-        cp(T.zt[:, b:768:4], T.pz[:, 512 * b:512 * b + NT], ["*z%d" % b], ["zt%d" % b])
+    for b in range(4):
+        move = (T.zt[:, b:768:4], T.pz[:, 512 * b:512 * b + NT])
+        if b % 2:
+            cp(move[0], move[1], ["*z%d" % b], ["zt%d" % b])
+        else:
+            act(move[0], move[1], F.Copy, ["*z%d" % b], ["zt%d" % b])
     quant("zq", 0, 192, "zt", 0, 768, ["zt0", "zt1", "zt2", "zt3"], ["zq"])
     mm(T.px[:, 0:NT], "vq", 0, "zq", 0, NT, True, True, ["vq", "zq"], ["*x0"])
     cp(T.ysb[:, :], T.px[:, 0:NT], ["*x0"], ["ysb"])
-    dma("S", "dos", T.ct[0:1, 0:NT], T.cst[0:6, 0:32], ["cst"], [], 2.0)
+    dma("Y", "doy", T.ct[0:1, 0:NT], T.cst[0:6, 0:32], ["cst"], [], 2.0)
     dma("Y", "doy", T.oc[:, 0:768], T.zq[:, 0:NT].bitcast(dt.uint8), ["zq"], [], 2.0)
     for i in range(4):
         q, s = ("S", "dos") if i < 3 else ("Y", "doy")

from concourse.bass import DstId, RemoteDMATransfer
from concourse.mybir import dt, AluOpType as A, AxisListType, ActivationFunctionType as F

NT, CP, CR = 192, 112, 48
NS = 7
TINY = 2.0 ** -100
EPS = 2.0 ** -120
BELOW = 1.0 - 2.0 ** -24
WHOLE = 1.5 * 2.0 ** 23
HOP, CY, PE, OUT, BACK = 0.11, 0.001, 0.0012, {1: 2.2, 2: 2.7, 3: 4.5}, 3.6
AHEAD = {"first": 0.2, "early": 21.0, "route": 0.8, "prep": -8.9, "out": 0.1, "look": -4.3, "ct": -2.1, "": -11.3,
         "k0": -4.2, "k0b": 4.3, "k0c": 0.1, "k1": 2.7, "k1b": -3.1, "k1c": 0.0, "k2": -3.0, "k2b": 0.3, "k2c": 0.5,
         "k3": -0.4, "k3b": 1.4, "k3c": 3.1, "h0": -13.7, "h1": -2.0, "h2": -1.8, "h3": -2.5}
HOLD, GAP = 0.5, 1.0
TAB = {0: 0, 2: 1, 3: 2, 1: 3}
POS = {0: 0, 3: 1, 1: 2, 2: 3}

SCRATCH = {
    "xt": ("sbuf", [128, 776], "bfloat16"), "gt": ("sbuf", [128, 776], "bfloat16"),
    "rtt": ("sbuf", [128, 512], "bfloat16"), "prt": ("sbuf", [128, 16], "bfloat16"), "nt": ("sbuf", [128, 512], "bfloat16"),
    "wt": ("sbuf", [128, 2048], "bfloat16"), "ut": ("sbuf", [128, 2048], "bfloat16"), "ppt": ("sbuf", [128, 512], "bfloat16"),
    "vt": ("sbuf", [128, 512], "bfloat16"), "et": ("sbuf", [128, 2048], "bfloat16"), "wnt": ("sbuf", [128, 512], "bfloat16"),
    "pt": ("sbuf", [128, 1024], "bfloat16"), "zt": ("sbuf", [128, 768], "bfloat16"),
    "fi": ("sbuf", [128, 224], "float32"), "own": ("sbuf", [128, 224], "float32"),
    "pf": ("sbuf", [128, 24], "float32"), "ii": ("sbuf", [128, 48], "float32"),
    "rl": ("sbuf", [128, 16], "uint16"), "tie": ("sbuf", [128, 8], "float32"), "sb": ("sbuf", [128, 16], "float32"),
    "tri0": ("sbuf", [128, 112], "float32"), "tri": ("sbuf", [128, 112], "float32"),
    "idn": ("sbuf", [128, 128], "bfloat16"), "idr": ("sbuf", [128, 128], "bfloat16"), "gid": ("sbuf", [128, 192], "bfloat16"),
    "vals": ("sbuf", [128, 50], "bfloat16"), "k4": ("sbuf", [128, 512], "bfloat16"),
    "s0": ("sbuf", [128, 192], "float32"), "dd": ("sbuf", [128, 576], "float32"), "sg": ("sbuf", [128, 576], "bfloat16"),
    "seg": ("sbuf", [128, 576], "bfloat16"), "ss": ("sbuf", [128, 576], "bfloat16"),
    "win": ("sbuf", [128, 192], "bfloat16"), "m": ("sbuf", [128, 192], "bfloat16"), "pref": ("sbuf", [128, 192], "bfloat16"),
    "le": ("sbuf", [128, 192 * (32 - NS)], "bfloat16"),
    "cn": ("sbuf", [128, 32], "float32"), "cnt": ("sbuf", [128, 32], "float32"), "off": ("sbuf", [128, 32], "uint16"),
    "tv": ("sbuf", [128, 384], "bfloat16"), "hh": ("sbuf", [128, 240], "float32"),
    "offt": ("sbuf", [128, 48], "uint16"), "wgt": ("sbuf", [128, 48], "float32"),
    "tab": ("sbuf", [128, 512], "bfloat16"), "gg": ("sbuf", [128, 1536], "bfloat16"), "hof": ("sbuf", [128, 48], "uint16"),
    "ff": ("sbuf", [128, 144], "float32"), "cs": ("sbuf", [128, 32], "float32"), "cst": ("sbuf", [128, 32], "float32"),
    "ysb": ("sbuf", [128, 192], "float32"), "ll": ("sbuf", [128, 32], "uint16"), "lo": ("sbuf", [128, 32], "uint16"),
    "mt": ("sbuf", [128, 2048], "bfloat16"), "dxt": ("sbuf", [128, 2048], "bfloat16"), "ot": ("sbuf", [128, 2048], "bfloat16"),
    "sm": ("sbuf", [128, 1792], "bfloat16"), "mk": ("sbuf", [128, 1792], "bfloat16"), "ra": ("sbuf", [128, 1344], "float32"),
    "ca": ("sbuf", [128, 16], "float32"), "rk": ("sbuf", [128, 16], "float32"),
    "pz": ("psum", [128, 2048], "float32"), "px": ("psum", [128, 2048], "float32"),
}
_CODES = [("xq", 194), ("gq", 194), ("rq", 128), ("rp", 160), ("pp", 128), ("wq", 512), ("uq", 512), ("wn", 128),
          ("vq", 128), ("eq", 512), ("cq", 256), ("zq", 192), ("qm", 512), ("qd", 512), ("qo", 512), ("nq", 224)]
for _k in range(4):
    _CODES += [("lc%d" % _k, 224), ("zc%d" % _k, 192)]
    if _k:
        _CODES += [("sc%d" % _k, 224), ("ld%d" % _k, 128)]
for _n, _w in _CODES:
    SCRATCH[_n] = ("sbuf", [128, _w], "float8_e4m3fn_x4")
    SCRATCH[_n + "s"] = ("sbuf", [128, _w], "uint8")

SEMAPHORES = ["cV", "cS", "cP", "cG", "dx", "dgr", "drt", "dpr", "dw", "dub", "dv", "doy", "dos", "left", "az"]
for _k in (1, 2, 3):
    SEMAPHORES += ["ax%d" % _k, "al%d" % _k, "ar%d" % _k]


def rank_program(g, core, T, topo):
    rank = T.rank_of(core)
    if rank is None:
        return
    queue = {"V": g.vector, "S": g.scalar, "P": g.tensor, "G": g, "Y": g.sync}
    tasks, wrote, read, total = [], {}, {}, {}
    turn_of = [""]

    def task(q, call, reads, writes, cost, sem=None, inc=1, late=0.0, after=()):
        before = {i: True for i in after}
        for k in reads:
            if k in wrote:
                before[wrote[k]] = True
            if k[0] == "*":
                for i in read.get(k, []):
                    if tasks[i]["q"] != q:
                        before[i] = True
        for k in writes:
            if k in wrote:
                i = wrote[k]
                before[i] = before.get(i, False) or not (q == "P" and tasks[i]["q"] == "P")
            for i in read.get(k, []):
                before[i] = before.get(i, False) or tasks[i]["q"] != q
        n = len(tasks)
        tasks.append({"q": q, "call": call, "before": before, "cost": cost, "late": late, "sem": sem, "inc": inc,
                      "ahead": AHEAD.get(turn_of[0], 0.0)})
        for k in reads:
            read.setdefault(k, []).append(n)
        for k in writes:
            wrote[k], read[k] = n, []
        return n

    def run(q, call, reads, writes, cost):
        return task(q, call, reads, writes, cost, "c" + q)

    def dma(q, sem, out, in_, reads, writes, late):
        return task(q, lambda e: e.dma_start(out, in_), reads, writes, 0.06, sem, 16, late)

    def n_of(a):
        n = 1
        for w in a.shape[1:]:
            n *= w
        return n

    def el(n):
        return max(64, n) * CY

    def ts(out, in0, s1, s2, o0, o1, reads, writes, fast=False):
        c = el(n_of(in0) // (2 if fast else 1))
        if o1 is None:
            run("V", lambda e: e.tensor_scalar(out, in0, s1, None, o0), reads, writes, c)
        else:
            run("V", lambda e: e.tensor_scalar(out, in0, s1, s2, o0, o1), reads, writes, c)

    def tt(out, a, b, op, reads, writes, psum=False):
        run("V", lambda e: e.tensor_tensor(out, a, b, op), reads, writes, el(n_of(out) * (1 if psum else 2)))

    def scan(out, a, b, op, reads, writes, start=0.0):
        run("V", lambda e: e.tensor_tensor_scan(out, a, b, start, op, A.add), reads, writes, el(n_of(out) // 2))

    def cp(out, a, reads, writes, cost=None):
        run("V", lambda e: e.tensor_copy(out, a), reads, writes, cost or el(n_of(out)))

    def turn(out, a, reads, writes, wide=False):
        run("V", lambda e: e.transpose(out, a), reads, writes, el(n_of(out) // (1 if wide else 2)))

    def fill(ap, v, writes):
        run("V", lambda e: e.memset(ap, v), [], writes, el(n_of(ap) // 2))

    def act(out, a, f, reads, writes, cost=None, **kw):
        run("S", lambda e: e.activation(out, a, f, **kw), reads, writes, cost or el(n_of(out)))

    def clear(ap, key):
        act(ap, T.nt[:, 0:n_of(ap)], F.Copy, ["nt"], [key])

    def quant(q, a, b, tile, c, d, reads, writes):
        o, s, i = T[q][:, a:b], T[q + "s"][:, a:b], T[tile][:, c:d]
        run("V", lambda e: e.quantize_mx(o, s, i), reads, writes, 0.014 + 0.00026 * (d - c))

    def mm(out, l, la, r, ra, n, start, stop, reads, writes):
        w, ws, x, xs = T[l][:, la:la + 128], T[l + "s"][:, la:la + 128], T[r][:, ra:ra + n], T[r + "s"][:, ra:ra + n]
        run("P", lambda e: e.matmul_mx(out, w, ws, x, xs, start, stop), reads, writes, (n + 16) * PE)

    def pick(dst, c, n, src, a, b, offs, reads, key):
        o, i = T[dst][:, c:c + n].bitcast(dt.uint32), T[src][:, a:b].bitcast(dt.uint32).indirect(offs)
        cp(o, i, reads, [key], 0.05 + 1.5 * n * CY)
        act(T[dst + "s"][:, c:c + n], T[src + "s"][:, a:b].indirect(offs), F.Copy, reads, [key + "s"], 0.065 + 1.5 * n * CY)

    peer = [T.cores[rank ^ k] for k in range(4)]
    away = [k for k in (1, 2, 3) if topo.chip(peer[k]) != topo.chip(core)]
    out_eng = topo.engines(core, peer[away[0]])
    near_eng = [e for e in topo.engines(core, peer[1]) if e not in out_eng] or out_eng
    eng = {k: (out_eng if k in away else near_eng) for k in (1, 2, 3)}
    half = {k: (out_eng[4 * away.index(k):4 * away.index(k) + 4] if k in away else near_eng) for k in (1, 2, 3)}

    def bits(es):
        return sum(1 << e for e in es)

    def send(parts, sem, reads):
        total["left"] = total.get("left", 0) + sum(len(p[3]) for p in parts)

        def call(e):
            if len(parts) == 1:
                k, dst, src, es = parts[0]
                rid, pid, _s = topo.addr(peer[k])
                g.remote_dma(out_ap=dst, in_ap=src, remote_sem=T.sem[sem % k], local_sem=T.sem["left"], pid=pid,
                             routing_id=rid, dma_engine_mask=bits(es))
                return
            tr = []
            for k, dst, src, es in parts:
                rid, pid, _s = topo.addr(peer[k])
                tr.append(RemoteDMATransfer(dst_ids=[DstId(rid=rid, pnc=pid)], dma_engine_mask=bits(es),
                                            remote_sem=T.sem[sem % k if "%" in sem else sem], srcs=[src], dsts=[dst]))
            g.remote_dma_fused(tr, local_sem=T.sem["left"])
        return task("G", call, reads, [], 0.9)

    def arrive(sem, n, keys, after, late):
        total[sem] = total.get(sem, 0) + n
        return task(None, None, [], keys, 0.0, sem, total[sem], late, after)

    def codes(name, a, b):
        return T[name][:, a:b].bitcast(dt.uint8)

    dma("S", "drt", T.rtt[:, 0:16], T.rt[:, 0:16], [], ["rtt"], 2.0)
    dma("Y", "dx", T.xt[:, 0:768], T.x[:, :], [], ["xt"], 3.0)
    dma("Y", "dgr", T.gt[:, 0:768], T.gr[:, :], [], ["gt"], 4.3)
    dma("Y", "dw", T.wt[:, :], T.w[:, :], [], ["wt"], 6.7)
    dma("Y", "dpr", T.prt[:, 0:8], T.pr[:, 0:8], [], ["prt"], 6.9)
    dma("Y", "dub", T.ut[:, :], T.ub[:, :], [], ["ut"], 9.4)
    dma("Y", "dv", T.vt[:, :], T.v[:, :], [], ["vt"], 10.0)

    turn_of[0] = "early"
    fill(T.nt[:, :], 0.0, ["nt"])
    turn_of[0] = "first"
    quant("nq", 48, 176, "nt", 0, 512, ["nt"], ["nq"])
    a = send([(k, codes("ld%d" % k, z, z + 2), codes("nq", c, c + 2), eng[k]) for k, z, c in ((2, 64, 174), (1, 48, 48))],
             "az", ["nq"])
    arrive("az", len(eng[1]) + len(eng[2]), ["ldz"], [a], 6.0)

    def iota(out, pattern, base, ch, key, **kw):
        run("G", lambda e: e.iota(out, pattern, base, ch, **kw), [], key if isinstance(key, list) else [key],
            0.15 + 2 * n_of(out) * CY)

    def pf(i):
        return T.pf[:, i:i + 1]

    fl_ok = {"allow_small_or_imprecise_dtypes": True}
    E3, TIE2, P7, P15, ODD, HIGH, ENT = (T.own[:, 32 * i:32 * i + 1] for i in range(7))
    turn_of[0] = "early"
    for i, (pattern, ch) in enumerate([([[0, 2], [1, 2], [0, 8]], 0), ([[2, 4], [0, 8]], 0), ([[0, 4], [1, 8]], 0)]):
        iota(T.fi[:, 32 * i:32 * i + 32], pattern, 0, ch, "fi%d" % i, **fl_ok)
    iota(T.ii[:, 16:26], [[0, 5], [2, 2]], 0, 0, "i10", **fl_ok)
    turn(T.own[:, 0:96], T.fi[:, 0:96], ["fi0", "fi1", "fi2"], ["owa"], True)
    turn_of[0] = "prep"
    for i, (pattern, ch) in enumerate([([[0, 2], [1, 16]], 0), ([[1, 2], [0, 16]], 0), ([[16, 2], [0, 16]], 1),
                                       ([[16, 2], [112, 16]], 1)], 3):
        iota(T.fi[:, 32 * i:32 * i + 32], pattern, 0, ch, "fi%d" % i, **fl_ok)
    turn(T.own[:, 96:224], T.fi[:, 96:224], ["fi%d" % i for i in range(3, 7)], ["owb"], True)
    iota(T.ii[:, 32:35], [[-2, 3]], 5, 0, "i3", **fl_ok)
    iota(T.ii[:, 0:16], [[7, 16]], 0, 0, "i16", **fl_ok)
    iota(T.seg[:, :], [[0, NT], [1, 3]], 0, 0, "seg", **fl_ok)
    iota(T.ot[:, 0:512], [[0, 512]], 1, 0, ["one", "oneb"], **fl_ok)
    iota(T.tri0[:, :], [[16, 7], [112, 16]], 0, 0, "tri0", **fl_ok)
    turn_of[0] = "early"
    clear(T.rtt[:, 16:512], "rtz")
    clear(T.xt[:, 768:776], "xz")
    turn_of[0] = "prep"
    clear(T.gt[:, 768:776], "gz")
    turn_of[0] = "early"
    ts(T.rl[:, 0:10], T.ii[:, 16:26], E3, None, A.add, None, ["i10", "owa"], ["rl"])
    turn_of[0] = "prep"
    ts(T.tie[:, 0:3], T.ii[:, 32:35], TIE2, TINY, A.subtract, A.mult, ["i3", "owa"], ["tie"])
    ts(T.sb[:, :], T.ii[:, 0:16], P7, 0.5, A.add, A.add, ["i16", "owa"], ["sb"])
    ts(pf(9), P15, 3.5, 0.5 * NT, A.mult, A.add, ["owb"], ["pf9"])
    ts(pf(17), HIGH, float(CP), 2048.0, A.is_ge, A.mult, ["owb"], ["pf17"])
    ts(pf(18), pf(17), ENT, None, A.add, None, ["pf17", "owb"], ["pf18"])
    ts(T.tri[:, :], T.tri0[:, :], pf(18), BELOW - 1.0, A.is_lt, A.mult, ["tri0", "pf18"], ["tri1"])
    ts(T.tri[:, :], T.tri[:, :], 1.0, None, A.add, None, ["tri1"], ["tri"])
    for b in range(4):
        clear(T.et[:, 512 * b:512 * b + 512], "ez%d" % b)
    run("G", lambda e: e.affine_select(T.idn[:, :], T.ot[:, 0:128], [[-1, 128]], A.is_equal, 0.0, 0, 1), ["one"], ["idn"], 0.4)
    iota(T.idr[:, :], [[1, 128]], -CP, 0, "idr", **fl_ok)
    iota(T.k4[:, :], [[0, 8], [1, 16], [16, 4]], 0, 0, "k4", **fl_ok)
    iota(T.vals[:, :], [[1, CR + 2]], 0, 0, "vals", **fl_ok)

    turn_of[0] = "route"
    quant("rq", 0, 128, "rtt", 0, 512, ["rtt", "rtz"], ["rq"])
    pick("rp", 0, 160, "rq", 0, 128, T.rl[:, 0:10], ["rq", "rl"], "rp")
    quant("xq", 0, 194, "xt", 0, 776, ["xt", "xz"], ["xq"])
    for r in range(4):
        mm(T.pz[:, 512 * r:512 * r + NT], "rp", 8 * r, "xq", 0, NT, True, True, ["rp", "rps", "xq"], ["*z%d" % r])
    act(T.s0[:, :], T.pz[:, 0:NT], F.Copy, ["*z0"], ["s0"])
    for r in (1, 2, 3):
        a = NT * (r - 1)
        tt(T.dd[:, a:a + NT], T.s0[:, :], T.pz[:, 512 * r:512 * r + NT], A.subtract, ["s0", "*z%d" % r], ["dd%d" % r], True)
        act(T.sg[:, r - 1:3 * NT:3], T.dd[:, a:a + NT], F.Sign, ["dd%d" % r, "tie"], ["sg%d" % r], bias=T.tie[:, r - 1:r])
    scan(T.ss[:, :], T.seg[:, :], T.sg[:, :], A.mult, ["seg", "sg1", "sg2", "sg3"], ["ss"])
    ts(T.m[:, :], T.ss[:, 2:3 * NT:3], 0.0, None, A.is_gt, None, ["ss"], ["m"], True)
    scan(T.pref[:, :], T.m[:, :], T.nt[:, 0:NT], A.add, ["m", "nt"], ["pref"])

    def piece(i, t):
        return T.le[:, NT * i + 7 * t:NT * i + NT]

    for t in range(NS):
        act(piece(t, t), T.pref[:, 7 * t:NT], F.Sign, ["pref", "sb"], ["cn%d" % t], bias=T.sb[:, t:t + 1], scale=-1.0,
            accum_out=T.cn[:, t:t + 1])
    for t in range(NS, 16):
        ts(piece(t, t), T.pref[:, 7 * t:NT], T.sb[:, t:t + 1], 2.0, A.is_le, A.mult, ["pref", "sb"], ["le%d" % t], True)
    for t in range(NS, 16):
        scan(piece(t + 16 - NS, t), piece(t, t), T.nt[:, 0:NT - 7 * t], A.add, ["le%d" % t, "nt"], ["ls%d" % t],
             float(7 * t - NT))
    mine, last = ["cn%d" % t for t in range(NS)], T.le[:, NT * 17 - 1:NT * (32 - NS):NT]
    act(T.cn[:, 16:16 + NS], T.cn[:, 0:NS], F.Copy, mine, ["cnd"])
    for c in (0, 16):
        cp(T.cn[:, c + NS:c + 16], last, ["ls%d" % t for t in range(NS, 16)], ["cnl%d" % c])
    turn(T.cnt[:, :], T.cn[:, :], mine + ["cnd", "cnl0", "cnl16"], ["cnt"])
    ts(T.off[:, :], T.cnt[:, :], 0.5, pf(9), A.mult, A.add, ["cnt", "pf9"], ["off"])
    turn_of[0] = "prep"
    quant("gq", 0, 194, "gt", 0, 776, ["gt", "gz"], ["gq"])

    def take(k):
        o = T.off[:, 8 * (rank ^ k):8 * (rank ^ k) + 7]
        d = ("sc%d" if k else "lc%d") % k

        def part(c, src, key):
            cost, r = 1.5 * CP * CY, [src, "off"]
            cp(T[d][:, c:c + CP].bitcast(dt.uint32), T[src][:, 0:194].bitcast(dt.uint32).indirect(o), r, [d + key], 0.05 + cost)
            act(T[d + "s"][:, c:c + CP], T[src + "s"][:, 0:194].indirect(o), F.Copy, r, [d + key + "s"], 0.065 + cost)
        part(CP, "xq", "x")
        part(0, "gq", "g")

    turn_of[0] = "out"
    out = {}
    for k in (1, 2, 3):
        take(k)
        out[k] = send([(k, codes("lc%d" % k, 0, 2 * CP), codes("sc%d" % k, 0, 2 * CP), eng[k])], "ax%d",
                      ["sc%dx" % k, "sc%dg" % k])
    b = send([(k, T["lc%ds" % k][:, 0:2 * CP], T["sc%ds" % k][:, 0:2 * CP], half[k]) for k in (2, 3, 1)], "ax%d",
             [n % k for k in (2, 3, 1) for n in ("sc%dxs", "sc%dgs")])
    for k in (1, 2, 3):
        arrive("ax%d" % k, len(eng[k]) + len(half[k]), ["lc%d" % k], [out[k], b], OUT[k])
    turn_of[0] = "k0"
    take(0)
    came = {k: ["lc%d" % k] for k in (1, 2, 3)}
    came[0] = ["lc0x", "lc0g", "lc0xs", "lc0gs"]

    turn_of[0] = "prep"
    for b in range(4):
        act(T.et[:, 512 * b + b:512 * b + 512:4], T.idn[:, :], F.Copy, ["idn", "ez%d" % b], ["et%d" % b])
    quant("eq", 0, 512, "et", 0, 2048, ["et0", "et1", "et2", "et3"], ["eq"])
    quant("wq", 0, 512, "wt", 0, 2048, ["wt"], ["wq"])
    quant("uq", 0, 512, "ut", 0, 2048, ["ut"], ["uq"])
    quant("vq", 0, 128, "vt", 0, 512, ["vt"], ["vq"])
    for t in range(4):
        act(T.ppt[:, t:512:4], T.nt[:, 0:128], F.Identity, ["nt", "prt"], ["ppt%d" % t], bias=T.prt[:, t:t + 1])
    quant("pp", 0, 128, "ppt", 0, 512, ["ppt%d" % t for t in range(4)], ["pp"])
    for t, v in ((0, -256.0), (1, 160.0), (2, -1.0), (3, 0.0)):
        act(T.wnt[:, t:512:4], T.ot[:, 0:128], F.Copy, ["one"], ["wnt%d" % t], scale=v)
    quant("wn", 0, 128, "wnt", 0, 512, ["wnt%d" % t for t in range(4)], ["wn"])
    clear(T.pt[:, 0:512], "pt0")
    clear(T.pt[:, 512:1024], "pt1")
    ts(T.pt[:, 0:11:5], T.nt[:, 0:3], HIGH, None, A.add, None, ["nt", "owb", "pt0"], ["pth"])
    ts(T.pt[:, 512:523:5], T.nt[:, 0:3], P15, None, A.add, None, ["nt", "owb", "pt1"], ["ptl"])
    quant("cq", 0, 256, "pt", 0, 1024, ["pt0", "pt1", "pth", "ptl"], ["cq"])
    for k in range(4):
        clear(T.mt[:, 512 * k + 448:512 * k + 512], "mz%d" % k)
        clear(T.dxt[:, 512 * k + 448:512 * k + 512], "dz%d" % k)
    fill(pf(12), EPS, ["eps"])

    def bank(k, x):
        return (T.px if k % 2 else T.pz), 512 * x, "*%s%d" % ("zx"[k % 2], x)

    def stage1(k):
        lc, c = "lc%d" % k, came[k]
        for b in range(4):
            ps, x, key = bank(k, b % 2)
            mm(ps[:, x:x + 128], "wq", 128 * b, lc, 96, 128, True, True, ["wq"] + c, [key])
            o = 448 * k + CP * b
            if b == 3:
                ts(T.mk[:, o:o + CP], ps[:, x + 16:x + 128], 0.0, None, A.is_gt, None, [key], ["mk%d_%d" % (k, b)])
            else:
                act(T.sm[:, o:o + CP], ps[:, x + 16:x + 128], F.Sign, [key], ["sm%d_%d" % (k, b)])
                act(T.mk[:, o:o + CP], T.sm[:, o:o + CP], F.Relu, ["sm%d_%d" % (k, b)], ["mk%d_%d" % (k, b)])
            ps, x, key = bank(k, 2 + b % 2)
            mm(ps[:, x:x + 128], "eq", 128 * b, lc, 0, 128, True, True, ["eq"] + c, [key])
            tt(T.mt[:, 512 * k + b:512 * k + 448:4], T.mk[:, o:o + CP], ps[:, x:x + CP], A.mult,
               ["mk%d_%d" % (k, b), key], ["mt%d_%d" % (k, b)], True)
        quant("qm", 128 * k, 128 * k + 128, "mt", 512 * k, 512 * k + 512,
              ["mz%d" % k] + ["mt%d_%d" % (k, b) for b in range(4)], ["qm%d" % k])

    def stage2(k):
        m, rk, one_hot = "qm%d" % k, T.rk[:, 4 * k:4 * k + 1], T.ot[:, 512 * k:512 * k + 512]
        pc, xc, kc = bank(k, 1)
        pr, xr, kr = bank(k, 0)
        mm(pc[:, xc:xc + 128], "qm", 128 * k, "pp", 0, 128, True, True, [m, "pp"], [kc])
        mm(pr[:, xr:xr + 128], "pp", 0, "qm", 128 * k, 128, True, True, [m, "pp"], [kr])
        act(T.ca[:, 4 * k:4 * k + 1], pc[:, xc:xc + 1], F.Abs, [kc, "eps"], ["ca%d" % k], bias=pf(12))
        s, sd, sx = (slice(c + CP * k, c + CP * k + CP) for c in (0, 448, 896))
        act(T.ra[:, s], pr[:, xr:xr + CP], F.Abs, [kr, "eps"], ["ra%d" % k], bias=pf(12))
        act(T.ra[:, sd], T.tri[:, :], F.Copy, ["tri", "ca%d" % k], ["rd%d" % k], scale=T.ca[:, 4 * k:4 * k + 1])
        if k:
            tt(T.ra[:, sx], T.ra[:, s], T.ra[:, sd], A.is_gt, ["rd%d" % k, "ra%d" % k], ["rx%d" % k])
            run("V", lambda e: e.tensor_reduce(rk, T.ra[:, sx], AxisListType.X, A.add), ["rx%d" % k], ["rk%d" % k], 0.11)
            ts(one_hot, T.k4[:, :], rk, None, A.is_equal, None, ["k4", "rk%d" % k], ["ot%d" % k], True)
        else:
            tt(T.ot[:, 0:448:4], T.ra[:, s], T.ra[:, sd], A.is_gt, ["rd0", "ra0"], ["ot0", "one"])
        quant("qo", 128 * k, 128 * k + 128, "ot", 512 * k, 512 * k + 512, ["ot%d" % k], ["qo%d" % k])
        for b, y in ((0, 2), (1, 3), (2, 1), (3, 0)):
            ps, x, key = bank(k, y)
            mm(ps[:, x:x + 128], "uq", 128 * b, "qm", 128 * k, 128, True, True, ["uq", m], [key])
            act(T.dxt[:, 512 * k + b:512 * k + 448:4], ps[:, x:x + CP], F.Copy, [key], ["dt%d_%d" % (k, b)], scale=0.0625)

    def stage3(k):
        ps, x, key = bank(k, 2)
        quant("qd", 128 * k, 128 * k + 128, "dxt", 512 * k, 512 * k + 512,
              ["dz%d" % k] + ["dt%d_%d" % (k, b) for b in range(4)], ["qd%d" % k])
        if not k:
            mm(ps[:, x:x + 128], "wn", 0, "qo", 0, 128, True, True, ["qo0", "wn"], [key])
            tt(T.tab[:, 0:CP], T.idr[:, 0:CP], ps[:, x:x + CP], A.max, ["idr", key], ["tab0"], True)
            return
        if k == 3:
            a = send([(3, codes("ld3", 0, CP + 2), codes("qd", 384, 386 + CP), eng[3])], "ar%d", ["qd3"])
            b = send([(3, T.ld3s[:, 0:CP + 2], T.qds[:, 384:386 + CP], eng[3])], "ar%d", ["qd3"])
            arrive("ar3", 2 * len(eng[3]), ["ld3", "ld3s"], [a, b], BACK)
        for c in (0, 1):
            mm(ps[:, x:x + 128], "qo", 128 * k, "cq", 128 * c, 128, c == 0, c == 1, ["qo%d" % k, "cq"], [key])
        cp(T.lo[:, 8 * k:8 * k + 3], ps[:, x:x + 3], [key], ["lo%d" % k])
        if k < 3:
            d, (c, z, h) = "sd%d" % k, {1: (0, 0, 0), 2: (176, 128, 66)}[k]
            pick("nq", c, CR, "qd", 128 * k, 128 * k + 128, T.lo[:, 8 * k:8 * k + 3], ["qd%d" % k, "lo%d" % k], d)
        if k != 2:
            to = (1,) if k == 1 else (2, 3)
            a = send([(j, T.ll[:, 8 * j:8 * j + 3], T.lo[:, 8 * j:8 * j + 3], half[j]) for j in to], "al%d",
                     ["lo%d" % j for j in to])
            for j in to:
                arrive("al%d" % j, len(half[j]), ["ll%d" % j], [a], BACK - 0.5)
        if k < 3:
            b = send([(k, codes("ld%d" % k, h, h + 24), codes("nq", c, c + 24), eng[k][0:2]),
                      (k, codes("ld%d" % k, h + 24, h + 48), codes("nq", c + 24, c + 48), eng[k][2:4]),
                      (k, T["ld%ds" % k][:, h + z - c:h + z - c + 96], T.nqs[:, z:z + 96], eng[k][4:8])], "ar%d",
                     [d, d + "s", "nq"])
            arrive("ar%d" % k, len(eng[k]), ["ld%d" % k, "ld%ds" % k], [b], BACK)

    turn_of[0] = "look"
    fill(T.tab[:, 0:384], 0.0, ["tab0", "tab2", "tab3"])
    fill(T.tab[:, 384:512], float(CR), ["tab1"])
    for k in range(4):
        turn_of[0] = "k%d" % k
        stage1(k)
        turn_of[0] = "k%db" % k
        stage2(k)
        turn_of[0] = "k%dc" % k
        stage3(k)

    turn_of[0] = "look"
    h1, h2, h3, h4, h5, h6, h7, h8, h9, h10 = (T.hh[:, 24 * i:24 * i + 24] for i in range(10))
    cp(T.win[:, :], T.ss[:, 2:3 * NT:3], ["ss"], ["win"], el(NT // 2))
    turn(T.tv[:, 0:NT], T.win[:, :], ["win"], ["tw"])
    turn(T.tv[:, NT:2 * NT], T.pref[:, :], ["pref"], ["tp"])
    tw, tp = T.tv[:, 0:NT:8], T.tv[:, NT:2 * NT:8]
    ts(h1, tw, 0.0, None, A.is_gt, None, ["tw"], ["h1"])
    ts(h2, tp, float(CP), None, A.is_le, None, ["tp"], ["h2"])
    ts(h6, tw, 4.0, 1.0, A.is_lt, A.add, ["tw"], ["h6"])
    tt(h4, h1, h2, A.mult, ["h1", "h2"], ["h4"])
    ts(h7, tp, 1.0 / 7, -4.0 / 7, A.mult, A.add, ["tp"], ["h7"])
    ts(h8, h7, WHOLE, WHOLE, A.add, A.subtract, ["h7"], ["h8"])
    ts(h9, h8, -111.0, -16.0 - CP, A.mult, A.add, ["h8"], ["h9"])
    act(h10, tp, F.Copy, ["tp"], ["h10"], scale=16.0)
    tt(h3, h9, h10, A.add, ["h9", "h10"], ["h3"])
    tt(h5, h4, h3, A.mult, ["h4", "h3"], ["h5"])
    ts(pf(10), ODD, -1.0, 1.0, A.mult, A.add, ["owb"], ["pf10"])
    for k in (0, 1, 2, 3):
        e = rank ^ k
        for h in (0, 1):
            o, p = slice(12 * POS[k] + h, 12 * POS[k] + 12, 2), (pf(10), ODD)[h]
            ts(T.offt[:, o], T.hh[:, 96 + e:120:4], float(CP), None, A.add, None, ["h5"], ["offt%d%d" % (k, h)])
            act(T.wgt[:, o], T.hh[:, 120 + e:144:4], F.Copy, ["h6", "owb", "pf10"], ["wgt%d%d" % (k, h)], scale=p)
    fill(T.cs[:, :], 0.0, ["csz"])

    def home(k, first, last):
        tab, zc, q = T.tab[:, 128 * TAB[k]:128 * TAB[k] + 128], "zc%d" % k, 12 * POS[k]
        offt, of, ko = T.offt[:, q:q + 12], T.hof[:, q:q + 12], ["offt%d0" % k, "offt%d1" % k]
        s, s1 = slice(192 * k, 192 * k + 192), slice(768 + 192 * k, 960 + 192 * k)
        lst, g1 = T.ll[:, 8 * k:8 * k + 3], T.gg[:, 768 + 192 * k:960 + 192 * k:16]
        if k in (1, 2):
            cp(tab.indirect(lst), T.vals[:, 2 * k - 2:2 * k - 2 + CR], ["vals", "ll%d" % k], ["tab%d" % k], 0.23)
        elif k:
            cp(tab.indirect(lst), T.ot[:, 448:448 + CR], ["oneb", "ll3"], ["tab3"], 0.23)
            act(T.gid[:, :], T.idr[:, :].indirect(offt), F.Copy, ["idr"] + ko, ["gid"], 0.35)
        if k == 3:
            run("V", lambda e: e.tensor_tensor(T.gg[:, s], tab.indirect(offt), T.gid[:, :], A.mult),
                ["tab3", "gid"] + ko, ["gr03"], 0.35)
        else:
            act(T.gg[:, s], tab.indirect(offt), F.Copy, ["tab%d" % k] + ko, ["gr0%d" % k], 0.35)
        turn(T.gg[:, s1], T.gg[:, s], ["gr0%d" % k], ["gr1%d" % k])
        if k in (1, 2):
            cp(of, g1, ["gr1%d" % k], ["hof%d" % k])
            pick(zc, 0, NT, "ld%d" % k, 64 * k - 64, 64 * k - 14, of, ["hof%d" % k, "ld%d" % k, "ld%ds" % k, "ldz"], zc)
        else:
            ts(of, g1, 0.0, float(CP), A.min, A.add, ["gr1%d" % k], ["hof%d" % k])
            if k:
                pick(zc, 0, NT, "ld3", 0, CP + 2, of, ["hof3", "ld3", "ld3s"], zc)
            else:
                pick(zc, 0, NT, "qd", 0, 128, of, ["hof0", "qd0"], zc)
        for b in range(4):
            mm(T.pz[:, 512 * b:512 * b + NT], "eq", 128 * b, zc, 0, NT, first, last, ["eq", zc, zc + "s"], ["*z%d" % b])

    for k in range(4):
        turn_of[0] = "h%d" % k
        home(k, k == 0, k == 3)
    turn_of[0] = "ct"
    ts(T.ff[:, 0:24], T.hof[:, 0:24], CP - 0.5, None, A.is_lt, None, ["hof0", "hof3"], ["fl0"])
    ts(T.ff[:, 24:36], T.hof[:, 24:36], CR - 0.5, None, A.is_lt, None, ["hof1"], ["fl1"])
    ts(T.ff[:, 36:48], T.hof[:, 36:48], 1.0, None, A.is_gt, None, ["hof2"], ["fl2"])
    tt(T.ff[:, 48:96], T.ff[:, 0:48], T.wgt[:, :], A.mult,
       ["fl0", "fl1", "fl2"] + ["wgt%d%d" % (k, h) for k in range(4) for h in (0, 1)], ["fw"])
    tt(T.ff[:, 96:120], T.ff[:, 48:72], T.ff[:, 72:96], A.add, ["fw"], ["fs"])
    tt(T.ff[:, 120:132], T.ff[:, 96:108], T.ff[:, 108:120], A.add, ["fs"], ["ft"])
    tt(T.cs[:, 0:6], T.ff[:, 120:132:2], T.ff[:, 121:132:2], A.add, ["ft", "csz"], ["cs"])
    turn(T.cst[0:32, :], T.cs[0:32, :], ["cs", "csz"], ["cst"], True)

    turn_of[0] = ""
    for b in range(4):
        move = (T.zt[:, b:768:4], T.pz[:, 512 * b:512 * b + NT])
        if b % 2:
            cp(move[0], move[1], ["*z%d" % b], ["zt%d" % b])
        else:
            act(move[0], move[1], F.Copy, ["*z%d" % b], ["zt%d" % b])
    quant("zq", 0, 192, "zt", 0, 768, ["zt0", "zt1", "zt2", "zt3"], ["zq"])
    mm(T.px[:, 0:NT], "vq", 0, "zq", 0, NT, True, True, ["vq", "zq"], ["*x0"])
    cp(T.ysb[:, :], T.px[:, 0:NT], ["*x0"], ["ysb"])
    dma("Y", "doy", T.ct[0:1, 0:NT], T.cst[0:6, 0:32], ["cst"], [], 2.0)
    dma("Y", "doy", T.oc[:, 0:768], T.zq[:, 0:NT].bitcast(dt.uint8), ["zq"], [], 2.0)
    for i in range(4):
        q, s = ("S", "dos") if i < 3 else ("Y", "doy")
        dma(q, s, T.osc[4 * i:4 * i + 4, 0:NT], T.zqs[32 * i:32 * i + 4, 0:NT], ["zq"], [], 2.0)
    dma("Y", "doy", T.y[:, :], T.ysb[:, :], ["ysb"], [], 2.0)

    n = len(tasks)
    follow = [[] for _i in range(n)]
    for i, t in enumerate(tasks):
        for j in t["before"]:
            follow[j].append(i)
    rest = [0.0] * n
    for i in range(n - 1, -1, -1):
        far = max([rest[j] + (HOP if tasks[j]["before"][i] else 0.0) for j in follow[i]] or [0.0])
        rest[i] = max(far, 0.0) + tasks[i]["cost"] + tasks[i]["late"] + tasks[i]["ahead"]
    left = [len(t["before"]) for t in tasks]
    ready = [0.0] * n
    free = {q: 0.0 for q in ("V", "S", "P", "G", "Y", None)}
    able = [i for i in range(n) if not left[i]]
    order = []
    while able:
        best = None
        for q in free:
            mine = sorted(i for i in able if tasks[i]["q"] == q)
            if not mine:
                continue
            at = max(free[q], min(ready[i] for i in mine)) if q else min(ready[i] for i in mine)
            pool = [i for i in mine if ready[i] <= at + 1e-9]
            i = min(pool) if q == "Y" else max(pool, key=lambda j: rest[j])
            for j in mine:
                if q not in ("Y", None) and ready[j] < at + HOLD * tasks[i]["cost"] and rest[j] > rest[i] + GAP:
                    i = j
            at = max(at, ready[i])
            if best is None or at < best[0]:
                best = (at, i)
        at, i = best
        t = tasks[i]
        able.remove(i)
        order.append(i)
        if t["q"]:
            free[t["q"]] = at + t["cost"]
        done = at + t["cost"] + t["late"]
        for j in follow[i]:
            ready[j] = max(ready[j], done + HOP if tasks[j]["before"][i] else at + t["cost"])
            left[j] -= 1
            if not left[j]:
                able.append(j)

    waited, token = {}, {}

    def need(q, tok):
        if waited.get((q, tok[0]), 0) < tok[1]:
            queue[q].wait_ge(T.sem[tok[0]], tok[1])
            waited[(q, tok[0])] = tok[1]

    for i in order:
        t = tasks[i]
        if t["q"] is None:
            token[i] = (t["sem"], t["inc"])
            continue
        best = {}
        for j, full in t["before"].items():
            if full:
                s, v = token[j]
                best[s] = max(best.get(s, 0), v)
        for s, v in best.items():
            need(t["q"], (s, v))
        made = t["call"](queue[t["q"]])
        if t["sem"]:
            made.then_inc(T.sem[t["sem"]], t["inc"])
            total[t["sem"]] = total.get(t["sem"], 0) + t["inc"]
            token[i] = (t["sem"], total[t["sem"]])
    for s, v in total.items():
        need("G", (s, v))
